import numpy as np, ml_dtypes
CORES = [3,7,11,15,131,135,139,143]
N = 8
import mx_ref
BF = ml_dtypes.bfloat16
def entries(a):
    return np.ascontiguousarray(a.T).reshape(-1)
def table(e):
    return np.ascontiguousarray(np.reshape(e, (-1, 16)).T).astype(np.int32)
def gcols(t, e):
    v = np.concatenate([t.reshape(8, 16, -1, 4), np.zeros((8, 16, 1, 4), BF)], axis=2)
    return np.ascontiguousarray(np.stack([v[g][:, e[g]] for g in range(8)])).reshape(128, -1)
def tile(rs):
    return np.stack(rs, axis=2).reshape(128, -1).astype(BF)
def pick(q, e):
    c = np.concatenate([q[0].reshape(128, -1, 4), np.zeros((128, 1, 4), np.uint8)], axis=1); s = np.concatenate([q[1], np.ones((16, 1), np.uint8)], axis=1)
    return (np.ascontiguousarray(c[:, e].reshape(128, -1)), np.ascontiguousarray(s[:, e]))
def join(*qs):
    return (np.concatenate([q[0] for q in qs], axis=1), np.concatenate([q[1] for q in qs], axis=1))
def put(q, e, v):
    c, s = q[0].reshape(128, -1, 4).copy(), q[1].copy(); c[:, e] = v[0].reshape(128, -1, 4); s[:, e] = v[1]
    return (c.reshape(128, -1), s)
def pk(c, s):
    return (np.ascontiguousarray(c), mx_ref.live(s))
def emit(q):
    return q[0], q[1]
def packed(v, rng):
    q = [mx_ref.quantize(np.ascontiguousarray(v[r])) for r in range(N)]
    return np.stack([a for a, b in q]), np.stack([mx_ref.plane(b, rng) for a, b in q])
def values_of_codes():
    e, c = np.zeros((128, 128, 4), np.float32), np.zeros((128, 2, 4), np.uint8)
    e[np.arange(128), np.arange(128), 0] = 1
    c[:127, :, 0] = np.arange(256).reshape(2, 128).T[:127]
    return mx_ref.matmul(mx_ref.quantize(e.reshape(128, 512).astype(BF)), (c.reshape(128, 8), np.full((16, 2), 127, np.uint8))).T.reshape(-1).astype(np.float64)
CODE_VALUE, SCALE_VALUE = values_of_codes(), 2.0 ** (np.arange(256) - 127.0)
def decode(q):
    return (CODE_VALUE[q[0]].reshape(16, 8, -1, 4) * SCALE_VALUE[q[1]][:, None, :, None] + 0.0).reshape(128, -1).astype(np.float32)
def f(rng, *shape):
    return mx_ref.flush((rng.standard_normal(shape, dtype=np.float32) * np.exp2(rng.integers(-2, 3, shape[:-1] + (1,)))).astype(BF))
def wide(rng, *shape, cols=0):
    v = rng.standard_normal(shape, dtype=np.float32) * np.exp2(rng.integers(-12, 13, shape)).astype(np.float32)
    if cols: v *= np.repeat(np.exp2(rng.integers(-cols, cols + 1, shape[:-2] + (1, shape[-1] // 4))) * (rng.random(shape[:-2] + (1, shape[-1] // 4)) > 0.0625), 4, axis=-1).astype(np.float32)
    return mx_ref.flush(v.astype(BF))
C, K = 256, 96
PARTNER = [1, 2, 4]
LOCAL = np.arange(C) % 32
ROOT = np.arange(C) - LOCAL
PLACE = np.arange(32)
def big(v):
    v = v.astype(np.float32)
    v[np.abs(v) < np.float32(2.0 ** -16)] = 0
    return v.astype(BF)
def numbers_of(rng):
    return {"x": big(f(rng, N, 128, 4 * C)), "u": np.array(f(rng, N, 128, 512)), "v": np.array(f(rng, N, 128, 512))}
def parents(rng):
    return {k: np.stack([table(ROOT + rng.integers(0, np.maximum(LOCAL, 1), C)) for r in range(N)]) for k in ("p0", "p1")}
def weights(rng, still=[]):
    w = np.array(big(f(rng, N, 128, 2048))).reshape(N, 128, 4, 128, 4)
    for i in still:
        w[:, i] = 0
        w[:, :, :, i] = 0
    c, p = packed(w.reshape(N, 128, 2048), rng)
    return {"wc": c, "ws": p}
def setup_inputs(rng):
    return {**numbers_of(rng), **parents(rng), **weights(rng)}
def setup_inputs_ties(rng):
    d = numbers_of(rng)
    x = d["x"].reshape(N, 128, C, 4)
    x[:, ::64] = 0
    x[:, ::64, :, 0] = rng.integers(0, 3, (N, 2, C)).astype(np.float32).astype(BF)
    u = d["u"].reshape(N, 128, 128, 4)
    u[:, :, ::64] = 0
    o = rng.permutation(N)
    for r in range(N):
        for h in (0, 64): u[r, h, h, 0] = 0.0 if r == o[0] else -1.0 if r == o[1] else 1.0
    return {"x": x.reshape(N, 128, 4 * C), "u": u.reshape(N, 128, 512), "v": d["v"], **parents(rng), **weights(rng, [0, 64])}
def setup_inputs_near(rng):
    d = numbers_of(rng)
    x = d["x"].astype(np.float32).reshape(N, 128, C, 4)
    u = d["u"].reshape(N, 128, 128, 4)
    u[:, :, ::64] = 0
    o = rng.permutation(N) % 4
    for r in range(N):
        k = 2.0 ** -30 if o[r] > 0 else 1.0
        for h in (0, 64):
            x[r, h:h + 16] = 0
            sign = np.repeat(rng.permutation(C // 32) % 2 * 2.0 - 1.0, 32)
            far = 32 * np.arange(C // 32) + rng.integers(0, 32, C // 32)
            s = rng.integers(0, 16, C)
            if o[r] < 3:
                x[r, h + 8] = ((s[:, None] >> np.arange(4)) & 1) * np.exp2(np.arange(4) - 23.0)
                u[r, h + 8, h] = k
            if o[r] < 2:
                x[r, h, :, 0] = sign
                x[r, h + 11, :, 0] = 2.0 ** -10
                u[r, h, h, 0] = k
                u[r, h + 11, h, 0] = k
            if o[r] == 2:
                x[r, h, far, 0] = sign[far] * 2.0 ** 29
                u[r, h, h, 0] = 1.0
            if o[r] == 3:
                odd = np.arange(C) // 32 % 2
                j = rng.integers(0, 3, C)
                x[r, h + 10, :, 0] = (1 - odd) * np.array([1.0, 0.0, 1.125])[j] * 2.0 ** -29
                x[r, h + 12, :, 0] = (1 - odd) * (j == 1) * 2.0 ** -29
                u[r, h + 10, h, 0] = 1.125 * k
                u[r, h + 12, h, 0] = 1.25 * k
                x[r, h, :, 0] = odd * 1.96875
                x[r, h + 1, :, 0] = odd * rng.integers(3, 5, C) * np.exp2(np.arange(C) // 64 % 4 - 16.0)
                u[r, h + 1, h, 0] = k
    still = [h + i for h in (0, 64) for i in range(16)]
    return {"x": x.reshape(N, 128, 4 * C).astype(BF), "u": u.reshape(N, 128, 512), "v": d["v"], **parents(rng), **weights(rng, still)}
def setup_inputs_huge(rng):
    d = numbers_of(rng)
    o = rng.permutation(N) % 2
    x = (0.5 + 0.12 * rng.random((N, 128, C, 4))) * 2.0 ** 30
    for r in range(N):
        if o[r] == 0: c = np.repeat(rng.permutation(C // 32) % 2 * 2.0 - 1.0, 32)
        else: c = rng.permutation(C) % 2 * 2.0 - 1.0
        x[r] *= c[None, :, None]
    u = d["u"].reshape(N, 128, 128, 4)
    a = 2.0 ** 30 * (1.0 - 0.1 * rng.random((N, 128, 2, 4))) * rng.choice([-1.0, 1.0], (N, 1, 2, 1))
    u[:, :, ::64] = a.astype(np.float32).astype(BF)
    w = np.zeros((N, 128, 4, 128, 4), np.float32)
    i = np.arange(128)
    for b in range(4): w[:, i, b, i, b] = -2
    c, p = packed(w.reshape(N, 128, 2048).astype(BF), rng)
    return {"x": x.astype(np.float32).reshape(N, 128, 4 * C).astype(BF), "u": u.reshape(N, 128, 512), "v": d["v"], **parents(rng), "wc": c, "ws": p}
def setup_inputs_late(rng):
    d = numbers_of(rng)
    x = d["x"].astype(np.float32).reshape(N, 8, 16, C, 4)
    odd = 1.0 + (2.0 * rng.integers(0, 64, (N, 8, 8, C, 4)) + 1.0) * 2.0 ** -7
    x[:, :, 8:] = odd * np.exp2(rng.integers(-14, -7, (N, 8, 8, C, 4))) * rng.choice([-1.0, 1.0], (N, 8, 8, C, 4))
    x[:, :, 8, :, 0] = 1.96875 * rng.choice([-1.0, 1.0], (N, 8, C))
    x[:, ::4, 0] = 0
    u = d["u"].reshape(N, 128, 128, 4)
    u[:, :, ::64] = 0
    for h in (0, 64): u[:, h, h, 0] = 1.0
    before = np.maximum(LOCAL - 1, 0)
    a, b = [], []
    for r in range(N):
        k = np.repeat(rng.permutation(C // 32) % 4, 32)
        a.append(table(ROOT + np.where(k == 1, 0, np.where(k == 3, before // 2, before))))
        b.append(table(ROOT + np.where((k == 1) | (k == 2), 0, before)))
    return {"x": x.reshape(N, 128, 4 * C).astype(BF), "u": u.reshape(N, 128, 512), "v": d["v"], "p0": np.stack(a), "p1": np.stack(b), **weights(rng)}
def setup_inputs_spread(rng):
    d = setup_inputs(rng)
    d["x"] = big(wide(rng, N, 128, 4 * C, cols=6))
    return d
def check_inputs(d):
    b = []
    for k in ("x", "u", "v"):
        a = np.abs(d[k].astype(np.float32))
        if not (np.isfinite(a).all() and ((a == 0) | (a >= 2.0 ** -30) & (a <= 2.0 ** 30)).all()): b.append("a value of " + k)
    none, least, most = [emit(mx_ref.quantize(np.full((128, 16), k, np.float32).astype(BF)))[1][0, 0] for k in (0.0, 2.0 ** -30, 2.0 ** 30)]
    for r in range(N):
        for k in ("p0", "p1"):
            e = entries(d[k][r])
            if not ((e >= ROOT) & (e < ROOT + np.maximum(LOCAL, 1))).all(): b.append("an entry of " + k)
        if ((d["wc"][r] == 0x7F) | (d["wc"][r] == 0xFF)).any(): b.append("wc: a code that is no number")
        s = mx_ref.live(d["ws"][r])
        if ((s != none) & ((s < least) | (s > most))).any(): b.append("ws: a scale out of range")
    return b
def split(s, a, b):
    a, b = np.stack([a, a], axis=1), np.stack([b, b], axis=1)
    up = np.where(np.take_along_axis(s, a, axis=2) >= np.take_along_axis(s, b, axis=2), a, b).reshape(-1, 32) % 32
    n = len(up)
    above = np.zeros((n, 32, 32), bool)
    for j in range(32):
        if j > 0: above[:, :, j] = above[np.arange(n), :, up[:, j]]
        above[:, j, j] = True
    left, top = np.ones((n, 32), bool), np.zeros((n, 32), np.int64)
    c, w = [], []
    for l in range(4):
        one = (top[:, :, None] == top[:, None]) & left[:, :, None] & left[:, None]
        size = np.sum(above & one, axis=2)
        half = 2 * size >= np.sum(one, axis=2)
        best = np.max(np.where(one & half[:, None], PLACE, -1), axis=2)
        c.append(np.where(left, best, PLACE))
        w.append(size)
        left = left & (best != PLACE)
        cut = ~np.take_along_axis(left, up, axis=1)
        cut[:, 0] = True
        top = np.max(np.where(above & cut[:, :, None], PLACE[:, None], 0), axis=1)
    c, w = [np.stack(k, axis=1).reshape(N, 2, -1, 4, 32).transpose(0, 1, 3, 2, 4).reshape(N, 8, C) for k in (c, w)]
    return c + ROOT, np.argsort(-w, axis=2, kind="stable")
def reference(x, u, v, p0, p1, wc, ws):
    qu = [mx_ref.quantize(u[r]) for r in range(N)]
    lay = [pk(wc[r], ws[r]) for r in range(N)]
    a, b = np.stack([entries(p0[r]) for r in range(N)]), np.stack([entries(p1[r]) for r in range(N)])
    now = [x[r] for r in range(N)]
    for m in PARTNER:
        q = [mx_ref.quantize(now[r]) for r in range(N)]
        own = [decode(q[r]) for r in range(N)]
        s = np.stack([mx_ref.matmul(qu[r], q[r])[::64] for r in range(N)]) + np.float32(0.0)
        c, o = split(s, a, b)
        mosaic = [gcols(own[r].astype(BF), c[r]) for r in range(N)]
        sent = [mx_ref.quantize(gcols(mosaic[r], o[r][:, :K])) for r in range(N)]
        for r in range(N):
            e = np.argsort(o[r], axis=1)
            e = np.where(e < K, e, K + np.arange(C))
            mate = gcols(np.concatenate([decode(sent[r ^ m]).astype(BF), mosaic[r]], axis=1), e).astype(np.float32)
            z = mx_ref.quantize(((mosaic[r].astype(np.float32) + mate) * np.float32(0.5)).astype(BF))
            now[r] = tile([mx_ref.matmul(pick(lay[r], np.arange(128 * k, 128 * k + 128)), z) * np.float32(0.03125) + own[r][:, k::4] for k in range(4)])
    y, cl = np.zeros((N, 128, C), np.float32), np.zeros((N, 8, C), np.float32)
    oc, osc = np.zeros((N, 128, 4 * C), np.uint8), np.zeros((N, 16, C), np.uint8)
    for r in range(N):
        q = mx_ref.quantize(now[r])
        y[r] = mx_ref.matmul(mx_ref.quantize(v[r]), q)
        cl[r] = c[r]
        oc[r], osc[r] = emit(q)
    return {"y": y, "cl": cl, "oc": oc, "osc": osc}

@@ -1,0 +1,570 @@
+from concourse.mybir import dt, AluOpType, ActivationFunctionType
+
+ALU = AluOpType
+ACT = ActivationFunctionType
+C, K = 256, 96
+PARTNER = [1, 2, 4]
+PL = K + C
+F32, BF, I32, U16, X4, U8 = "float32", "bfloat16", "int32", "uint16", "float8_e4m3fn_x4", "uint8"
+
+SCRATCH = {}
+PART = {}
+
+
+def _sb(name, n, d):
+    SCRATCH[name] = ("sbuf", [128, n], d)
+
+
+def _share(name, d, parts):
+    at = 0
+    for nm, w in parts:
+        PART[nm] = (name, at, w)
+        at += w
+    _sb(name, at, d)
+
+
+for _d, _l in [
+    (BF, "xt0 1024 ut 512 vt 512 iota 256 gv 68 e32t 2048 lut 2048 pmt 512 p0r 128 p1r 128 pd 128 sel 128 jm 128 jb0 160 "
+         "jb1 160 tj 288 ap 128 a0 128 a1 128 ac 128 act 128 ai 128 xx 128 xxt 128 d0 128 d0t 384 ee 128 gt 512 "
+         "mv 512 cr 256 sw 272 te 192 tw %d tp 1024 et 512 ztile 1024 xt1 1024" % (4 * PL)),
+    (F32, "pat 768 ssb 256 sb1 128 abo 128 ab2 128 abb 128 sz 128 thr 128 mm 128 mt 128 red 128 x2 128 x2t 128 cs 128 "
+          "rk 256 crf 256 zf 96 e32 384 ysb 256"),
+    (I32, "pin 16 ip 2 bi 16 wi 32 wd 64"),
+    (U16, "cl16 8 uoff 8 exl 4 poff 16 jo0 16 jo1 16 roff 16 coff 16 zoff 16 ll0 8 ll1 8 ll2 8 el0 16 el1 16 el2 16"),
+    (X4, "wq 512 uq 128 uq2 128 vq 128 e32q 512 luq 512 pmq 128 gq 192 mq 160 eq 128 zq 256 xq0 256 xq1 256 xq2 256 "
+         "xq3 256 lq0 256 lq1 256 lq2 256"),
+    (U8, "wsq 512 us 128 us2 128 vs 128 e32s 512 lus 512 pms 128 gs 192 ms 160 es 128 zs 256 xs0 256 xs1 256 xs2 256 "
+         "xs3 256 ls0 256 ls1 256 ls2 256"),
+]:
+    _w = _l.split()
+    for _i in range(0, len(_w), 2):
+        _sb(_w[_i], int(_w[_i + 1]), _d)
+_share("cb", BF, [(n, 128) for n in ("jt", "key", "hm", "b32", "cpos", "id32", "rst", "kl", "ku")])
+_share("cw", F32, [("cf", 16), ("cc", 32), ("rs", 64)])
+_share("sm", F32, [("pay", 4), ("nb", 4), ("s2h", 4), ("h64", 4), ("base", 4), ("sf", 16), ("t1", 4), ("size", 4),
+                   ("ns", 4), ("nrem", 4)])
+for _t in range(8):
+    SCRATCH["ps%d" % _t] = ("psum", [128, 512], F32)
+
+SEMAPHORES = (["qv", "qs", "qt", "qg", "dx", "du", "dp", "dw", "dv", "dout", "sent"]
+              + ["aq%d" % t for t in range(3)] + ["al%d" % t for t in range(3)])
+WHOLE = 12582912.0
+
+
+def V(name, a=0, b=None, s=1, p=None):
+    if name in PART:
+        buf, at, w = PART[name]
+        return (buf, at + a, at + (w if b is None else b), s, p, None)
+    if b is None:
+        b = SCRATCH[name][1][1]
+    return (name, a, b, s, p, None)
+
+
+def col(name, a):
+    return V(name, a, a + 1)
+
+
+def ind(win, off):
+    return win[:5] + (off,)
+
+
+def _mask(v):
+    if v[0].startswith("ps"):
+        return 1
+    m = 0
+    for c in range(v[1], v[2], v[3]):
+        m |= 1 << c
+    return m
+
+
+def rank_program(g, core, T, topo):
+    rank = T.rank_of(core)
+    if rank is None:
+        return
+    ops = []
+
+    def ap(v, cast=None):
+        if not isinstance(v, tuple):
+            return v
+        name, a, b, s, p, off = v
+        ps = slice(None) if p is None else slice(p[0], p[1])
+        x = T[name][ps, a:b] if s == 1 else T[name][ps, a:b:s]
+        if cast is not None:
+            x = x.bitcast(cast)
+        if off is not None:
+            x = x.indirect(ap(off))
+        return x
+
+    def op(eng, fn, rd, wr, sem=None, n=0, acc=False):
+        vs = [v for v in rd if isinstance(v, tuple)]
+        r = [(v[0], _mask(v)) for v in vs] + [(v[5][0], _mask(v[5])) for v in vs + wr if v[5] is not None]
+        ops.append({"e": eng, "fn": fn, "r": r, "w": [(v[0], _mask(v)) for v in wr], "sem": sem, "n": n, "acc": acc})
+
+    def tt(o, a, b, f):
+        op("v", lambda q: q.tensor_tensor(ap(o), ap(a), ap(b), f), [a, b], [o])
+
+    def ts(o, a, s1, f0, s2=None, f1=None):
+        if f1 is None:
+            op("v", lambda q: q.tensor_scalar(ap(o), ap(a), ap(s1), None, f0), [a, s1], [o])
+        else:
+            op("v", lambda q: q.tensor_scalar(ap(o), ap(a), ap(s1), ap(s2), f0, f1), [a, s1, s2], [o])
+
+    def cp(o, a, cast=None):
+        op("v", lambda q: q.tensor_copy(ap(o, cast), ap(a, cast)), [a], [o])
+
+    def ms(o, c):
+        op("v", lambda q: q.memset(ap(o), c), [], [o])
+
+    def tr(o, a):
+        op("v", lambda q: q.transpose(ap(o), ap(a)), [a], [o])
+
+    def scan(o, a, b, f0, f1):
+        op("v", lambda q: q.tensor_tensor_scan(ap(o), ap(a), ap(b), 0.0, f0, f1), [a, b], [o])
+
+    def qz(oq, osc, a):
+        op("v", lambda q: q.quantize_mx(ap(oq), ap(osc), ap(a)), [a], [oq, osc])
+
+    def act(o, a, f=ACT.Copy, scale=1.0, bias=None):
+        if bias is None:
+            op("s", lambda q: q.activation(ap(o), ap(a), f, scale=ap(scale)), [a, scale], [o])
+        else:
+            op("s", lambda q: q.activation(ap(o), ap(a), f, bias=ap(bias), scale=ap(scale)), [a, scale, bias], [o])
+
+    def lin(o, a, scale, bias):
+        act(o, a, ACT.Identity, scale, bias)
+
+    def mm(o, wq, ws, xq, xs, start=True, stop=True):
+        op("t", lambda q: q.matmul_mx(ap(o), ap(wq), ap(ws), ap(xq), ap(xs), start, stop), [wq, ws, xq, xs], [o],
+           acc=not start)
+
+    def iota(o, pattern, base, cm):
+        if SCRATCH[o[0]][2] == I32:
+            op("g", lambda q: q.iota(ap(o), pattern, base, cm), [], [o])
+        else:
+            op("g", lambda q: q.iota(ap(o), pattern, base, cm, allow_small_or_imprecise_dtypes=True), [], [o])
+
+    def select(o, pattern, f, fill, cm):
+        op("g", lambda q: q.affine_select(ap(o), ap(o), pattern, f, fill, 0, cm), [o], [o])
+
+    def load(eng, o, src, sem, cast=None):
+        op(eng, lambda q: q.dma_start(ap(o, cast), src), [], [o], sem=sem, n=16)
+
+    def store(eng, dst, a, cast=None):
+        op(eng, lambda q: q.dma_start(dst, ap(a, cast)), [a], [], sem="dout", n=16)
+
+    def send(to, o, a, rsem, cast=None):
+        rid, pid = topo.addr(to, core)
+        m = topo.mask(core, to)
+        op("g", lambda q: q.remote_dma(ap(o, cast), ap(a, cast), T.sem[rsem], T.sem["sent"], pid, rid, m), [a], [],
+           sem="sent", n=len(topo.engines(core, to)))
+
+    def arrive(frm, views, rsem, calls):
+        op("x", None, [], views, sem=rsem, n=calls * len(topo.engines(frm, core)))
+
+    S4 = lambda name: V(name, 31, 128, 32)
+    blk = lambda name, b: V(name, 32 * b, 32 * b + 32)
+    end = lambda name, b: col(name, 32 * b + 31)
+    run = lambda name, i, n: V(name, n * i, n * i + n)
+    bank = lambda b, n, a=0: V("ps%d" % b, a, n)
+
+    load("y", V("xt0"), T.x[:], "dx")
+    load("s", V("ut"), T.u[:], "du")
+    for gi in range(8):
+        a1 = (gi >> 1) & 1
+        load("y", V("pin", 0, 8, 1, (16 * gi, 16 * gi + 16)), T.p0[:, 8 * a1:8 * a1 + 8], "dp")
+        load("s", V("pin", 8, 16, 1, (16 * gi, 16 * gi + 16)), T.p1[:, 8 * a1:8 * a1 + 8], "dp")
+    load("y", V("wq"), T.wc[:], "dw", dt.uint8)
+    load("y", V("wsq"), T.ws[:], "dw")
+    load("y", V("vt"), T.v[:], "dv")
+
+    iota(V("ip", 0, 1), [[0, 1]], 0, 1)
+    iota(V("jt"), [[0, 4], [1, 32]], 0, 0)
+    iota(V("iota"), [[1, 256]], 0, 0)
+    iota(V("key"), [[0, 2], [128, 2], [1, 32]], 0, 0)
+    iota(V("hm"), [[1, 2], [0, 64]], 0, 0)
+    iota(V("gv"), [[-2, 34], [-2, 2]], 1, 0)
+    iota(V("e32t"), [[0, 2048]], 32, 0)
+    ms(V("uoff", 0, 4), 0)
+    ms(V("uoff", 4, 8), 64)
+    ms(V("jb0"), 0.0)
+    ms(V("jb1"), 0.0)
+    FIELDS = [(0, 1), (1, 1), (4, 1), (5, 1), (6, 1), (0, 7), (0, 31), (0, 3), (2, 3), (0, 15)]
+    for i, (sh, mk) in enumerate(FIELDS):
+        ts(col("bi", i), V("ip", 0, 1), sh, ALU.logical_shift_right, mk, ALU.bitwise_and)
+    ms(V("mv"), 0.0)
+    cp(V("cf", 0, 10), V("bi", 0, 10))
+    B0, B1, B4, B5, B6, K7, J31, R3, Q3, R15 = [col("cf", i) for i in range(10)]
+    cc = lambda i: col("cc", i)
+    lin(cc(0), B0, -288.0, 128.0)
+    lin(cc(1), B0, 9.0, K7)
+    lin(cc(4), B5, -128.0, 0.0)
+    lin(cc(5), B5, 128.0, J31)
+    lin(cc(2), cc(0), B4, 0.0)
+    for i, d in enumerate((-32.0, 0.0, 32.0)):
+        lin(cc(20 + i), cc(5), -1.0, -d - 0.5)
+        lin(cc(24 + i), cc(5), 1.0, d - 0.5)
+    lin(cc(6), cc(5), 1.0 / 2048, 64.0)
+    lin(cc(9), J31, -1.0 / 64, -255.5)
+    lin(cc(11), B6, 64.0, R15)
+    lin(cc(12), B4, 16.0, 0.0)
+    lin(cc(13), B0, 5.0, K7)
+    lin(cc(14), B0, -12.0, 26.0)
+    lin(cc(15), B0, 17.0, 31.0)
+    lin(cc(16), B4, 4.0, R3)
+    lin(cc(17), Q3, 8.0, cc(16))
+    lin(cc(18), cc(13), 16.0, cc(12))
+    lin(cc(19), cc(14), B1, cc(15))
+    lin(cc(3), B5, 32.0, cc(17))
+    ms(V("sw"), 0.0)
+    ms(V("rs"), 0.0)
+    ms(V("et", 4 * K, 512), 0.0)
+    ms(V("gt", 252, 256), 0.0)
+    ms(V("gt", 508, 512), 0.0)
+    qz(V("gq", 64, 192), V("gs", 64, 192), V("mv"))
+    qz(V("mq", 32, 160), V("ms", 32, 160), V("mv"))
+    ts(V("kl"), V("hm"), B6, ALU.not_equal, 500.0, ALU.mult)
+    for c0 in (0, 32, 49, 58):
+        ms(col("rs", c0), 1000.0)
+    tt(V("ku"), V("key"), V("kl"), ALU.add)
+    tt(V("kl"), V("key"), V("kl"), ALU.subtract)
+
+    qz(V("uq"), V("us"), V("ut"))
+    ts(V("id32"), V("jt"), J31, ALU.is_equal)
+    cp(V("uq2"), ind(V("uq"), V("uoff")), dt.uint32)
+    cp(V("us2"), ind(V("us"), V("uoff")))
+    cp(V("poff"), V("pin"))
+    tt(V("b32"), V("iota", 0, 128), V("jt"), ALU.subtract)
+    JT, ET, RX = V("cl16", 0, 1), V("cl16", 2, 3), V("cl16", 4, 5)
+
+    act(V("pat", 128, 256), V("kl"), ACT.Sign, 1.0, cc(21))
+    lin(V("p1r"), ind(V("iota"), V("poff", 8, 16)), 1.0, cc(4))
+    lin(V("p0r"), ind(V("iota"), V("poff", 0, 8)), 1.0, cc(4))
+    select(V("pat", 128, 256), [[-1, 128]], ALU.not_equal, -513.0, 1)
+    select(V("e32t"), [[1, 4], [-4, 128], [-1, 4]], ALU.is_equal, 0.0, 4)
+
+    def patterns():
+        for i in (0, 2):
+            act(run("pat", i, 128), V("kl"), ACT.Sign, 1.0, cc(20 + i))
+        for i in range(3):
+            act(run("pat", 3 + i, 128), V("ku"), ACT.Sign, -1.0, cc(24 + i))
+
+    def lu_tile(k, slots=range(4)):
+        pair = [(1, 2), (2, 2), (0, 1), (0, 0)][k]
+        for sl in slots:
+            lin(V("lut", 512 * k + sl, 512 * k + 512, 4), run("pat", pair[sl & 1] + 3 * (sl >> 1), 128), 0.25, 0.25)
+
+    def consts_a():
+        ts(cc(7), J31, 0.0, ALU.is_equal, 1000.0, ALU.mult)
+        ts(col("cl16", 0), cc(1), 16.0, ALU.mult, cc(2), ALU.add)
+        ts(V("cpos"), V("b32"), J31, ALU.add)
+        ts(V("rst"), V("jt"), 0.0, ALU.not_equal)
+        ts(cc(8), cc(7), 0.3, ALU.add)
+
+    def consts_b():
+        ts(col("cl16", 2), cc(18), 191.0, ALU.min)
+        ts(col("cl16", 4), Q3, 64.0, ALU.mult, cc(19), ALU.add)
+        ts(V("exl"), V("iota", 0, 256, 64), cc(3), ALU.add)
+
+    def consts_c(slots):
+        for sl in slots:
+            ts(V("pmt", sl, 512, 4), V("iota", 0, 128), -16.0 * sl, ALU.add, cc(11), ALU.is_equal)
+
+    SEG = [(0, 32, 1), (32, 17, 0), (49, 9, 0), (58, 5, 0)]
+
+    def decode(bank0, xq, xs, n, stop=True):
+        for b in range(4):
+            mm(bank(bank0 + b, n), run("e32q", b, 128), run("e32s", b, 128), xq, xs, True, stop)
+
+    def signs(l, w):
+        c0, n, v0 = SEG[l]
+        for b in range(4):
+            e0 = 4 * (64 * (b >> 1) + c0) + (b & 1)
+            act(V("gt", e0, e0 + 4 * n - 1, 2), V("gv", 2 * v0, 2 * (v0 + n)), ACT.Sign, 0.5, w(b))
+
+    def places(b):
+        scan(V("rk", 64 * b, 64 * b + 63), V("rs", 0, 63), bank(4 + b, 63), ALU.add, ALU.min)
+
+    def own_t(bs):
+        for b in bs:
+            act(V("tw", PL * b + K, PL * b + PL), bank(b, 256), ACT.Copy, 2.0)
+
+    def mate_t():
+        for b in range(4):
+            act(run("tp", b, 256), bank(b, 256), ACT.Copy, 1.0 / 32)
+
+    def halves(dst, wq, ws, xq, xs):
+        for h in range(2):
+            mm(bank(4 + h, 128), wq, ws, run(xq, h, 128), run(xs, h, 128))
+        cp(V(dst, 0, 128), bank(4, 128))
+        act(V(dst, 128, 256), bank(5, 128))
+
+    xt = "xt0"
+    for t, m in enumerate(PARTNER):
+        mate = T.cores[rank ^ m]
+        XQ, XS = V("xq%d" % t), V("xs%d" % t)
+        LQ, LS = V("lq%d" % t), V("ls%d" % t)
+        first = t == 0
+        qz(XQ, XS, V(xt))
+        if first:
+            consts_a()
+        halves("ssb", V("uq2"), V("us2"), XQ[0], XS[0])
+        send(mate, LQ, XQ, "aq%d" % t, dt.uint8)
+        send(mate, LS, XS, "aq%d" % t)
+        act(V("sb1"), ind(V("ssb"), V("poff", 8, 16)))
+        cp(V("mm"), ind(V("ssb"), V("poff", 0, 8)))
+        if first:
+            tt(V("pd"), V("p0r"), V("p1r"), ALU.subtract)
+            patterns()
+        else:
+            decode(0, XQ, XS, 256)
+            own_t((0, 1))
+        tt(V("sel"), V("mm"), V("sb1"), ALU.is_ge)
+        tt(V("jm"), V("sel"), V("pd"), ALU.mult)
+        tt(V("jb0", 16, 144), V("jm"), V("p1r"), ALU.add)
+        for k in range(5):
+            jb, jn, jo = "jb%d" % (k & 1), "jb%d" % (1 - (k & 1)), "jo%d" % (k & 1)
+            tr(V("tj", 0, 128), V(jb, 16, 144))
+            tr(V("tj", 128, 288), V(jb))
+            cp(V(jo), ind(V("tj"), JT))
+            if k < 4:
+                act(V(jn, 16, 144), ind(V(jb, 16, 144), V(jo, 0, 8)))
+            if k == 0:
+                tt(V("ap"), V(jb, 16, 144), V("cpos"), ALU.is_equal)
+                tt(V("a1"), V("ap"), V("id32"), ALU.max)
+            else:
+                tt(V("a%d" % (1 - (k & 1))), ind(V("a%d" % (k & 1)), V(jo, 0, 8)), V("ap"), ALU.max)
+            if k < 4:
+                act(V("ap"), V("a%d" % (1 - (k & 1))))
+            if first:
+                if k < 3:
+                    lu_tile(1 + 2 * (k & 1), (0, 1) if k < 2 else (2, 3))
+                if k == 3:
+                    lu_tile(3, (2, 3))
+                    lu_tile(0)
+                if k == 1:
+                    consts_b()
+                if k in (2, 3):
+                    consts_c((2 * k - 4, 2 * k - 3))
+            elif k == 3:
+                own_t((2, 3))
+        A = V("a1")
+        lin(V("act"), A, cc(9), 256.0)
+        scan(V("sz"), V("rst"), A, ALU.mult, ALU.add)
+        ts(V("ac"), A, -256.0, ALU.mult, 256.0, ALU.add)
+        tr(V("ai"), V("act"))
+        ts(S4("thr"), S4("sz"), 16.0, ALU.is_ge, 0.5, ALU.subtract)
+        lin(V("pay"), S4("sz"), -1.0, cc(6))
+        for b in range(4):
+            lin(blk("abo", b), blk("a1", b), 256.0, -256.0 + 32.0 * b / 2048)
+        for l in range(4):
+            if l > 0:
+                scan(V("cs"), V("rst") if l == 1 else run("d0t", l - 2, 128), V("x2t"), ALU.mult, ALU.max)
+            if l < 3:
+                ts(V("h64"), S4("thr"), 0.0, ALU.is_gt, 64.0, ALU.mult)
+            for b in range(4):
+                ts(blk("mm", b), blk("ai", b), end("thr", b), ALU.is_le, col("pay", b), ALU.mult)
+            if l > 0:
+                for b in range(4):
+                    lin(blk("ab2", b), blk("abo", b), 1.0, col("nrem", b))
+            if l < 3:
+                tt(V("base"), S4("sz") if l == 0 else V("size"), V("h64"), ALU.subtract)
+                for b in range(4):
+                    lin(blk("abb", b), blk("abo", b), 1.0, col("base", b))
+            else:
+                places(0)
+            tr(V("mt"), V("mm"))
+            if l > 0:
+                ts(V("wi", 16 + l - 1, 32, 4), S4("cs"), 2048.0, ALU.mult)
+            scan(V("red"), V("rst"), V("mt"), ALU.mult, ALU.max)
+            if l == 3:
+                for b in range(4):
+                    lin(blk("x2", b), blk("ab2", b), 1.0, end("red", b))
+                for b in range(1, 4):
+                    places(b)
+                tr(V("x2t"), V("x2"))
+                ts(V("wi", 0, 16), ind(V("rk"), RX), 255.5, ALU.add)
+                scan(V("cs"), run("d0t", 2, 128), V("x2t"), ALU.mult, ALU.max)
+                ts(V("wi", 16 + l, 32, 4), S4("cs"), 2048.0, ALU.mult)
+                break
+            sf = run("sf", l, 4)
+            for b in range(4):
+                lin(blk("xx", b), blk("abb", b), 1.0, end("red", b))
+            ts(V("nb"), V("base"), -1.0, ALU.mult, cc(8), ALU.add)
+            tt(sf, V("base"), S4("red"), ALU.add)
+            for b in range(4):
+                ts(blk("d0", b), blk("ac", b), end("red", b), ALU.add, col("nb", b), ALU.is_gt)
+            ts(V("s2h"), sf, 2.0, ALU.mult, 0.4, ALU.add)
+            if l == 2:
+                signs(l + 1, lambda b: col("sf", 4 * l + b))
+            lin(V("t1"), sf, 1.0, WHOLE)
+            for b in range(4):
+                lin(blk("x2", b), blk("abo" if l == 0 else "ab2", b), 1.0, end("red", b))
+            lin(V("size"), V("t1"), 1.0, -WHOLE)
+            act(V("ns"), sf, ACT.Sign, 1.0, -0.3)
+            lin(V("pay"), V("size"), -1.0, cc(6))
+            lin(V("nrem"), V("ns"), 32.0, -32.0)
+            if l < 2:
+                signs(l + 1, lambda b: col("sf", 4 * l + b))
+            if l == 0:
+                signs(0, lambda b: end("sz", b))
+            nm = run("d0t", l, 128)
+            tr(V("xxt"), V("xx"))
+            tr(nm, V("d0"))
+            for b in range(4):
+                ts(blk("ee", b), blk("xxt", b), col("s2h", b), ALU.is_le, 63.0 / 64, ALU.subtract)
+            if l == 2:
+                qz(V("gq", 0, 128), V("gs", 0, 128), V("gt"))
+                for b in range(4):
+                    for pr in range(2):
+                        k = [[0, 1], [2, 1], [3, 0], [3, 2]][b][pr]
+                        mm(bank(4 + b, 128), run("luq", k, 128), run("lus", k, 128),
+                           V("gq", 64 * pr, 64 * pr + 128), V("gs", 64 * pr, 64 * pr + 128), pr == 0, pr == 1)
+            tr(V("x2t"), V("x2"))
+            scan(V("thr"), nm, V("ee"), ALU.mult, ALU.add)
+            if first and l == 0:
+                lu_tile(2)
+                qz(V("pmq"), V("pms"), V("pmt"))
+            if first and l == 1:
+                qz(V("e32q"), V("e32s"), V("e32t"))
+                qz(V("luq"), V("lus"), V("lut"))
+                decode(0, XQ, XS, 256)
+        if first:
+            own_t(range(4))
+        arrive(mate, [LQ, LS], "aq%d" % t, 2)
+        if not first:
+            decode(0, LQ, LS, 256)
+            mate_t()
+        ts(V("wd", 0, 32), V("wi"), 15, ALU.bitwise_and)
+        ts(V("wd", 32, 64), V("wi"), 240, ALU.bitwise_and)
+        cp(ind(V("mv", 0, 256), V("exl")), V("wd"))
+        qz(V("mq", 0, 128), V("ms", 0, 128), V("mv"))
+        mm(bank(4, 128), V("pmq"), V("pms"), V("mq", 0, 128), V("ms", 0, 128), True, False)
+        mm(bank(4, 128), V("pmq"), V("pms"), V("mq", 32, 160), V("ms", 32, 160), False, True)
+        if first:
+            decode(0, LQ, LS, 256)
+        cp(V("coff"), bank(4, 32, 16))
+        ts(V("roff"), bank(4, 16), cc(12), ALU.add)
+        cp(V("cr", 0, 128), ind(V("iota"), V("coff", 0, 8)))
+        act(V("cr", 128, 256), ind(V("iota"), V("coff", 8, 16)))
+        if first:
+            mate_t()
+        cp(ind(V("sw"), V("roff")), V("cr"))
+        tr(V("te", 0, 96), V("sw", 0, 96))
+        tr(V("te", 96, 192), V("sw", 16, 112))
+        EL = "el%d" % t
+        cp(V(EL), ind(V("te"), ET))
+        send(mate, V("ll%d" % t, 0, 6), V(EL, 0, 6), "al%d" % t)
+        decode(0, XQ, XS, 256, False)
+        for b in range(4):
+            act(run("e32", b, K), ind(V("tw", PL * b + K, PL * b + PL), V(EL, 0, 6)), ACT.Copy, 0.5)
+        z = lambda i: run("zf", i, 16)
+        cp(V("zf", 0, 32), bank(4, 32))
+        ts(z(2), z(1), float(K), ALU.add)
+        ts(z(3), z(0), float(K), ALU.is_lt)
+        tt(z(4), z(0), z(2), ALU.subtract)
+        tt(z(5), z(4), z(3), ALU.mult)
+        tt(z(4), z(5), z(2), ALU.add)
+        cp(V("zoff"), z(4))
+        if first:
+            qz(V("vq"), V("vs"), V("vt"))
+        if t == 2:
+            cp(V("crf"), V("cr"))
+            for gi in range(8):
+                store("y", T.cl[gi:gi + 1, :], V("crf", 0, 256, 1, (16 * gi, 16 * gi + 1)))
+        LL = V("ll%d" % t, 0, 6)
+        arrive(mate, [LL], "al%d" % t, 1)
+        for b in range(4):
+            (cp if b < 2 else act)(V("et", b, 4 * K, 4), ind(run("tp", b, 256), LL))
+        qz(V("eq"), V("es"), V("et"))
+        decode(4, V("eq"), V("es"), 128)
+        for b in range(4):
+            tt(V("tw", PL * b, PL * b + K), bank(4 + b, K), run("e32", b, K), ALU.add)
+        for b in range(4):
+            w = ind(run("tw", b, PL), V("zoff"))
+            if b < 2:
+                act(V("ztile", b, 1024, 4), w, ACT.Copy, 1.0 / 64)
+            else:
+                ts(V("ztile", b, 1024, 4), w, 1.0 / 64, ALU.mult)
+        qz(V("zq"), V("zs"), V("ztile"))
+        for b in range(4):
+            mm(bank(b, 256), run("wq", b, 128), run("wsq", b, 128), V("zq"), V("zs"), False, True)
+        for b in range(4):
+            if b & 1:
+                act(V("xt1", b, 1024, 4), bank(b, 256), ACT.Copy, 1.0 / 32)
+            else:
+                ts(V("xt1", b, 1024, 4), bank(b, 256), 1.0 / 32, ALU.mult)
+        xt = "xt1"
+
+    qz(V("xq3"), V("xs3"), V(xt))
+    store("y", T.oc[:], V("xq3"), dt.uint8)
+    halves("ysb", V("vq"), V("vs"), "xq3", "xs3")
+    store("s", T.y[:], V("ysb"))
+    for k in range(4):
+        store("y", T.osc[4 * k:4 * k + 4, :], V("xs3", 0, 256, 1, (32 * k, 32 * k + 4)))
+
+    emit(g, T, ops)
+
+
+def emit(g, T, ops):
+    Q = {"v": g.vector, "s": g.scalar, "t": g.tensor, "g": g, "y": g.sync}
+    hist, total, semall = {}, {}, {}
+    known = {e: 0 for e in Q}
+    issued = {e: 0 for e in Q}
+    snap, waits = [], []
+    for i, o in enumerate(ops):
+        if o["sem"] is not None:
+            total[o["sem"]] = total.get(o["sem"], 0) + o["n"]
+            semall[o["sem"]] = semall.get(o["sem"], 0) | (1 << i)
+    for i, o in enumerate(ops):
+        e = o["e"]
+        deps = set()
+        for kind in ("r", "w"):
+            for name, m in o[kind]:
+                for (j, mj, wj) in hist.get(name, []):
+                    if not (m & mj):
+                        continue
+                    if name.startswith("ps"):
+                        if ops[j]["e"] != e or not o["acc"] and (wj or kind == "w"):
+                            deps.add(j)
+                    elif (wj or kind == "w") and (o["sem"] is None or ops[j]["sem"] != o["sem"]):
+                        deps.add(j)
+        w = []
+        if e == "x":
+            snap.append(semall[o["sem"]])
+        else:
+            for j in sorted(deps, reverse=True):
+                if not known[e] >> j & 1:
+                    w.append(j)
+                    known[e] |= snap[j]
+            if o["sem"] is None:
+                issued[e] |= 1 << i
+                snap.append(known[e] | issued[e])
+            else:
+                snap.append(known[e] | semall[o["sem"]])
+        waits.append(w)
+        for name, m in o["w"]:
+            hist[name] = [h for h in hist.get(name, []) if h[1] & ~m] + [(i, m, True)]
+        for name, m in o["r"]:
+            hist.setdefault(name, []).append((i, m, False))
+    wanted = set(j for w in waits for j in w)
+    count, mark, seen = {}, {}, {}
+    for i, o in enumerate(ops):
+        e = o["e"]
+        if e == "x":
+            continue
+        for j in waits[i]:
+            s, n = (ops[j]["sem"], total[ops[j]["sem"]]) if ops[j]["sem"] is not None else mark[j]
+            Q[e].wait_ge(T.sem[s], n)
+            seen[s] = max(seen.get(s, 0), n)
+        if o["sem"] is None and i in wanted:
+            s = "q" + e
+            count[s] = count.get(s, 0) + 1
+            mark[i] = (s, count[s])
+            o["fn"](Q[e]).then_inc(T.sem[s], 1)
+        elif o["sem"] is not None and o["sem"] != "sent":
+            o["fn"](Q[e]).then_inc(T.sem[o["sem"]], 16)
+        else:
+            o["fn"](Q[e])
+    for s, n in total.items():
+        if seen.get(s, 0) < n:
+            g.wait_ge(T.sem[s], n)

@@ -24,13 +24,13 @@ def _share(name, d, parts):
 
 
 for _d, _l in [
-    (BF, "xt0 1024 ut 512 vt 512 iota 256 gv 68 e32t 2048 lut 2048 pmt 512 p0r 128 p1r 128 pd 128 sel 128 jm 128 jb0 160 "
-         "jb1 160 tj 288 ap 128 a0 128 a1 128 ac 128 act 128 ai 128 xx 128 xxt 128 d0 128 d0t 384 ee 128 gt 512 "
+    (BF, "xt0 1024 ut 512 vt 512 iota 256 gv 68 e32t 2048 lut 2048 pmt 512 p0r 128 p1r 128 pd 128 sel 128 jm 128 jb 384 "
+         "tj 320 aa 128 ab 128 a4 128 a4c 128 ac 128 act 128 ai 128 xx 128 xxt 128 d0 128 d0t 384 ee 128 gt 512 "
          "mv 512 cr 256 sw 272 te 192 tw %d tp 1024 et 512 ztile 1024 xt1 1024" % (4 * PL)),
-    (F32, "pat 768 ssb 256 sb1 128 abo 128 ab2 128 abb 128 sz 128 thr 128 mm 128 mt 128 red 128 x2 128 x2t 128 cs 128 "
-          "rk 256 crf 256 zf 96 e32 384 ysb 256"),
+    (F32, "pat 768 ssb 256 sb0 128 sb1 128 abo 128 ab2 128 abb 128 sz 128 thr 128 mm 128 mt 128 red 128 x2 128 x2t 128 "
+          "cs 128 rk 256 crf 256 zf 96 e32 384 ysb 256"),
     (I32, "pin 16 ip 2 bi 16 wi 32 wd 64"),
-    (U16, "cl16 8 uoff 8 exl 4 poff 16 jo0 16 jo1 16 roff 16 coff 16 zoff 16 ll0 8 ll1 8 ll2 8 el0 16 el1 16 el2 16"),
+    (U16, "cl16 8 uoff 8 exl 4 poff 16 jo 32 roff 16 coff 16 zoff 16 ll0 8 ll1 8 ll2 8 el0 16 el1 16 el2 16"),
     (X4, "wq 512 uq 128 uq2 128 vq 128 e32q 512 luq 512 pmq 128 gq 192 mq 160 eq 128 zq 256 xq0 256 xq1 256 xq2 256 "
          "xq3 256 lq0 256 lq1 256 lq2 256"),
     (U8, "wsq 512 us 128 us2 128 vs 128 e32s 512 lus 512 pms 128 gs 192 ms 160 es 128 zs 256 xs0 256 xs1 256 xs2 256 "
@@ -39,7 +39,7 @@ for _d, _l in [
     _w = _l.split()
     for _i in range(0, len(_w), 2):
         _sb(_w[_i], int(_w[_i + 1]), _d)
-_share("cb", BF, [(n, 128) for n in ("jt", "key", "hm", "b32", "cpos", "id32", "rst", "kl", "ku")])
+_share("cb", BF, [(n, 128) for n in ("jt", "key", "hm", "cpos", "id32", "rst", "kl", "ku")])
 _share("cw", F32, [("cf", 16), ("cc", 32), ("rs", 64)])
 _share("sm", F32, [("pay", 4), ("nb", 4), ("s2h", 4), ("h64", 4), ("base", 4), ("sf", 16), ("t1", 4), ("size", 4),
                    ("ns", 4), ("nrem", 4)])
@@ -49,6 +49,7 @@ for _t in range(8):
 SEMAPHORES = (["qv", "qs", "qt", "qg", "dx", "du", "dp", "dw", "dv", "dout", "sent"]
               + ["aq%d" % t for t in range(3)] + ["al%d" % t for t in range(3)])
 WHOLE = 12582912.0
+CYC, WAKE, AHEAD = 0.00083, 0.2, 0.1
 
 
 def V(name, a=0, b=None, s=1, p=None):
@@ -77,6 +78,20 @@ def _mask(v):
     return m
 
 
+def _n(v):
+    return len(range(v[1], v[2], v[3]))
+
+
+def _time(o, a, k=1.0):
+    if o[5] is not None:
+        return 0.05 + 3.5 * CYC * _n(a)
+    if a[5] is not None:
+        return 0.06 + 1.5 * CYC * _n(o)
+    if SCRATCH[o[0]][2] == BF and SCRATCH[a[0]][2] == BF:
+        k *= 0.5
+    return CYC * max(64, k * _n(o))
+
+
 def rank_program(g, core, T, topo):
     rank = T.rank_of(core)
     if rank is None:
@@ -95,79 +110,82 @@ def rank_program(g, core, T, topo):
             x = x.indirect(ap(off))
         return x
 
-    def op(eng, fn, rd, wr, sem=None, n=0, acc=False):
+    def op(eng, fn, rd, wr, c, sem=None, n=0, acc=False, late=0.0, after=None):
         vs = [v for v in rd if isinstance(v, tuple)]
         r = [(v[0], _mask(v)) for v in vs] + [(v[5][0], _mask(v[5])) for v in vs + wr if v[5] is not None]
-        ops.append({"e": eng, "fn": fn, "r": r, "w": [(v[0], _mask(v)) for v in wr], "sem": sem, "n": n, "acc": acc})
+        ops.append({"e": eng, "fn": fn, "r": r, "w": [(v[0], _mask(v)) for v in wr], "sem": sem, "n": n, "acc": acc,
+                    "c": c, "late": late, "after": after})
+        return len(ops) - 1
 
     def tt(o, a, b, f):
-        op("v", lambda q: q.tensor_tensor(ap(o), ap(a), ap(b), f), [a, b], [o])
+        op("v", lambda q: q.tensor_tensor(ap(o), ap(a), ap(b), f), [a, b], [o], _time(o, a, 2.0))
 
     def ts(o, a, s1, f0, s2=None, f1=None):
         if f1 is None:
-            op("v", lambda q: q.tensor_scalar(ap(o), ap(a), ap(s1), None, f0), [a, s1], [o])
+            op("v", lambda q: q.tensor_scalar(ap(o), ap(a), ap(s1), None, f0), [a, s1], [o], _time(o, a))
         else:
-            op("v", lambda q: q.tensor_scalar(ap(o), ap(a), ap(s1), ap(s2), f0, f1), [a, s1, s2], [o])
+            op("v", lambda q: q.tensor_scalar(ap(o), ap(a), ap(s1), ap(s2), f0, f1), [a, s1, s2], [o], _time(o, a))
 
     def cp(o, a, cast=None):
-        op("v", lambda q: q.tensor_copy(ap(o, cast), ap(a, cast)), [a], [o])
+        op("v", lambda q: q.tensor_copy(ap(o, cast), ap(a, cast)), [a], [o], _time(o, a))
 
     def ms(o, c):
-        op("v", lambda q: q.memset(ap(o), c), [], [o])
+        op("v", lambda q: q.memset(ap(o), c), [], [o], _time(o, o))
 
     def tr(o, a):
-        op("v", lambda q: q.transpose(ap(o), ap(a)), [a], [o])
+        op("v", lambda q: q.transpose(ap(o), ap(a)), [a], [o], _time(o, a))
 
     def scan(o, a, b, f0, f1):
-        op("v", lambda q: q.tensor_tensor_scan(ap(o), ap(a), ap(b), 0.0, f0, f1), [a, b], [o])
+        op("v", lambda q: q.tensor_tensor_scan(ap(o), ap(a), ap(b), 0.0, f0, f1), [a, b], [o], _time(o, a))
 
     def qz(oq, osc, a):
-        op("v", lambda q: q.quantize_mx(ap(oq), ap(osc), ap(a)), [a], [oq, osc])
+        op("v", lambda q: q.quantize_mx(ap(oq), ap(osc), ap(a)), [a], [oq, osc], 0.012 + 0.00022 * _n(a))
 
     def act(o, a, f=ACT.Copy, scale=1.0, bias=None):
+        c = _time(o, a) if a[5] is not None else CYC * max(64, _n(o))
         if bias is None:
-            op("s", lambda q: q.activation(ap(o), ap(a), f, scale=ap(scale)), [a, scale], [o])
+            op("s", lambda q: q.activation(ap(o), ap(a), f, scale=ap(scale)), [a, scale], [o], c)
         else:
-            op("s", lambda q: q.activation(ap(o), ap(a), f, bias=ap(bias), scale=ap(scale)), [a, scale, bias], [o])
+            op("s", lambda q: q.activation(ap(o), ap(a), f, bias=ap(bias), scale=ap(scale)), [a, scale, bias], [o], c)
 
     def lin(o, a, scale, bias):
         act(o, a, ACT.Identity, scale, bias)
 
     def mm(o, wq, ws, xq, xs, start=True, stop=True):
         op("t", lambda q: q.matmul_mx(ap(o), ap(wq), ap(ws), ap(xq), ap(xs), start, stop), [wq, ws, xq, xs], [o],
-           acc=not start)
+           0.0006 * (_n(o) + 16), acc=not start)
 
     def iota(o, pattern, base, cm):
+        c = 0.13 + 2 * CYC * _n(o)
         if SCRATCH[o[0]][2] == I32:
-            op("g", lambda q: q.iota(ap(o), pattern, base, cm), [], [o])
+            op("g", lambda q: q.iota(ap(o), pattern, base, cm), [], [o], c)
         else:
-            op("g", lambda q: q.iota(ap(o), pattern, base, cm, allow_small_or_imprecise_dtypes=True), [], [o])
+            op("g", lambda q: q.iota(ap(o), pattern, base, cm, allow_small_or_imprecise_dtypes=True), [], [o], c)
 
     def select(o, pattern, f, fill, cm):
-        op("g", lambda q: q.affine_select(ap(o), ap(o), pattern, f, fill, 0, cm), [o], [o])
+        op("g", lambda q: q.affine_select(ap(o), ap(o), pattern, f, fill, 0, cm), [o], [o], 0.17 + 2 * CYC * _n(o))
 
-    def load(eng, o, src, sem, cast=None):
-        op(eng, lambda q: q.dma_start(ap(o, cast), src), [], [o], sem=sem, n=16)
+    def load(eng, o, src, sem, cast=None, late=2.2):
+        op(eng, lambda q: q.dma_start(ap(o, cast), src), [], [o], 0.1, sem=sem, n=16, late=late)
 
     def store(eng, dst, a, cast=None):
-        op(eng, lambda q: q.dma_start(dst, ap(a, cast)), [a], [], sem="dout", n=16)
+        op(eng, lambda q: q.dma_start(dst, ap(a, cast)), [a], [], 0.1, sem="dout", n=16, late=2.5)
 
     def send(to, o, a, rsem, cast=None):
         rid, pid = topo.addr(to, core)
         m = topo.mask(core, to)
-        op("g", lambda q: q.remote_dma(ap(o, cast), ap(a, cast), T.sem[rsem], T.sem["sent"], pid, rid, m), [a], [],
-           sem="sent", n=len(topo.engines(core, to)))
+        return op("g", lambda q: q.remote_dma(ap(o, cast), ap(a, cast), T.sem[rsem], T.sem["sent"], pid, rid, m), [a], [],
+                  0.5, sem="sent", n=len(topo.engines(core, to)), late=2.0 if cast is None else 4.0)
 
-    def arrive(frm, views, rsem, calls):
-        op("x", None, [], views, sem=rsem, n=calls * len(topo.engines(frm, core)))
+    def arrive(frm, views, rsem, sends):
+        op("x", None, [], views, 0.0, sem=rsem, n=len(sends) * len(topo.engines(frm, core)), after=sends)
 
-    S4 = lambda name: V(name, 31, 128, 32)
     blk = lambda name, b: V(name, 32 * b, 32 * b + 32)
     end = lambda name, b: col(name, 32 * b + 31)
     run = lambda name, i, n: V(name, n * i, n * i + n)
     bank = lambda b, n, a=0: V("ps%d" % b, a, n)
 
-    load("y", V("xt0"), T.x[:], "dx")
+    load("y", V("xt0"), T.x[:], "dx", late=3.3)
     load("s", V("ut"), T.u[:], "du")
     for gi in range(8):
         a1 = (gi >> 1) & 1
@@ -178,16 +196,15 @@ def rank_program(g, core, T, topo):
     load("y", V("vt"), T.v[:], "dv")
 
     iota(V("ip", 0, 1), [[0, 1]], 0, 1)
-    iota(V("jt"), [[0, 4], [1, 32]], 0, 0)
     iota(V("iota"), [[1, 256]], 0, 0)
+    iota(V("jt"), [[0, 4], [1, 32]], 0, 0)
+    iota(V("cpos"), [[0, 2], [32, 2], [0, 32]], 0, 0)
     iota(V("key"), [[0, 2], [128, 2], [1, 32]], 0, 0)
     iota(V("hm"), [[1, 2], [0, 64]], 0, 0)
     iota(V("gv"), [[-2, 34], [-2, 2]], 1, 0)
-    iota(V("e32t"), [[0, 2048]], 32, 0)
     ms(V("uoff", 0, 4), 0)
     ms(V("uoff", 4, 8), 64)
-    ms(V("jb0"), 0.0)
-    ms(V("jb1"), 0.0)
+    ms(V("jb"), 0.0)
     FIELDS = [(0, 1), (1, 1), (4, 1), (5, 1), (6, 1), (0, 7), (0, 31), (0, 3), (2, 3), (0, 15)]
     for i, (sh, mk) in enumerate(FIELDS):
         ts(col("bi", i), V("ip", 0, 1), sh, ALU.logical_shift_right, mk, ALU.bitwise_and)
@@ -195,9 +212,10 @@ def rank_program(g, core, T, topo):
     cp(V("cf", 0, 10), V("bi", 0, 10))
     B0, B1, B4, B5, B6, K7, J31, R3, Q3, R15 = [col("cf", i) for i in range(10)]
     cc = lambda i: col("cc", i)
-    lin(cc(0), B0, -288.0, 128.0)
-    lin(cc(1), B0, 9.0, K7)
+    lin(cc(0), B0, -160.0, 64.0)
+    lin(cc(1), B0, 5.0, R3)
     lin(cc(4), B5, -128.0, 0.0)
+    lin(cc(10), B5, -128.0, -64.0)
     lin(cc(5), B5, 128.0, J31)
     lin(cc(2), cc(0), B4, 0.0)
     for i, d in enumerate((-32.0, 0.0, 32.0)):
@@ -227,47 +245,41 @@ def rank_program(g, core, T, topo):
         ms(col("rs", c0), 1000.0)
     tt(V("ku"), V("key"), V("kl"), ALU.add)
     tt(V("kl"), V("key"), V("kl"), ALU.subtract)
-
     qz(V("uq"), V("us"), V("ut"))
+    qz(V("vq"), V("vs"), V("vt"))
     ts(V("id32"), V("jt"), J31, ALU.is_equal)
     cp(V("uq2"), ind(V("uq"), V("uoff")), dt.uint32)
     cp(V("us2"), ind(V("us"), V("uoff")))
     cp(V("poff"), V("pin"))
-    tt(V("b32"), V("iota", 0, 128), V("jt"), ALU.subtract)
+    for h in range(2):
+        lin(run("p1r", h, 64), ind(V("iota"), V("poff", 8 + 4 * h, 12 + 4 * h)), 1.0, cc(4 + 6 * h))
+        lin(run("p0r", h, 64), ind(V("iota"), V("poff", 4 * h, 4 + 4 * h)), 1.0, cc(4 + 6 * h))
+    tt(V("pd"), V("p0r"), V("p1r"), ALU.subtract)
+    ts(cc(7), J31, 0.0, ALU.is_equal, 1000.0, ALU.mult)
+    ts(V("cpos"), V("cpos"), J31, ALU.add)
+    ts(V("rst"), V("jt"), 0.0, ALU.not_equal)
+    ts(cc(8), cc(7), 0.3, ALU.add)
     JT, ET, RX = V("cl16", 0, 1), V("cl16", 2, 3), V("cl16", 4, 5)
-
-    act(V("pat", 128, 256), V("kl"), ACT.Sign, 1.0, cc(21))
-    lin(V("p1r"), ind(V("iota"), V("poff", 8, 16)), 1.0, cc(4))
-    lin(V("p0r"), ind(V("iota"), V("poff", 0, 8)), 1.0, cc(4))
+    ts(JT, cc(1), 16.0, ALU.mult, cc(2), ALU.add)
+    ts(ET, cc(18), 191.0, ALU.min)
+    ts(RX, Q3, 64.0, ALU.mult, cc(19), ALU.add)
+    ts(V("exl"), V("iota", 0, 256, 64), cc(3), ALU.add)
+    for sl in range(4):
+        ts(V("pmt", sl, 512, 4), V("iota", 0, 128), -16.0 * sl, ALU.add, cc(11), ALU.is_equal)
+    qz(V("pmq"), V("pms"), V("pmt"))
+    for i in range(3):
+        act(run("pat", i, 128), V("kl"), ACT.Sign, 1.0, cc(20 + i))
+        act(run("pat", 3 + i, 128), V("ku"), ACT.Sign, -1.0, cc(24 + i))
     select(V("pat", 128, 256), [[-1, 128]], ALU.not_equal, -513.0, 1)
-    select(V("e32t"), [[1, 4], [-4, 128], [-1, 4]], ALU.is_equal, 0.0, 4)
-
-    def patterns():
-        for i in (0, 2):
-            act(run("pat", i, 128), V("kl"), ACT.Sign, 1.0, cc(20 + i))
-        for i in range(3):
-            act(run("pat", 3 + i, 128), V("ku"), ACT.Sign, -1.0, cc(24 + i))
-
-    def lu_tile(k, slots=range(4)):
-        pair = [(1, 2), (2, 2), (0, 1), (0, 0)][k]
-        for sl in slots:
+    for k, pair in enumerate([(1, 2), (2, 2), (0, 1), (0, 0)]):
+        for sl in range(4):
             lin(V("lut", 512 * k + sl, 512 * k + 512, 4), run("pat", pair[sl & 1] + 3 * (sl >> 1), 128), 0.25, 0.25)
-
-    def consts_a():
-        ts(cc(7), J31, 0.0, ALU.is_equal, 1000.0, ALU.mult)
-        ts(col("cl16", 0), cc(1), 16.0, ALU.mult, cc(2), ALU.add)
-        ts(V("cpos"), V("b32"), J31, ALU.add)
-        ts(V("rst"), V("jt"), 0.0, ALU.not_equal)
-        ts(cc(8), cc(7), 0.3, ALU.add)
-
-    def consts_b():
-        ts(col("cl16", 2), cc(18), 191.0, ALU.min)
-        ts(col("cl16", 4), Q3, 64.0, ALU.mult, cc(19), ALU.add)
-        ts(V("exl"), V("iota", 0, 256, 64), cc(3), ALU.add)
-
-    def consts_c(slots):
-        for sl in slots:
-            ts(V("pmt", sl, 512, 4), V("iota", 0, 128), -16.0 * sl, ALU.add, cc(11), ALU.is_equal)
+        qz(run("luq", k, 128), run("lus", k, 128), run("lut", k, 512))
+    for b in range(4):
+        iota(run("e32t", b, 512), [[0, 512]], 32, 0)
+        op("g", lambda q, b=b: q.affine_select(ap(run("e32t", b, 512)), ap(run("e32t", b, 512)), [[-4, 128], [-1, 4]],
+                                               ALU.is_equal, 0.0, b, 4), [run("e32t", b, 512)], [run("e32t", b, 512)], 1.02)
+        qz(run("e32q", b, 128), run("e32s", b, 128), run("e32t", b, 512))
 
     SEG = [(0, 32, 1), (32, 17, 0), (49, 9, 0), (58, 5, 0)]
 
@@ -275,22 +287,10 @@ def rank_program(g, core, T, topo):
         for b in range(4):
             mm(bank(bank0 + b, n), run("e32q", b, 128), run("e32s", b, 128), xq, xs, True, stop)
 
-    def signs(l, w):
+    def signs(l, b, w):
         c0, n, v0 = SEG[l]
-        for b in range(4):
-            e0 = 4 * (64 * (b >> 1) + c0) + (b & 1)
-            act(V("gt", e0, e0 + 4 * n - 1, 2), V("gv", 2 * v0, 2 * (v0 + n)), ACT.Sign, 0.5, w(b))
-
-    def places(b):
-        scan(V("rk", 64 * b, 64 * b + 63), V("rs", 0, 63), bank(4 + b, 63), ALU.add, ALU.min)
-
-    def own_t(bs):
-        for b in bs:
-            act(V("tw", PL * b + K, PL * b + PL), bank(b, 256), ACT.Copy, 2.0)
-
-    def mate_t():
-        for b in range(4):
-            act(run("tp", b, 256), bank(b, 256), ACT.Copy, 1.0 / 32)
+        e0 = 4 * (64 * (b >> 1) + c0) + (b & 1)
+        act(V("gt", e0, e0 + 4 * n - 1, 2), V("gv", 2 * v0, 2 * (v0 + n)), ACT.Sign, 0.5, w)
 
     def halves(dst, wq, ws, xq, xs):
         for h in range(2):
@@ -298,163 +298,139 @@ def rank_program(g, core, T, topo):
         cp(V(dst, 0, 128), bank(4, 128))
         act(V(dst, 128, 256), bank(5, 128))
 
+    def above(h):
+        H = lambda name: run(name, h, 64)
+        J = lambda i: V("jb", 192 * h + 96 * i + 16, 192 * h + 96 * i + 80)
+        jo = V("jo", 16 * h, 16 * h + 4)
+
+        def offsets(i):
+            tr(V("tj", 160 * h, 160 * h + 64), J(i))
+            tr(V("tj", 160 * h + 64, 160 * h + 160), run("jb", 2 * h + i, 96))
+            cp(run("jo", h, 16), ind(run("tj", h, 160), JT))
+
+        act(H("sb1"), ind(V("ssb"), V("poff", 8 + 4 * h, 12 + 4 * h)))
+        cp(H("sb0"), ind(V("ssb"), V("poff", 4 * h, 4 + 4 * h)))
+        tt(H("sel"), H("sb0"), H("sb1"), ALU.is_ge)
+        tt(H("jm"), H("sel"), H("pd"), ALU.mult)
+        tt(J(0), H("jm"), H("p1r"), ALU.add)
+        offsets(0)
+        tt(H("ab"), J(0), H("cpos"), ALU.is_equal)
+        tt(H("aa"), H("ab"), H("id32"), ALU.max)
+        for i in range(3):
+            act(J(1 - (i & 1)), ind(J(i & 1), jo))
+        tt(H("ab"), ind(H("aa"), jo), H("id32"), ALU.max)
+        tt(H("a4"), ind(H("ab"), jo), H("id32"), ALU.max)
+        tt(H("a4c"), ind(H("ab"), jo), H("id32"), ALU.max)
+        offsets(1)
+        for i in range(3):
+            act(J(i & 1), ind(J(1 - (i & 1)), jo))
+        tt(H("aa"), ind(H("a4"), jo), H("a4c"), ALU.max)
+        tt(H("ab"), ind(H("aa"), jo), H("a4"), ALU.max)
+        tt(H("aa"), ind(H("ab"), jo), H("a4"), ALU.max)
+        tt(H("a4c"), ind(H("ab"), jo), H("a4"), ALU.max)
+        offsets(0)
+        tt(H("a4"), ind(H("aa"), jo), H("a4c"), ALU.max)
+
+    def levels(h):
+        H = lambda name: run(name, h, 64)
+        S2 = lambda name: V(name, 64 * h + 31, 64 * h + 64, 32)
+        P2 = lambda name: run(name, h, 2)
+        mask = lambda l: H("rst") if l == 0 else run("d0t", 2 * l - 2 + h, 64)
+        bs = (2 * h, 2 * h + 1)
+        lin(H("act"), H("a4"), cc(9), 256.0)
+        scan(H("sz"), H("rst"), H("a4"), ALU.mult, ALU.add)
+        ts(H("ac"), H("a4"), -256.0, ALU.mult, 256.0, ALU.add)
+        tr(H("ai"), H("act"))
+        ts(S2("thr"), S2("sz"), 16.0, ALU.is_ge, 0.5, ALU.subtract)
+        lin(P2("pay"), S2("sz"), -1.0, cc(6))
+        for b in bs:
+            lin(blk("abo", b), blk("a4", b), 256.0, -256.0 + 32.0 * b / 2048)
+            signs(0, b, end("sz", b))
+        for l in range(4):
+            for b in bs:
+                ts(blk("mm", b), blk("ai", b), end("thr", b), ALU.is_le, col("pay", b), ALU.mult)
+            if l < 3:
+                ts(P2("h64"), S2("thr"), 0.0, ALU.is_gt, 64.0, ALU.mult)
+                tt(P2("base"), S2("sz") if l == 0 else P2("size"), P2("h64"), ALU.subtract)
+                ts(P2("nb"), P2("base"), -1.0, ALU.mult, cc(8), ALU.add)
+                for b in bs:
+                    lin(blk("abb", b), blk("abo", b), 1.0, col("base", b))
+            tr(H("mt"), H("mm"))
+            scan(H("red"), H("rst"), H("mt"), ALU.mult, ALU.max)
+            if l < 3:
+                sf = run("sf", 2 * l + h, 2)
+                for b in bs:
+                    lin(blk("xx", b), blk("abb", b), 1.0, end("red", b))
+                tt(sf, P2("base"), S2("red"), ALU.add)
+                for b in bs:
+                    ts(blk("d0", b), blk("ac", b), end("red", b), ALU.add, col("nb", b), ALU.is_gt)
+                ts(P2("s2h"), sf, 2.0, ALU.mult, 0.4, ALU.add)
+            for b in bs:
+                lin(blk("x2", b), blk("abo" if l == 0 else "ab2", b), 1.0, end("red", b))
+            tr(H("x2t"), H("x2"))
+            scan(H("cs"), mask(l), H("x2t"), ALU.mult, ALU.max)
+            ts(V("wi", 16 + 8 * h + l, 24 + 8 * h, 4), S2("cs"), 2048.0, ALU.mult)
+            if l == 3:
+                break
+            lin(P2("t1"), sf, 1.0, WHOLE)
+            lin(P2("size"), P2("t1"), 1.0, -WHOLE)
+            lin(P2("pay"), P2("size"), -1.0, cc(6))
+            act(P2("ns"), sf, ACT.Sign, 1.0, -0.3)
+            lin(P2("nrem"), P2("ns"), 32.0, -32.0)
+            for b in bs:
+                lin(blk("ab2", b), blk("abo", b), 1.0, col("nrem", b))
+                signs(l + 1, b, col("sf", 4 * l + b))
+            tr(H("xxt"), H("xx"))
+            tr(mask(l + 1), H("d0"))
+            for b in bs:
+                ts(blk("ee", b), blk("xxt", b), col("s2h", b), ALU.is_le, 63.0 / 64, ALU.subtract)
+            scan(H("thr"), mask(l + 1), H("ee"), ALU.mult, ALU.add)
+
     xt = "xt0"
     for t, m in enumerate(PARTNER):
         mate = T.cores[rank ^ m]
         XQ, XS = V("xq%d" % t), V("xs%d" % t)
         LQ, LS = V("lq%d" % t), V("ls%d" % t)
-        first = t == 0
         qz(XQ, XS, V(xt))
-        if first:
-            consts_a()
         halves("ssb", V("uq2"), V("us2"), XQ[0], XS[0])
-        send(mate, LQ, XQ, "aq%d" % t, dt.uint8)
-        send(mate, LS, XS, "aq%d" % t)
-        act(V("sb1"), ind(V("ssb"), V("poff", 8, 16)))
-        cp(V("mm"), ind(V("ssb"), V("poff", 0, 8)))
-        if first:
-            tt(V("pd"), V("p0r"), V("p1r"), ALU.subtract)
-            patterns()
-        else:
-            decode(0, XQ, XS, 256)
-            own_t((0, 1))
-        tt(V("sel"), V("mm"), V("sb1"), ALU.is_ge)
-        tt(V("jm"), V("sel"), V("pd"), ALU.mult)
-        tt(V("jb0", 16, 144), V("jm"), V("p1r"), ALU.add)
-        for k in range(5):
-            jb, jn, jo = "jb%d" % (k & 1), "jb%d" % (1 - (k & 1)), "jo%d" % (k & 1)
-            tr(V("tj", 0, 128), V(jb, 16, 144))
-            tr(V("tj", 128, 288), V(jb))
-            cp(V(jo), ind(V("tj"), JT))
-            if k < 4:
-                act(V(jn, 16, 144), ind(V(jb, 16, 144), V(jo, 0, 8)))
-            if k == 0:
-                tt(V("ap"), V(jb, 16, 144), V("cpos"), ALU.is_equal)
-                tt(V("a1"), V("ap"), V("id32"), ALU.max)
-            else:
-                tt(V("a%d" % (1 - (k & 1))), ind(V("a%d" % (k & 1)), V(jo, 0, 8)), V("ap"), ALU.max)
-            if k < 4:
-                act(V("ap"), V("a%d" % (1 - (k & 1))))
-            if first:
-                if k < 3:
-                    lu_tile(1 + 2 * (k & 1), (0, 1) if k < 2 else (2, 3))
-                if k == 3:
-                    lu_tile(3, (2, 3))
-                    lu_tile(0)
-                if k == 1:
-                    consts_b()
-                if k in (2, 3):
-                    consts_c((2 * k - 4, 2 * k - 3))
-            elif k == 3:
-                own_t((2, 3))
-        A = V("a1")
-        lin(V("act"), A, cc(9), 256.0)
-        scan(V("sz"), V("rst"), A, ALU.mult, ALU.add)
-        ts(V("ac"), A, -256.0, ALU.mult, 256.0, ALU.add)
-        tr(V("ai"), V("act"))
-        ts(S4("thr"), S4("sz"), 16.0, ALU.is_ge, 0.5, ALU.subtract)
-        lin(V("pay"), S4("sz"), -1.0, cc(6))
+        sends = [send(mate, LQ, XQ, "aq%d" % t, dt.uint8), send(mate, LS, XS, "aq%d" % t)]
+        decode(0, XQ, XS, 256)
         for b in range(4):
-            lin(blk("abo", b), blk("a1", b), 256.0, -256.0 + 32.0 * b / 2048)
-        for l in range(4):
-            if l > 0:
-                scan(V("cs"), V("rst") if l == 1 else run("d0t", l - 2, 128), V("x2t"), ALU.mult, ALU.max)
-            if l < 3:
-                ts(V("h64"), S4("thr"), 0.0, ALU.is_gt, 64.0, ALU.mult)
-            for b in range(4):
-                ts(blk("mm", b), blk("ai", b), end("thr", b), ALU.is_le, col("pay", b), ALU.mult)
-            if l > 0:
-                for b in range(4):
-                    lin(blk("ab2", b), blk("abo", b), 1.0, col("nrem", b))
-            if l < 3:
-                tt(V("base"), S4("sz") if l == 0 else V("size"), V("h64"), ALU.subtract)
-                for b in range(4):
-                    lin(blk("abb", b), blk("abo", b), 1.0, col("base", b))
-            else:
-                places(0)
-            tr(V("mt"), V("mm"))
-            if l > 0:
-                ts(V("wi", 16 + l - 1, 32, 4), S4("cs"), 2048.0, ALU.mult)
-            scan(V("red"), V("rst"), V("mt"), ALU.mult, ALU.max)
-            if l == 3:
-                for b in range(4):
-                    lin(blk("x2", b), blk("ab2", b), 1.0, end("red", b))
-                for b in range(1, 4):
-                    places(b)
-                tr(V("x2t"), V("x2"))
-                ts(V("wi", 0, 16), ind(V("rk"), RX), 255.5, ALU.add)
-                scan(V("cs"), run("d0t", 2, 128), V("x2t"), ALU.mult, ALU.max)
-                ts(V("wi", 16 + l, 32, 4), S4("cs"), 2048.0, ALU.mult)
-                break
-            sf = run("sf", l, 4)
-            for b in range(4):
-                lin(blk("xx", b), blk("abb", b), 1.0, end("red", b))
-            ts(V("nb"), V("base"), -1.0, ALU.mult, cc(8), ALU.add)
-            tt(sf, V("base"), S4("red"), ALU.add)
-            for b in range(4):
-                ts(blk("d0", b), blk("ac", b), end("red", b), ALU.add, col("nb", b), ALU.is_gt)
-            ts(V("s2h"), sf, 2.0, ALU.mult, 0.4, ALU.add)
-            if l == 2:
-                signs(l + 1, lambda b: col("sf", 4 * l + b))
-            lin(V("t1"), sf, 1.0, WHOLE)
-            for b in range(4):
-                lin(blk("x2", b), blk("abo" if l == 0 else "ab2", b), 1.0, end("red", b))
-            lin(V("size"), V("t1"), 1.0, -WHOLE)
-            act(V("ns"), sf, ACT.Sign, 1.0, -0.3)
-            lin(V("pay"), V("size"), -1.0, cc(6))
-            lin(V("nrem"), V("ns"), 32.0, -32.0)
-            if l < 2:
-                signs(l + 1, lambda b: col("sf", 4 * l + b))
-            if l == 0:
-                signs(0, lambda b: end("sz", b))
-            nm = run("d0t", l, 128)
-            tr(V("xxt"), V("xx"))
-            tr(nm, V("d0"))
-            for b in range(4):
-                ts(blk("ee", b), blk("xxt", b), col("s2h", b), ALU.is_le, 63.0 / 64, ALU.subtract)
-            if l == 2:
-                qz(V("gq", 0, 128), V("gs", 0, 128), V("gt"))
-                for b in range(4):
-                    for pr in range(2):
-                        k = [[0, 1], [2, 1], [3, 0], [3, 2]][b][pr]
-                        mm(bank(4 + b, 128), run("luq", k, 128), run("lus", k, 128),
-                           V("gq", 64 * pr, 64 * pr + 128), V("gs", 64 * pr, 64 * pr + 128), pr == 0, pr == 1)
-            tr(V("x2t"), V("x2"))
-            scan(V("thr"), nm, V("ee"), ALU.mult, ALU.add)
-            if first and l == 0:
-                lu_tile(2)
-                qz(V("pmq"), V("pms"), V("pmt"))
-            if first and l == 1:
-                qz(V("e32q"), V("e32s"), V("e32t"))
-                qz(V("luq"), V("lus"), V("lut"))
-                decode(0, XQ, XS, 256)
-        if first:
-            own_t(range(4))
-        arrive(mate, [LQ, LS], "aq%d" % t, 2)
-        if not first:
-            decode(0, LQ, LS, 256)
-            mate_t()
+            for h in range(2):
+                act(V("tw", PL * b + K + 128 * h, PL * b + K + 128 * h + 128), bank(b, 128 * h + 128, 128 * h), ACT.Copy, 2.0)
+        arrive(mate, [LQ, LS], "aq%d" % t, sends)
+        decode(0, LQ, LS, 256)
+        for b in range(4):
+            for h in range(2):
+                act(run("tp", 2 * b + h, 128), bank(b, 128 * h + 128, 128 * h), ACT.Copy, 1.0 / 32)
+        decode(0, XQ, XS, 256, False)
+        for h in range(2):
+            above(h)
+            levels(h)
+        qz(V("gq", 0, 128), V("gs", 0, 128), V("gt"))
+        for b in range(4):
+            for pr in range(2):
+                k = [[0, 1], [2, 1], [3, 0], [3, 2]][b][pr]
+                mm(bank(4 + b, 128), run("luq", k, 128), run("lus", k, 128),
+                   V("gq", 64 * pr, 64 * pr + 128), V("gs", 64 * pr, 64 * pr + 128), pr == 0, pr == 1)
+            scan(V("rk", 64 * b, 64 * b + 63), V("rs", 0, 63), bank(4 + b, 63), ALU.add, ALU.min)
+        ts(V("wi", 0, 16), ind(V("rk"), RX), 255.5, ALU.add)
         ts(V("wd", 0, 32), V("wi"), 15, ALU.bitwise_and)
         ts(V("wd", 32, 64), V("wi"), 240, ALU.bitwise_and)
         cp(ind(V("mv", 0, 256), V("exl")), V("wd"))
         qz(V("mq", 0, 128), V("ms", 0, 128), V("mv"))
         mm(bank(4, 128), V("pmq"), V("pms"), V("mq", 0, 128), V("ms", 0, 128), True, False)
         mm(bank(4, 128), V("pmq"), V("pms"), V("mq", 32, 160), V("ms", 32, 160), False, True)
-        if first:
-            decode(0, LQ, LS, 256)
         cp(V("coff"), bank(4, 32, 16))
         ts(V("roff"), bank(4, 16), cc(12), ALU.add)
         cp(V("cr", 0, 128), ind(V("iota"), V("coff", 0, 8)))
         act(V("cr", 128, 256), ind(V("iota"), V("coff", 8, 16)))
-        if first:
-            mate_t()
         cp(ind(V("sw"), V("roff")), V("cr"))
         tr(V("te", 0, 96), V("sw", 0, 96))
         tr(V("te", 96, 192), V("sw", 16, 112))
         EL = "el%d" % t
         cp(V(EL), ind(V("te"), ET))
-        send(mate, V("ll%d" % t, 0, 6), V(EL, 0, 6), "al%d" % t)
-        decode(0, XQ, XS, 256, False)
+        sends = [send(mate, V("ll%d" % t, 0, 6), V(EL, 0, 6), "al%d" % t)]
         for b in range(4):
             act(run("e32", b, K), ind(V("tw", PL * b + K, PL * b + PL), V(EL, 0, 6)), ACT.Copy, 0.5)
         z = lambda i: run("zf", i, 16)
@@ -465,14 +441,12 @@ def rank_program(g, core, T, topo):
         tt(z(5), z(4), z(3), ALU.mult)
         tt(z(4), z(5), z(2), ALU.add)
         cp(V("zoff"), z(4))
-        if first:
-            qz(V("vq"), V("vs"), V("vt"))
         if t == 2:
-            cp(V("crf"), V("cr"))
+            act(V("crf"), V("cr"))
             for gi in range(8):
                 store("y", T.cl[gi:gi + 1, :], V("crf", 0, 256, 1, (16 * gi, 16 * gi + 1)))
         LL = V("ll%d" % t, 0, 6)
-        arrive(mate, [LL], "al%d" % t, 1)
+        arrive(mate, [LL], "al%d" % t, sends)
         for b in range(4):
             (cp if b < 2 else act)(V("et", b, 4 * K, 4), ind(run("tp", b, 256), LL))
         qz(V("eq"), V("es"), V("et"))
@@ -507,55 +481,90 @@ def rank_program(g, core, T, topo):
 
 def emit(g, T, ops):
     Q = {"v": g.vector, "s": g.scalar, "t": g.tensor, "g": g, "y": g.sync}
-    hist, total, semall = {}, {}, {}
-    known = {e: 0 for e in Q}
-    issued = {e: 0 for e in Q}
-    snap, waits = [], []
+    n = len(ops)
+    hist, total, members = {}, {}, {}
     for i, o in enumerate(ops):
         if o["sem"] is not None:
             total[o["sem"]] = total.get(o["sem"], 0) + o["n"]
-            semall[o["sem"]] = semall.get(o["sem"], 0) | (1 << i)
+            members.setdefault(o["sem"], []).append(i)
+    deps, before, lasty = [], [], None
     for i, o in enumerate(ops):
-        e = o["e"]
-        deps = set()
+        d, b = set(), set(o["after"] or [])
         for kind in ("r", "w"):
             for name, m in o[kind]:
                 for (j, mj, wj) in hist.get(name, []):
                     if not (m & mj):
                         continue
                     if name.startswith("ps"):
-                        if ops[j]["e"] != e or not o["acc"] and (wj or kind == "w"):
-                            deps.add(j)
+                        if ops[j]["e"] != o["e"] or not o["acc"] and (wj or kind == "w"):
+                            d.add(j)
+                        elif o["acc"]:
+                            b.add(j)
                     elif (wj or kind == "w") and (o["sem"] is None or ops[j]["sem"] != o["sem"]):
-                        deps.add(j)
-        w = []
-        if e == "x":
-            snap.append(semall[o["sem"]])
-        else:
-            for j in sorted(deps, reverse=True):
-                if not known[e] >> j & 1:
-                    w.append(j)
-                    known[e] |= snap[j]
-            if o["sem"] is None:
-                issued[e] |= 1 << i
-                snap.append(known[e] | issued[e])
-            else:
-                snap.append(known[e] | semall[o["sem"]])
-        waits.append(w)
+                        d.add(j)
+        for j in d:
+            b.update(members[ops[j]["sem"]] if ops[j]["sem"] is not None else [j])
+        if o["e"] == "y":
+            if lasty is not None:
+                b.add(lasty)
+            lasty = i
+        deps.append(d)
+        before.append(b)
         for name, m in o["w"]:
             hist[name] = [h for h in hist.get(name, []) if h[1] & ~m] + [(i, m, True)]
         for name, m in o["r"]:
             hist.setdefault(name, []).append((i, m, False))
-    wanted = set(j for w in waits for j in w)
+    way, after, left = [0.0] * n, [[] for _ in range(n)], [len(b) for b in before]
+    lag = lambda j, i: (ops[j]["late"] + WAKE) if j in deps[i] or ops[i]["e"] == "x" or ops[j]["e"] != ops[i]["e"] else 0.0
+    for i in range(n - 1, -1, -1):
+        way[i] += ops[i]["c"] + (ops[i]["late"] if not after[i] else 0.0)
+        for j in before[i]:
+            after[j].append(i)
+            way[j] = max(way[j], way[i] + lag(j, i))
+    free, ready, can, order = {e: 0.0 for e in "vstgyx"}, [i for i in range(n) if not left[i]], [0.0] * n, []
+    while ready:
+        at = lambda i: max(can[i], free[ops[i]["e"]])
+        i0 = min(ready, key=at)
+        near = [i for i in ready if ops[i]["e"] == ops[i0]["e"] and at(i) <= at(i0) + min(ops[i0]["c"], AHEAD)]
+        i = max(near, key=lambda k: (way[k], -k))
+        ready.remove(i)
+        order.append(i)
+        done = at(i) + ops[i]["c"]
+        free[ops[i]["e"]] = done
+        for k in after[i]:
+            can[k] = max(can[k], done + lag(i, k))
+            left[k] -= 1
+            if not left[k]:
+                ready.append(k)
+    known, issued = {e: 0 for e in Q}, {e: 0 for e in Q}
+    place = {i: k for k, i in enumerate(order)}
+    snap, waits = {}, {}
+    for i in order:
+        o, w = ops[i], []
+        e, all_ = o["e"], sum(1 << j for j in members.get(o["sem"], []))
+        if e == "x":
+            snap[i] = all_
+            continue
+        for j in sorted(deps[i], key=lambda k: -place[k]):
+            if not known[e] >> j & 1:
+                w.append(j)
+                known[e] |= snap[j]
+        if o["sem"] is None:
+            issued[e] |= 1 << i
+            all_ = issued[e]
+        snap[i] = known[e] | all_
+        waits[i] = w
+    wanted = set(j for w in waits.values() for j in w)
     count, mark, seen = {}, {}, {}
-    for i, o in enumerate(ops):
+    for i in order:
+        o = ops[i]
         e = o["e"]
         if e == "x":
             continue
         for j in waits[i]:
-            s, n = (ops[j]["sem"], total[ops[j]["sem"]]) if ops[j]["sem"] is not None else mark[j]
-            Q[e].wait_ge(T.sem[s], n)
-            seen[s] = max(seen.get(s, 0), n)
+            s, k = (ops[j]["sem"], total[ops[j]["sem"]]) if ops[j]["sem"] is not None else mark[j]
+            Q[e].wait_ge(T.sem[s], k)
+            seen[s] = max(seen.get(s, 0), k)
         if o["sem"] is None and i in wanted:
             s = "q" + e
             count[s] = count.get(s, 0) + 1
@@ -565,6 +574,6 @@ def emit(g, T, ops):
             o["fn"](Q[e]).then_inc(T.sem[o["sem"]], 16)
         else:
             o["fn"](Q[e])
-    for s, n in total.items():
-        if seen.get(s, 0) < n:
-            g.wait_ge(T.sem[s], n)
+    for s, k in total.items():
+        if seen.get(s, 0) < k:
+            g.wait_ge(T.sem[s], k)

@@ -5,6 +5,9 @@ ACT = ActivationFunctionType
 C, K = 256, 96
 PARTNER = [1, 2, 4]
 PL = K + C
+PASSES = [[0], [1, 2], [3]]
+SEG = [(32, 1), (17, 0), (9, 0), (5, 0)]
+NP = len(PASSES)
 F32, BF, I32, U16, X4, U8 = "float32", "bfloat16", "int32", "uint16", "float8_e4m3fn_x4", "uint8"
 
 SCRATCH = {}
@@ -24,32 +27,37 @@ def _share(name, d, parts):
 
 
 for _d, _l in [
-    (BF, "xt0 1024 ut 512 vt 512 iota 256 gv 68 e32t 2048 lut 2048 pmt 512 p0r 128 p1r 128 pd 128 sel 128 jm 128 jb 384 "
-         "tj 320 aa 128 ab 128 a4 128 a4c 128 ac 128 act 128 ai 128 xx 128 xxt 128 d0 128 d0t 384 ee 128 gt 512 "
-         "mv 512 cr 256 sw 272 te 192 tw %d tp 1024 et 512 ztile 1024 xt1 1024" % (4 * PL)),
-    (F32, "pat 768 ssb 256 sb0 128 sb1 128 abo 128 ab2 128 abb 128 sz 128 thr 128 mm 128 mt 128 red 128 x2 128 x2t 128 "
-          "cs 128 rk 256 crf 256 zf 96 e32 384 ysb 256"),
-    (I32, "pin 16 ip 2 bi 16 wi 32 wd 64"),
-    (U16, "cl16 8 uoff 8 exl 4 poff 16 jo 32 roff 16 coff 16 zoff 16 ll0 8 ll1 8 ll2 8 el0 16 el1 16 el2 16"),
-    (X4, "wq 512 uq 128 uq2 128 vq 128 e32q 512 luq 512 pmq 128 gq 192 mq 160 eq 128 zq 256 xq0 256 xq1 256 xq2 256 "
-         "xq3 256 lq0 256 lq1 256 lq2 256"),
-    (U8, "wsq 512 us 128 us2 128 vs 128 e32s 512 lus 512 pms 128 gs 192 ms 160 es 128 zs 256 xs0 256 xs1 256 xs2 256 "
-         "xs3 256 ls0 256 ls1 256 ls2 256"),
+    (BF, "xt0 1024 ut 512 vt 512 iota 256 gv 68 e32t 516 lut 1024 pmt 768 elt 704 xm 128 xn 128 jj 320 "
+         "v1 128 va 128 vb 128 v5 128 v22 160 nn 256 szs 256 st 224 lt 288 lb 130 dl 128 tb 320 uu 128 "
+         "ss 128 ny 128 ls 128 cx 192 cv 256 wt 256 gt 2048 ab 224 sc0 1088 sc1 1088 "
+         "sc2 1088 sc3 1088 mv 512 tw %d tp 1024 tq 1024 eh 384 ztile 1024 xt1 1024" % (4 * PL)),
+    (F32, "ssb 128 sb0 64 rk 1024 rs 512 te 192 crf 256 zf 96 ysb 256 pf 6 pg 16 csn 512"),
+    (I32, "pin 4 ip 2 bi 16 wi 16 wd 32"),
+    (U16, "uoff 8 poff 16 jo 48 cl16 36 lab 64 roff 64 zoff 16 ll0 8 ll1 8 ll2 8 el0 16 el1 16 el2 16"),
+    (X4, "wq 512 uq 128 uq2 128 vq 128 e32q 512 luq 256 pmq 192 elq 176 gq 512 scq 512 mq 192 tpq 256 zq 256 xq0 256 "
+         "xq1 256 xq2 256 xq3 256 lq0 256 lq1 256 lq2 256"),
+    (U8, "wsq 512 us 128 us2 128 vs 128 e32s 512 lus 256 pms 192 els 176 gs 512 scs 512 ms 192 tps 256 zs 256 xs0 256 "
+         "xs1 256 xs2 256 xs3 256 ls0 256 ls1 256 ls2 256"),
 ]:
     _w = _l.split()
     for _i in range(0, len(_w), 2):
         _sb(_w[_i], int(_w[_i + 1]), _d)
-_share("cb", BF, [(n, 128) for n in ("jt", "key", "hm", "cpos", "id32", "rst", "kl", "ku")])
-_share("cw", F32, [("cf", 16), ("cc", 32), ("rs", 64)])
-_share("sm", F32, [("pay", 4), ("nb", 4), ("s2h", 4), ("h64", 4), ("base", 4), ("sf", 16), ("t1", 4), ("size", 4),
-                   ("ns", 4), ("nrem", 4)])
+_share("cb", BF, [("jf", 64), ("hf", 64), ("diag", 64), ("r16", 64), ("r32", 128), ("dc", 128), ("r64", 256), ("row", 16),
+                  ("dn", 128), ("base", 128), ("tmp", 128), ("one", 128), ("eq", 128), ("fp", 64), ("jv", 64)])
+_share("sm", BF, [("jm", 64), ("jn", 64), ("sel", 64), ("sg", 64), ("pp", 64), ("mh", 64), ("vm", 128), ("v1c", 128),
+                  ("thr", 128)])
+_share("cq", BF, [("p0f", 64), ("p1f", 64), ("pd", 64), ("pdm", 64), ("p0m", 128), ("p1m", 128), ("dm", 128)])
+_share("cw", F32, [("cf", 16), ("cc", 32)])
 for _t in range(8):
     SCRATCH["ps%d" % _t] = ("psum", [128, 512], F32)
 
-SEMAPHORES = (["qv", "qs", "qt", "qg", "dx", "du", "dp", "dw", "dv", "dout", "sent"]
+SEMAPHORES = (["qv", "qs", "qt", "qg", "dx0", "dx1", "du", "dp", "dw", "dv", "dout", "sent"]
               + ["aq%d" % t for t in range(3)] + ["al%d" % t for t in range(3)])
-WHOLE = 12582912.0
-CYC, WAKE, AHEAD = 0.00083, 0.2, 0.1
+CYC, WAKE, TURNS = 0.00104, 0.17, 3
+LEADS = [(0, a, b) for a in (0, 5) for b in (0, 6)]
+ONV = 3
+ZS = [[1, 1, 0, 0], [1, 1, 1, 0]]
+XA = [[0, 1, 0, 1], [0, 1, 0, 1]]
 
 
 def V(name, a=0, b=None, s=1, p=None):
@@ -84,9 +92,9 @@ def _n(v):
 
 def _time(o, a, k=1.0):
     if o[5] is not None:
-        return 0.05 + 3.5 * CYC * _n(a)
+        return 0.05 + 3.8 * CYC * _n(a)
     if a[5] is not None:
-        return 0.06 + 1.5 * CYC * _n(o)
+        return 0.06 + 1.56 * CYC * _n(o)
     if SCRATCH[o[0]][2] == BF and SCRATCH[a[0]][2] == BF:
         k *= 0.5
     return CYC * max(64, k * _n(o))
@@ -96,7 +104,7 @@ def rank_program(g, core, T, topo):
     rank = T.rank_of(core)
     if rank is None:
         return
-    ops = []
+    ops, side = [], [1]
 
     def ap(v, cast=None):
         if not isinstance(v, tuple):
@@ -114,7 +122,7 @@ def rank_program(g, core, T, topo):
         vs = [v for v in rd if isinstance(v, tuple)]
         r = [(v[0], _mask(v)) for v in vs] + [(v[5][0], _mask(v[5])) for v in vs + wr if v[5] is not None]
         ops.append({"e": eng, "fn": fn, "r": r, "w": [(v[0], _mask(v)) for v in wr], "sem": sem, "n": n, "acc": acc,
-                    "c": c, "late": late, "after": after})
+                    "c": c, "late": late, "after": after, "side": side[0]})
         return len(ops) - 1
 
     def tt(o, a, b, f):
@@ -139,7 +147,7 @@ def rank_program(g, core, T, topo):
         op("v", lambda q: q.tensor_tensor_scan(ap(o), ap(a), ap(b), 0.0, f0, f1), [a, b], [o], _time(o, a))
 
     def qz(oq, osc, a):
-        op("v", lambda q: q.quantize_mx(ap(oq), ap(osc), ap(a)), [a], [oq, osc], 0.012 + 0.00022 * _n(a))
+        op("v", lambda q: q.quantize_mx(ap(oq), ap(osc), ap(a)), [a], [oq, osc], 0.015 + 0.000275 * _n(a))
 
     def act(o, a, f=ACT.Copy, scale=1.0, bias=None):
         c = _time(o, a) if a[5] is not None else CYC * max(64, _n(o))
@@ -151,327 +159,432 @@ def rank_program(g, core, T, topo):
     def lin(o, a, scale, bias):
         act(o, a, ACT.Identity, scale, bias)
 
+    def fill(name, a, b, c):
+        for at in range(a, b, 256):
+            lin(V(name, at, min(b, at + 256)), V("iota", 0, min(256, b - at)), 0.0, c)
+
     def mm(o, wq, ws, xq, xs, start=True, stop=True):
         op("t", lambda q: q.matmul_mx(ap(o), ap(wq), ap(ws), ap(xq), ap(xs), start, stop), [wq, ws, xq, xs], [o],
-           0.0006 * (_n(o) + 16), acc=not start)
+           0.00063 * (_n(o) + 16), acc=not start)
 
     def iota(o, pattern, base, cm):
-        c = 0.13 + 2 * CYC * _n(o)
+        c = 0.16 + 2 * CYC * _n(o)
         if SCRATCH[o[0]][2] == I32:
             op("g", lambda q: q.iota(ap(o), pattern, base, cm), [], [o], c)
         else:
             op("g", lambda q: q.iota(ap(o), pattern, base, cm, allow_small_or_imprecise_dtypes=True), [], [o], c)
 
-    def select(o, pattern, f, fill, cm):
-        op("g", lambda q: q.affine_select(ap(o), ap(o), pattern, f, fill, 0, cm), [o], [o], 0.17 + 2 * CYC * _n(o))
+    def select(o, a, pattern, f, other, base, cm):
+        op("g", lambda q: q.affine_select(ap(o), ap(a), pattern, f, other, base, cm), [a], [o], 0.2 + 2 * CYC * _n(o))
 
-    def load(eng, o, src, sem, cast=None, late=2.2):
-        op(eng, lambda q: q.dma_start(ap(o, cast), src), [], [o], 0.1, sem=sem, n=16, late=late)
+    def load(eng, o, src, sem, cast=None, late=2.0):
+        op(eng, lambda q: q.dma_start(ap(o, cast), src), [], [o], 0.06, sem=sem, n=16, late=late)
 
     def store(eng, dst, a, cast=None):
-        op(eng, lambda q: q.dma_start(dst, ap(a, cast)), [a], [], 0.1, sem="dout", n=16, late=2.5)
+        op(eng, lambda q: q.dma_start(dst, ap(a, cast)), [a], [], 0.06, sem="dout", n=16, late=2.5)
 
     def send(to, o, a, rsem, cast=None):
         rid, pid = topo.addr(to, core)
         m = topo.mask(core, to)
         return op("g", lambda q: q.remote_dma(ap(o, cast), ap(a, cast), T.sem[rsem], T.sem["sent"], pid, rid, m), [a], [],
-                  0.5, sem="sent", n=len(topo.engines(core, to)), late=2.0 if cast is None else 4.0)
+                  0.5, sem="sent", n=len(topo.engines(core, to)), late=1.5 if cast is None else 4.0)
 
     def arrive(frm, views, rsem, sends):
         op("x", None, [], views, 0.0, sem=rsem, n=len(sends) * len(topo.engines(frm, core)), after=sends)
 
-    blk = lambda name, b: V(name, 32 * b, 32 * b + 32)
-    end = lambda name, b: col(name, 32 * b + 31)
     run = lambda name, i, n: V(name, n * i, n * i + n)
     bank = lambda b, n, a=0: V("ps%d" % b, a, n)
+    ends = lambda name, n=128, s=32: V(name, s - 1, n, s)
+    block = lambda gi: (gi >> 1) + 4 * (gi & 1)
+    TURN = ((0, 0, 32), (32, 48, 16), (48, 32, 16))
 
-    load("y", V("xt0"), T.x[:], "dx", late=3.3)
-    load("s", V("ut"), T.u[:], "du")
+    load("s", V("ut"), T.u[:], "du", late=2.4)
+    for k in range(2):
+        load("y", run("xt0", k, 512), T.x[:, 512 * k:512 * k + 512], "dx%d" % k, late=2.6 + 0.6 * k)
     for gi in range(8):
-        a1 = (gi >> 1) & 1
-        load("y", V("pin", 0, 8, 1, (16 * gi, 16 * gi + 16)), T.p0[:, 8 * a1:8 * a1 + 8], "dp")
-        load("s", V("pin", 8, 16, 1, (16 * gi, 16 * gi + 16)), T.p1[:, 8 * a1:8 * a1 + 8], "dp")
+        b = block(gi)
+        load("y", V("pin", 0, 2, 1, (16 * gi, 16 * gi + 16)), T.p0[:, 2 * b:2 * b + 2], "dp")
+        load("s", V("pin", 2, 4, 1, (16 * gi, 16 * gi + 16)), T.p1[:, 2 * b:2 * b + 2], "dp")
     load("y", V("wq"), T.wc[:], "dw", dt.uint8)
     load("y", V("wsq"), T.ws[:], "dw")
     load("y", V("vt"), T.v[:], "dv")
 
     iota(V("ip", 0, 1), [[0, 1]], 0, 1)
     iota(V("iota"), [[1, 256]], 0, 0)
-    iota(V("jt"), [[0, 4], [1, 32]], 0, 0)
-    iota(V("cpos"), [[0, 2], [32, 2], [0, 32]], 0, 0)
-    iota(V("key"), [[0, 2], [128, 2], [1, 32]], 0, 0)
-    iota(V("hm"), [[1, 2], [0, 64]], 0, 0)
+    iota(V("jf"), [[0, 2], [1, 32]], 0, 0)
+    iota(V("hf"), [[32, 2], [0, 32]], 0, 0)
+    iota(V("diag"), [[0, 4], [1, 16]], 0, 0)
+    iota(V("row", 0, 4), [[32, 2], [64, 2]], 0, 0)
     iota(V("gv"), [[-2, 34], [-2, 2]], 1, 0)
-    ms(V("uoff", 0, 4), 0)
-    ms(V("uoff", 4, 8), 64)
-    ms(V("jb"), 0.0)
-    FIELDS = [(0, 1), (1, 1), (4, 1), (5, 1), (6, 1), (0, 7), (0, 31), (0, 3), (2, 3), (0, 15)]
+    ms(V("uoff"), 0)
+    ms(V("uoff", 2, 4), 64)
+    FIELDS = [(0, 1), (1, 1), (4, 1), (0, 96), (0, 15), (2, 3), (1, 7), (2, 1), (3, 1), (0, 3)]
     for i, (sh, mk) in enumerate(FIELDS):
         ts(col("bi", i), V("ip", 0, 1), sh, ALU.logical_shift_right, mk, ALU.bitwise_and)
-    ms(V("mv"), 0.0)
     cp(V("cf", 0, 10), V("bi", 0, 10))
-    B0, B1, B4, B5, B6, K7, J31, R3, Q3, R15 = [col("cf", i) for i in range(10)]
+    B0, B1, PAR, BAND, P16, Q3, H7, B2, B3, R3 = [col("cf", i) for i in range(10)]
     cc = lambda i: col("cc", i)
-    lin(cc(0), B0, -160.0, 64.0)
-    lin(cc(1), B0, 5.0, R3)
-    lin(cc(4), B5, -128.0, 0.0)
-    lin(cc(10), B5, -128.0, -64.0)
-    lin(cc(5), B5, 128.0, J31)
-    lin(cc(2), cc(0), B4, 0.0)
-    for i, d in enumerate((-32.0, 0.0, 32.0)):
-        lin(cc(20 + i), cc(5), -1.0, -d - 0.5)
-        lin(cc(24 + i), cc(5), 1.0, d - 0.5)
-    lin(cc(6), cc(5), 1.0 / 2048, 64.0)
-    lin(cc(9), J31, -1.0 / 64, -255.5)
-    lin(cc(11), B6, 64.0, R15)
-    lin(cc(12), B4, 16.0, 0.0)
-    lin(cc(13), B0, 5.0, K7)
-    lin(cc(14), B0, -12.0, 26.0)
-    lin(cc(15), B0, 17.0, 31.0)
-    lin(cc(16), B4, 4.0, R3)
-    lin(cc(17), Q3, 8.0, cc(16))
-    lin(cc(18), cc(13), 16.0, cc(12))
-    lin(cc(19), cc(14), B1, cc(15))
-    lin(cc(3), B5, 32.0, cc(17))
-    ms(V("sw"), 0.0)
-    ms(V("rs"), 0.0)
-    ms(V("et", 4 * K, 512), 0.0)
-    ms(V("gt", 252, 256), 0.0)
-    ms(V("gt", 508, 512), 0.0)
-    qz(V("gq", 64, 192), V("gs", 64, 192), V("mv"))
-    qz(V("mq", 32, 160), V("ms", 32, 160), V("mv"))
-    ts(V("kl"), V("hm"), B6, ALU.not_equal, 500.0, ALU.mult)
-    for c0 in (0, 32, 49, 58):
-        ms(col("rs", c0), 1000.0)
-    tt(V("ku"), V("key"), V("kl"), ALU.add)
-    tt(V("kl"), V("key"), V("kl"), ALU.subtract)
+    B32, I1 = cc(0), cc(1)
+    lin(B32, PAR, 128.0, BAND)
+    lin(I1, P16, 1.0, 16.0)
+    lin(cc(2), B32, -1.0, 0.0)
+    lin(cc(3), B32, -1.0, 32.0)
+    lin(cc(4), PAR, 64.0, cc(2))
+    lin(cc(5), PAR, 64.0, cc(3))
+    for a, b, n in TURN:
+        act(V("fp", a, a + n), V("iota", b, b + n))
+        act(V("jv", a, a + n), V("jf", b, b + n))
+    for k in range(2):
+        cp(V("pf", 3 * k, 3 * k + 2), run("pin", k, 2))
+    cp(V("pf", 2, 6, 3), V("pin", 0, 4, 2))
+    for k in range(2):
+        for h in range(2):
+            a = V("pf", 3 * k + h, 3 * k + h + 2)
+            lin(V("pg", 4 * k + 2 * h, 4 * k + 2 * h + 2), a, 1.0, cc(4 + h))
+            lin(V("pg", 8 + 4 * k + 2 * h, 10 + 4 * k + 2 * h), a, 1.0, cc(2 + h))
+    cp(V("poff"), V("pg"))
+    for k in range(2):
+        act(V("p%df" % k), ind(V("fp"), V("poff", 8 + 4 * k, 12 + 4 * k)))
     qz(V("uq"), V("us"), V("ut"))
-    qz(V("vq"), V("vs"), V("vt"))
-    ts(V("id32"), V("jt"), J31, ALU.is_equal)
     cp(V("uq2"), ind(V("uq"), V("uoff")), dt.uint32)
     cp(V("us2"), ind(V("us"), V("uoff")))
-    cp(V("poff"), V("pin"))
-    for h in range(2):
-        lin(run("p1r", h, 64), ind(V("iota"), V("poff", 8 + 4 * h, 12 + 4 * h)), 1.0, cc(4 + 6 * h))
-        lin(run("p0r", h, 64), ind(V("iota"), V("poff", 4 * h, 4 + 4 * h)), 1.0, cc(4 + 6 * h))
-    tt(V("pd"), V("p0r"), V("p1r"), ALU.subtract)
-    ts(cc(7), J31, 0.0, ALU.is_equal, 1000.0, ALU.mult)
-    ts(V("cpos"), V("cpos"), J31, ALU.add)
-    ts(V("rst"), V("jt"), 0.0, ALU.not_equal)
-    ts(cc(8), cc(7), 0.3, ALU.add)
-    JT, ET, RX = V("cl16", 0, 1), V("cl16", 2, 3), V("cl16", 4, 5)
-    ts(JT, cc(1), 16.0, ALU.mult, cc(2), ALU.add)
-    ts(ET, cc(18), 191.0, ALU.min)
-    ts(RX, Q3, 64.0, ALU.mult, cc(19), ALU.add)
-    ts(V("exl"), V("iota", 0, 256, 64), cc(3), ALU.add)
-    for sl in range(4):
-        ts(V("pmt", sl, 512, 4), V("iota", 0, 128), -16.0 * sl, ALU.add, cc(11), ALU.is_equal)
-    qz(V("pmq"), V("pms"), V("pmt"))
-    for i in range(3):
-        act(run("pat", i, 128), V("kl"), ACT.Sign, 1.0, cc(20 + i))
-        act(run("pat", 3 + i, 128), V("ku"), ACT.Sign, -1.0, cc(24 + i))
-    select(V("pat", 128, 256), [[-1, 128]], ALU.not_equal, -513.0, 1)
-    for k, pair in enumerate([(1, 2), (2, 2), (0, 1), (0, 0)]):
-        for sl in range(4):
-            lin(V("lut", 512 * k + sl, 512 * k + 512, 4), run("pat", pair[sl & 1] + 3 * (sl >> 1), 128), 0.25, 0.25)
-        qz(run("luq", k, 128), run("lus", k, 128), run("lut", k, 512))
-    for b in range(4):
-        iota(run("e32t", b, 512), [[0, 512]], 32, 0)
-        op("g", lambda q, b=b: q.affine_select(ap(run("e32t", b, 512)), ap(run("e32t", b, 512)), [[-4, 128], [-1, 4]],
-                                               ALU.is_equal, 0.0, b, 4), [run("e32t", b, 512)], [run("e32t", b, 512)], 1.02)
-        qz(run("e32q", b, 128), run("e32s", b, 128), run("e32t", b, 512))
+    ts(V("r16"), V("diag"), 0.0, ALU.not_equal)
+    ts(V("diag"), V("diag"), P16, ALU.is_equal)
+    for pg, i in enumerate((P16, I1)):
+        ts(run("r32", pg, 64), V("jf"), 0.0, ALU.not_equal)
+        ts(run("dn", pg, 64), V("jv"), 0.0, ALU.not_equal, 128.0, ALU.mult)
+        lin(run("tmp", pg, 64), V("hf"), 1.0, i)
+        ts(run("eq", pg, 64), V("jf"), i, ALU.is_equal)
+        ts(run("base", pg, 64), V("jv"), i, ALU.is_equal, 64.0, ALU.mult)
+        for k in range(2):
+            act(run("p%dm" % k, pg, 64), ind(run("eq", pg, 64), V("poff", 8 + 4 * k, 12 + 4 * k)))
+        tt(run("dn", pg, 64), run("dn", pg, 64), V("fp"), ALU.add)
+    ms(V("dn", 48, 128, 64), 0.0)
+    tt(V("base"), V("base"), V("tmp"), ALU.add)
+    ms(V("dc"), -1.0)
+    for at, step in ((15, -1.125), (16, -0.875), (31, 15.0)):
+        ms(V("dc", at, 128, 32), step)
+    ms(V("r64"), 1.0)
+    ms(V("r64", 0, 256, 64), 0.0)
+    for k in range(2):
+        tt(V("p%dm" % k), V("p%dm" % k), V("dn"), ALU.mult)
+        tt(V("p%dm" % k), V("p%dm" % k), V("base"), ALU.max)
+    tt(V("dm"), V("p0m"), V("p1m"), ALU.subtract)
+    tt(V("pd"), V("p0f"), V("p1f"), ALU.subtract)
+    tt(V("pdm"), V("pd"), V("diag"), ALU.mult)
+    tt(V("xm", 1, 128, 2), V("p1f"), V("diag"), ALU.mult)
+    ts(cc(6), P16, 0.0, ALU.not_equal, 64.0, ALU.mult)
+    ms(V("v22"), 0.0)
+    ms(V("nn"), 0.0)
+    ms(V("vm"), 0.0)
+    for o in (V("va", 64), V("vb", 64), V("v5", 64), V("v1", 64), V("v22", 80, 144)):
+        act(o, V("base", 64))
+    ms(V("lb", 128, 130), 0.0)
+    ms(V("tb", 64, 128), 0.0)
+    act(V("cx", 0, 64), V("jf"))
+    act(V("cx", 64, 128), V("jf"))
+    RE, ET, EXL, L1 = V("cl16", 0, 1), V("cl16", 2, 3), V("cl16", 4, 6), V("cl16", 8, 16)
+    RX = [V("cl16", 16 + 2 * i, 17 + 2 * i) for i in range(NP)]
+    RY, R16, R32 = V("cl16", 24, 25), V("cl16", 26, 27), V("cl16", 28, 29)
+    lin(cc(7), B0, 64.0, 31.0)
+    ts(RE, B1, 32.0, ALU.mult, cc(7), ALU.add)
+    lin(cc(8), PAR, 16.0, 0.0)
+    lin(cc(22), P16, 1.0, cc(8))
+    SF = V("cl16", 32, 36)
+    ts(SF, V("row", 0, 4), 2.0, ALU.mult, cc(22), ALU.add)
+    lin(cc(9), B0, 96.0, cc(8))
+    lin(cc(10), H7, 32.0, cc(9))
+    ts(ET, cc(10), 191.0, ALU.min)
+    lin(cc(11), B32, 0.25, Q3)
+    lin(cc(12), B0, 64.0, cc(11))
+    lin(cc(13), B1, 4.0, cc(12))
+    ts(EXL, V("iota", 0, 256, 128), cc(13), ALU.add)
+    lin(cc(14), PAR, 144.0, P16)
+    lin(cc(15), PAR, -144.0, P16)
+    for pj in range(2):
+        for h in range(2):
+            o = V("cl16", 8 + 4 * pj + 2 * h, 10 + 4 * pj + 2 * h)
+            ts(o, run("row", h, 2), cc(14 + (pj ^ h)), ALU.add, 160.0 * (pj ^ h), ALU.add)
+    lin(cc(29), B0, -2.0, 1.0)
+    lin(cc(30), cc(29), B1, 0.0)
+    lin(cc(29), cc(30), B2, R3)
+    lin(cc(30), cc(29), 1.0, B3)
+    ts(cc(29), cc(30), 3.0, ALU.min)
+    ts(R16, cc(29), 16.0, ALU.mult, 15.0, ALU.add)
+    ts(R32, cc(29), 32.0, ALU.mult, 31.0, ALU.add)
+    first, last = {}, {}
+    fill("rs", 0, 128 * NP, 0.0)
+    fill("gt", 0, 512 * NP, 0.0)
+    for i, ls_ in enumerate(PASSES):
+        at = 0
+        for l in ls_:
+            first[l], last[l] = at, at + SEG[l][0]
+            ms(V("rs", 128 * i + at, 128 * i + 128, 64), 1000.0)
+            for h in range(2):
+                ms(col("rs", 128 * i + 64 * h + last[l]), h - 2.0)
+            at = last[l] + 1
 
-    SEG = [(0, 32, 1), (32, 17, 0), (49, 9, 0), (58, 5, 0)]
+    def by_quarter(o, vals):
+        ts(o, Q3, 0.0, ALU.mult, float(vals[0]), ALU.add)
+        for k in range(1, len(vals)):
+            ts(cc(31), Q3, float(k), ALU.is_ge, float(vals[k] - vals[k - 1]), ALU.mult)
+            tt(o, o, cc(31), ALU.add)
+
+    lin(cc(16), B1, 64.0, 0.0)
+    lin(cc(17), B0, 128.0, cc(16))
+    for i, ls_ in enumerate(PASSES):
+        by_quarter(cc(18 + i), [last[l] for l in ls_])
+        ts(RX[i], cc(18 + i), cc(17), ALU.add)
+    lin(cc(28), B0, 64.0, 0.0)
+    lin(cc(23), B1, 128.0, cc(28))
+    by_quarter(cc(24), [256 * i + last[l] - 1 for i, ls_ in enumerate(PASSES) for l in ls_])
+    ts(RY, cc(24), cc(23), ALU.add)
+    lin(cc(25), B32, 1.0, -16.0)
+    fill("e32t", 0, 516, 32.0)
+    select(V("e32t"), V("e32t"), [[-1, 516]], ALU.is_equal, 0.0, 3, 4)
+    for b in range(4):
+        qz(run("e32q", b, 128), run("e32s", b, 128), V("e32t", 3 - b, 515 - b))
+    qz(V("vq"), V("vs"), V("vt"))
+    ms(V("one"), 1.0)
+    for pg in range(2):
+        for par in range(2):
+            pat, o = [[32, 4], [128, 2], [1, 16]], 16 * pg - 128 * par
+            e = V("lut", 512 * pg + par, 512 * pg + 512, 4)
+            select(e, V("one"), pat, ALU.is_gt, 0.0, o, -1)
+            select(e, e, pat, ALU.not_equal, -256.0, o, -1)
+            select(V("lut", 512 * pg + par + 2, 512 * pg + 512, 4), V("one"), [[-s, n] for s, n in pat], ALU.is_gt, 0.0, -o, 1)
+        qz(run("luq", pg, 128), run("lus", pg, 128), run("lut", pg, 512))
+    fill("elt", 0, 704, 0.0)
+    lin(cc(27), B32, 1.0, 16.0)
+    for h in range(2):
+        for k in range(2):
+            e0 = 192 + 256 * h + 2 * h + k
+            lin(V("elt", e0, e0 + 61, 4), V("iota", 0, 16), 0.0, cc(27) if k else 1.0)
+    qz(V("elq"), V("els"), V("elt"))
+    fill("pmt", 0, 768, 0.0)
+    for sl in range(4):
+        ts(V("pmt", 256 + sl, 512, 4), V("iota", 0, 64), -16.0 * sl, ALU.add, P16, ALU.is_equal)
+    qz(V("pmq"), V("pms"), V("pmt"))
+    fill("mv", 0, 512, 0.0)
+    qz(V("mq", 64, 192), V("ms", 64, 192), V("mv"))
+    for l in range(4):
+        fill("sc%d" % l, 448, 512, 0.0)
 
     def decode(bank0, xq, xs, n, stop=True):
         for b in range(4):
             mm(bank(bank0 + b, n), run("e32q", b, 128), run("e32s", b, 128), xq, xs, True, stop)
 
-    def signs(l, b, w):
-        c0, n, v0 = SEG[l]
-        e0 = 4 * (64 * (b >> 1) + c0) + (b & 1)
-        act(V("gt", e0, e0 + 4 * n - 1, 2), V("gv", 2 * v0, 2 * (v0 + n)), ACT.Sign, 0.5, w)
+    W, D, A, A2 = V("tb", 128, 192), V("tb", 192, 256), V("tb", 256, 320), V("tb", 0, 64)
+    pg_ = lambda name, i: run(name, i, 64)
+    v22 = lambda i: V("v22", 16 + 64 * i, 80 + 64 * i)
 
-    def halves(dst, wq, ws, xq, xs):
+    def trees(t):
+        J = lambda i: run("jj", i - 1, 64)
+        O1, O3, O8 = [V("jo", 16 * i, 16 * i + 4) for i in range(3)]
+        part = lambda name, i, at=0: V(name, at + 80 * i, at + 64 + 48 * i)
+        plist = lambda o, i: V("jo", o[1] + 8 * i, o[1] + 4 + 6 * i)
+        act(V("sb0"), ind(V("ssb"), V("poff", 0, 4)))
+        tt(V("sel"), ind(V("ssb"), V("poff", 4, 8)), V("sb0"), ALU.is_le)
+        tt(V("xm", 0, 128, 2), V("sel"), V("pdm"), ALU.mult)
+        tt(V("jm"), V("sel"), V("pd"), ALU.mult)
+        for i in range(2):
+            tt(part("vm", i), V("sel", 16 * i, 64 - 16 * i), part("dm", i), ALU.mult)
+        scan(V("xn"), V("r32"), V("xm"), ALU.mult, ALU.add)
+        tt(J(1), V("jm"), V("p1f"), ALU.add)
+        tt(V("v1", 0, 112), V("vm", 0, 112), V("p1m", 0, 112), ALU.add)
+        cp(run("jo", 0, 16), ind(V("xn"), R32))
+        act(V("v1c", 0, 112), V("v1", 0, 112))
+
+        def far(o, j, off):
+            tt(V("jm"), ind(j, off), V("diag"), ALU.mult)
+            scan(V("jn"), V("r16"), V("jm"), ALU.mult, ALU.add)
+            cp(run("jo", o, 16), ind(V("jn"), R16))
+
+        act(J(2), ind(J(1), O1))
+        far(1, J(2), O1)
+        for i in (3, 4, 5):
+            act(J(i), ind(J(i - 1), O1))
+        far(2, J(5), O3)
+        if t == 2:
+            act(V("cx", 128, 192), ind(V("jv"), V("jo", 4, 8)))
+        for o, w, off, b in [("va", "v1", O1, "v1c"), ("vb", "va", O1, "v1"), ("va", "vb", O1, "v1"), ("v5", "va", O1, "v1"),
+                             ("vb", "v5", O3, "va"), ("va", "vb", O3, "v5"), ("vb", "va", O3, "v5")]:
+            for i in range(2):
+                tt(part(o, i), ind(pg_(w, i), plist(off, i)), part(b, i), ALU.max)
+        for i in range(2):
+            ts(part("thr", i), part("va", i), 64.0, ALU.is_lt, 64.0 if i else cc(6), ALU.mult)
+            tt(part("v22", i, 16), ind(pg_("vb", i), plist(O8, i)), part("va", i), ALU.max)
         for h in range(2):
-            mm(bank(4 + h, 128), wq, ws, run(xq, h, 128), run(xs, h, 128))
-        cp(V(dst, 0, 128), bank(4, 128))
-        act(V(dst, 128, 256), bank(5, 128))
-
-    def above(h):
-        H = lambda name: run(name, h, 64)
-        J = lambda i: V("jb", 192 * h + 96 * i + 16, 192 * h + 96 * i + 80)
-        jo = V("jo", 16 * h, 16 * h + 4)
-
-        def offsets(i):
-            tr(V("tj", 160 * h, 160 * h + 64), J(i))
-            tr(V("tj", 160 * h + 64, 160 * h + 160), run("jb", 2 * h + i, 96))
-            cp(run("jo", h, 16), ind(run("tj", h, 160), JT))
-
-        act(H("sb1"), ind(V("ssb"), V("poff", 8 + 4 * h, 12 + 4 * h)))
-        cp(H("sb0"), ind(V("ssb"), V("poff", 4 * h, 4 + 4 * h)))
-        tt(H("sel"), H("sb0"), H("sb1"), ALU.is_ge)
-        tt(H("jm"), H("sel"), H("pd"), ALU.mult)
-        tt(J(0), H("jm"), H("p1r"), ALU.add)
-        offsets(0)
-        tt(H("ab"), J(0), H("cpos"), ALU.is_equal)
-        tt(H("aa"), H("ab"), H("id32"), ALU.max)
-        for i in range(3):
-            act(J(1 - (i & 1)), ind(J(i & 1), jo))
-        tt(H("ab"), ind(H("aa"), jo), H("id32"), ALU.max)
-        tt(H("a4"), ind(H("ab"), jo), H("id32"), ALU.max)
-        tt(H("a4c"), ind(H("ab"), jo), H("id32"), ALU.max)
-        offsets(1)
-        for i in range(3):
-            act(J(i & 1), ind(J(1 - (i & 1)), jo))
-        tt(H("aa"), ind(H("a4"), jo), H("a4c"), ALU.max)
-        tt(H("ab"), ind(H("aa"), jo), H("a4"), ALU.max)
-        tt(H("aa"), ind(H("ab"), jo), H("a4"), ALU.max)
-        tt(H("a4c"), ind(H("ab"), jo), H("a4"), ALU.max)
-        offsets(0)
-        tt(H("a4"), ind(H("aa"), jo), H("a4c"), ALU.max)
-
-    def levels(h):
-        H = lambda name: run(name, h, 64)
-        S2 = lambda name: V(name, 64 * h + 31, 64 * h + 64, 32)
-        P2 = lambda name: run(name, h, 2)
-        mask = lambda l: H("rst") if l == 0 else run("d0t", 2 * l - 2 + h, 64)
-        bs = (2 * h, 2 * h + 1)
-        lin(H("act"), H("a4"), cc(9), 256.0)
-        scan(H("sz"), H("rst"), H("a4"), ALU.mult, ALU.add)
-        ts(H("ac"), H("a4"), -256.0, ALU.mult, 256.0, ALU.add)
-        tr(H("ai"), H("act"))
-        ts(S2("thr"), S2("sz"), 16.0, ALU.is_ge, 0.5, ALU.subtract)
-        lin(P2("pay"), S2("sz"), -1.0, cc(6))
-        for b in bs:
-            lin(blk("abo", b), blk("a4", b), 256.0, -256.0 + 32.0 * b / 2048)
-            signs(0, b, end("sz", b))
+            tt(V("nn", 64 * h, 64 * h + 32), ind(v22(0), V("jo", 32 + 2 * h, 34 + 2 * h)), run("thr", h, 32), ALU.is_ge)
+            tt(V("nn", 128 + 64 * h, 144 + 64 * h), ind(v22(1), col("jo", 40 - 6 * h)), run("thr", 5 + h, 16), ALU.is_ge)
+        scan(V("szs"), V("r64"), V("nn"), ALU.mult, ALU.add)
+        tr(V("st"), V("szs", 32, 256))
+        tr(V("lt", 0, 128), V("v22", 16, 144))
+        tr(V("lt", 128, 288), V("v22"))
+        act(V("lb", 0, 128), ind(V("lt"), L1))
+        tt(V("dl"), V("lb", 0, 128), V("lb", 1, 129), ALU.subtract)
+        cp(ends("dl"), ends("lb"))
+        ts(pg_("ny", 0), ind(V("st"), SF), 16.0, ALU.is_lt)
+        act(W, ind(V("st"), SF), ACT.Copy, 1.0 / 32)
+        lin(A, W, -1.0, 1.0)
+        lin(A2, W, -1.0, 1.0)
+        lin(D, W, 2.0, -1.0)
+        lin(pg_("uu", 0), W, 1.0, -0.5)
+        ts(V("sg"), W, 0.5, ALU.is_lt, 0.5, ALU.subtract)
         for l in range(4):
-            for b in bs:
-                ts(blk("mm", b), blk("ai", b), end("thr", b), ALU.is_le, col("pay", b), ALU.mult)
-            if l < 3:
-                ts(P2("h64"), S2("thr"), 0.0, ALU.is_gt, 64.0, ALU.mult)
-                tt(P2("base"), S2("sz") if l == 0 else P2("size"), P2("h64"), ALU.subtract)
-                ts(P2("nb"), P2("base"), -1.0, ALU.mult, cc(8), ALU.add)
-                for b in bs:
-                    lin(blk("abb", b), blk("abo", b), 1.0, col("base", b))
-            tr(H("mt"), H("mm"))
-            scan(H("red"), H("rst"), H("mt"), ALU.mult, ALU.max)
-            if l < 3:
-                sf = run("sf", 2 * l + h, 2)
-                for b in bs:
-                    lin(blk("xx", b), blk("abb", b), 1.0, end("red", b))
-                tt(sf, P2("base"), S2("red"), ALU.add)
-                for b in bs:
-                    ts(blk("d0", b), blk("ac", b), end("red", b), ALU.add, col("nb", b), ALU.is_gt)
-                ts(P2("s2h"), sf, 2.0, ALU.mult, 0.4, ALU.add)
-            for b in bs:
-                lin(blk("x2", b), blk("abo" if l == 0 else "ab2", b), 1.0, end("red", b))
-            tr(H("x2t"), H("x2"))
-            scan(H("cs"), mask(l), H("x2t"), ALU.mult, ALU.max)
-            ts(V("wi", 16 + 8 * h + l, 24 + 8 * h, 4), S2("cs"), 2048.0, ALU.mult)
+            i = [l in p for p in PASSES].index(True)
+            tr(run("wt", l, 64), W)
+            for h in range(2):
+                for par in range(2):
+                    e0, (n, v0) = 512 * i + 4 * (64 * h + first[l]) + par, SEG[l]
+                    act(V("gt", e0, e0 + 4 * n - 1, 2), V("gv", 2 * v0, 2 * (v0 + n)), ACT.Sign, 0.5 / 32,
+                        col("wt", 64 * l + 32 * h + 16 * par))
+            if l == 0:
+                for pg in range(2):
+                    scan(pg_("ls", pg), pg_("ny", 0), pg_("dl", pg), ALU.mult, ALU.add)
+                scan(pg_("csn", 0), pg_("ny", 0), pg_("dc", 0), ALU.mult, ALU.add)
+                act(pg_("csn", 1), pg_("csn", 0))
+            else:
+                if l < 3 or t == 2:
+                    scan(V("ls"), V("ny"), V("dl"), ALU.mult, ALU.add)
+                scan(run("csn", l, 128), V("ny"), V("dc"), ALU.mult, ALU.add)
+            if l < 3 or t == 2:
+                cp(run("lab", l, 16), ind(V("ls"), RE))
+            LB = V("lab", 16 * l, 16 * l + 4)
+            for h in range(2):
+                for pg in range(2):
+                    act(run("cv", 4 * l + 2 * h + pg, 16), V("diag", 0, 16), ACT.Copy,
+                        col("csn", 128 * l + 64 * pg * (l > 0) + 32 * h + 31))
+            if t == 2:
+                for h in range(2):
+                    act(run("crf", 4 * h + l, 32), ind(V("cx"), V("lab", 16 * l + 2 * h, 16 * l + 2 * h + 2)),
+                        ACT.Identity, 1.0, B32)
+            if l == PASSES[i][-1]:
+                places(i)
             if l == 3:
                 break
-            lin(P2("t1"), sf, 1.0, WHOLE)
-            lin(P2("size"), P2("t1"), 1.0, -WHOLE)
-            lin(P2("pay"), P2("size"), -1.0, cc(6))
-            act(P2("ns"), sf, ACT.Sign, 1.0, -0.3)
-            lin(P2("nrem"), P2("ns"), 32.0, -32.0)
-            for b in bs:
-                lin(blk("ab2", b), blk("abo", b), 1.0, col("nrem", b))
-                signs(l + 1, b, col("sf", 4 * l + b))
-            tr(H("xxt"), H("xx"))
-            tr(mask(l + 1), H("d0"))
-            for b in bs:
-                ts(blk("ee", b), blk("xxt", b), col("s2h", b), ALU.is_le, 63.0 / 64, ALU.subtract)
-            scan(H("thr"), mask(l + 1), H("ee"), ALU.mult, ALU.add)
+            u0, u1 = pg_("uu", l & 1), pg_("uu", 1 - (l & 1))
+            tt(V("pp"), ind(V("tb", 128, 320), LB), V("sg"), ALU.mult)
+            act(V("mh"), ind(V("tb", 0, 192), LB), ACT.Copy, 0.5)
+            for pg in range(2):
+                for h in range(2):
+                    o, me = run("ss", 2 * pg + h, 32), col("ls", 64 * pg + 32 * h + 31)
+                    a = ind(V("iota", 0, 192), V("lab", 16 * l + 2 * h, 16 * l + 2 * h + 2))
+                    if pg:
+                        act(o, a, ACT.Abs, -1.0, me)
+                    else:
+                        ts(o, a, me, ALU.not_equal)
+            tt(u1, u0, V("pp"), ALU.add)
+            for pg in range(2):
+                tt(pg_("ny", pg), u1, pg_("ss", pg), ALU.is_lt)
+            tt(W, V("mh"), u1, ALU.add)
+            if l < 2:
+                tt(A, V("mh"), u1, ALU.subtract)
+                act(A2, A)
+                lin(D, u1, 2.0, 0.0)
+                ts(V("sg"), u1, 0.0, ALU.is_lt, 0.5, ALU.subtract)
 
-    xt = "xt0"
+    def places(i):
+        qz(run("gq", i, 128), run("gs", i, 128), run("gt", i, 512))
+        n = 64 + last[PASSES[i][-1]] + 1
+        for pg in range(2):
+            mm(bank(4 + pg, 128), run("luq", pg, 128), run("lus", pg, 128), run("gq", i, 128), run("gs", i, 128))
+            at = 256 * i + 128 * pg
+            scan(V("rk", at, at + n), V("rs", 128 * i, 128 * i + n), bank(4 + pg, n), ALU.add, ALU.min)
+        ts(run("roff", i, 16), ind(run("rk", i, 256), RX[i]), 513.0, ALU.add, 2.0, ALU.mult)
+        for k, l in enumerate(PASSES[i]):
+            sc = "sc%d" % l
+            act(V(sc, 0, 448, 2), V("iota", 0, 224), ACT.Copy, 0.0)
+            cp(ind(V(sc, 64 * (l & 1), 64 * (l & 1) + 1024), V("roff", 16 * i + 4 * k, 16 * i + 4 * k + 4)), run("cv", l, 64))
+            if l < ONV:
+                act(V("ab"), V(sc, 0, 448, 2), ACT.Abs)
+                act(V(sc, 1, 448, 2), V("ab"), ACT.Sign)
+            else:
+                ts(V(sc, 1, 448, 2), V(sc, 0, 448, 2), 0.0, ALU.not_equal)
+            qz(run("scq", l, 128), run("scs", l, 128), V(sc, 0, 512))
+            mm(bank(7, 128), V("elq", 48 - 16 * l, 176 - 16 * l), V("els", 48 - 16 * l, 176 - 16 * l),
+               run("scq", l, 128), run("scs", l, 128), l == 0, l == 3)
+
+    xt, side[0] = "xt0", 0
     for t, m in enumerate(PARTNER):
         mate = T.cores[rank ^ m]
-        XQ, XS = V("xq%d" % t), V("xs%d" % t)
-        LQ, LS = V("lq%d" % t), V("ls%d" % t)
-        qz(XQ, XS, V(xt))
-        halves("ssb", V("uq2"), V("us2"), XQ[0], XS[0])
+        xq, xs = "xq%d" % t, "xs%d" % t
+        XQ, XS, LQ, LS = V(xq), V(xs), V("lq%d" % t), V("ls%d" % t)
+        for k in range(2):
+            qz(run(xq, k, 128), run(xs, k, 128), run(xt, k, 512))
+            mm(bank(k, 128), run(xq, k, 128), run(xs, k, 128), V("uq2"), V("us2"))
+            tr(run("ssb", k, 64), bank(k, 64))
         sends = [send(mate, LQ, XQ, "aq%d" % t, dt.uint8), send(mate, LS, XS, "aq%d" % t)]
+        side[0] = 2
         decode(0, XQ, XS, 256)
         for b in range(4):
             for h in range(2):
-                act(V("tw", PL * b + K + 128 * h, PL * b + K + 128 * h + 128), bank(b, 128 * h + 128, 128 * h), ACT.Copy, 2.0)
+                act(V("tw", PL * b + K + 128 * h, PL * b + K + 128 * h + 128), bank(b, 128 * h + 128, 128 * h), ACT.Copy, 1.0 / 32)
         arrive(mate, [LQ, LS], "aq%d" % t, sends)
         decode(0, LQ, LS, 256)
         for b in range(4):
             for h in range(2):
-                act(run("tp", 2 * b + h, 128), bank(b, 128 * h + 128, 128 * h), ACT.Copy, 1.0 / 32)
-        decode(0, XQ, XS, 256, False)
+                act(V("tp", 512 * h + b, 512 * h + 512, 4), bank(b, 128 * h + 128, 128 * h), ACT.Copy, 1.0 / 32)
         for h in range(2):
-            above(h)
-            levels(h)
-        qz(V("gq", 0, 128), V("gs", 0, 128), V("gt"))
+            qz(run("tpq", h, 128), run("tps", h, 128), run("tp", h, 512))
+        decode(0, V("tpq"), V("tps"), 256)
         for b in range(4):
-            for pr in range(2):
-                k = [[0, 1], [2, 1], [3, 0], [3, 2]][b][pr]
-                mm(bank(4 + b, 128), run("luq", k, 128), run("lus", k, 128),
-                   V("gq", 64 * pr, 64 * pr + 128), V("gs", 64 * pr, 64 * pr + 128), pr == 0, pr == 1)
-            scan(V("rk", 64 * b, 64 * b + 63), V("rs", 0, 63), bank(4 + b, 63), ALU.add, ALU.min)
-        ts(V("wi", 0, 16), ind(V("rk"), RX), 255.5, ALU.add)
-        ts(V("wd", 0, 32), V("wi"), 15, ALU.bitwise_and)
-        ts(V("wd", 32, 64), V("wi"), 240, ALU.bitwise_and)
-        cp(ind(V("mv", 0, 256), V("exl")), V("wd"))
-        qz(V("mq", 0, 128), V("ms", 0, 128), V("mv"))
-        mm(bank(4, 128), V("pmq"), V("pms"), V("mq", 0, 128), V("ms", 0, 128), True, False)
-        mm(bank(4, 128), V("pmq"), V("pms"), V("mq", 32, 160), V("ms", 32, 160), False, True)
-        cp(V("coff"), bank(4, 32, 16))
-        ts(V("roff"), bank(4, 16), cc(12), ALU.add)
-        cp(V("cr", 0, 128), ind(V("iota"), V("coff", 0, 8)))
-        act(V("cr", 128, 256), ind(V("iota"), V("coff", 8, 16)))
-        cp(ind(V("sw"), V("roff")), V("cr"))
-        tr(V("te", 0, 96), V("sw", 0, 96))
-        tr(V("te", 96, 192), V("sw", 16, 112))
+            for h in range(2):
+                act(run("tq", 2 * b + h, 128), bank(b, 128 * h + 128, 128 * h), ACT.Copy, 1.0 / 64)
+        decode(0, run(xq, 0, 128), run(xs, 0, 128), 128, False)
+        side[0] = 0
+        trees(t)
+        tr(V("te", 0, 96), bank(7, 96))
+        tr(V("te", 96, 192), bank(7, 112, 16))
         EL = "el%d" % t
         cp(V(EL), ind(V("te"), ET))
         sends = [send(mate, V("ll%d" % t, 0, 6), V(EL, 0, 6), "al%d" % t)]
         for b in range(4):
-            act(run("e32", b, K), ind(V("tw", PL * b + K, PL * b + PL), V(EL, 0, 6)), ACT.Copy, 0.5)
+            act(run("eh", b, K), ind(V("tw", PL * b + K, PL * b + PL), V(EL, 0, 6)), ACT.Copy, 0.5)
         z = lambda i: run("zf", i, 16)
-        cp(V("zf", 0, 32), bank(4, 32))
-        ts(z(2), z(1), float(K), ALU.add)
-        ts(z(3), z(0), float(K), ALU.is_lt)
-        tt(z(4), z(0), z(2), ALU.subtract)
-        tt(z(5), z(4), z(3), ALU.mult)
-        tt(z(4), z(5), z(2), ALU.add)
-        cp(V("zoff"), z(4))
+        ts(z(0), ind(V("rk", 0, 256 * NP), RY), 0.5, ALU.mult, 127.5, ALU.add)
+        lin(z(1), ends("csn", 512), 1.0, cc(25))
+        ts(z(2), z(0), -32.0, ALU.is_ge)
+        tt(z(3), z(1), z(0), ALU.subtract)
+        tt(z(4), z(3), z(2), ALU.mult)
+        tt(V("wi"), z(4), z(0), ALU.add)
+        ts(V("wd", 0, 16), V("wi"), 15, ALU.bitwise_and)
+        tt(V("wd", 16, 32), V("wi"), V("wd", 0, 16), ALU.subtract)
+        cp(ind(V("mv", 0, 256), EXL), V("wd"))
+        qz(V("mq", 0, 128), V("ms", 0, 128), V("mv"))
+        for q in range(4):
+            h = q & 1
+            mm(bank(6, 128), V("pmq", 64 - 64 * h, 192 - 64 * h), V("pms", 64 - 64 * h, 192 - 64 * h),
+               V("mq", 16 * q, 16 * q + 128), V("ms", 16 * q, 16 * q + 128), q == 0, q == 3)
+        ts(V("zoff"), bank(6, 16), 128.0, ALU.add)
+        decode(4, run(xq, 1, 128), run(xs, 1, 128), 128, False)
         if t == 2:
-            act(V("crf"), V("cr"))
             for gi in range(8):
-                store("y", T.cl[gi:gi + 1, :], V("crf", 0, 256, 1, (16 * gi, 16 * gi + 1)))
+                b = block(gi)
+                store("y", T.cl[:, 32 * b:32 * b + 32], V("crf", 0, 256, 1, (16 * gi, 16 * gi + 1)))
         LL = V("ll%d" % t, 0, 6)
         arrive(mate, [LL], "al%d" % t, sends)
         for b in range(4):
-            (cp if b < 2 else act)(V("et", b, 4 * K, 4), ind(run("tp", b, 256), LL))
-        qz(V("eq"), V("es"), V("et"))
-        decode(4, V("eq"), V("es"), 128)
-        for b in range(4):
-            tt(V("tw", PL * b, PL * b + K), bank(4 + b, K), run("e32", b, K), ALU.add)
-        for b in range(4):
-            w = ind(run("tw", b, PL), V("zoff"))
-            if b < 2:
-                act(V("ztile", b, 1024, 4), w, ACT.Copy, 1.0 / 64)
-            else:
-                ts(V("ztile", b, 1024, 4), w, 1.0 / 64, ALU.mult)
-        qz(V("zq"), V("zs"), V("ztile"))
-        for b in range(4):
-            mm(bank(b, 256), run("wq", b, 128), run("wsq", b, 128), V("zq"), V("zs"), False, True)
-        for b in range(4):
-            if b & 1:
-                act(V("xt1", b, 1024, 4), bank(b, 256), ACT.Copy, 1.0 / 32)
-            else:
-                ts(V("xt1", b, 1024, 4), bank(b, 256), 1.0 / 32, ALU.mult)
+            tt(V("tw", PL * b, PL * b + K), ind(run("tq", b, 256), LL), run("eh", b, K), ALU.add)
+        for k in range(2):
+            for b in range(4):
+                (act if ZS[k][b] else cp)(V("ztile", 512 * k + b, 512 * k + 512, 4), ind(run("tw", b, PL), run("zoff", k, 8)))
+            qz(run("zq", k, 128), run("zs", k, 128), run("ztile", k, 512))
+            for b in range(4):
+                mm(bank(4 * k + b, 128), run("wq", b, 128), run("wsq", b, 128), run("zq", k, 128), run("zs", k, 128), False, True)
+            for b in range(4):
+                o = V("xt1", 512 * k + b, 512 * k + 512, 4)
+                if XA[k][b]:
+                    act(o, bank(4 * k + b, 128), ACT.Copy, 1.0 / 32)
+                else:
+                    ts(o, bank(4 * k + b, 128), 1.0 / 32, ALU.mult)
         xt = "xt1"
 
-    qz(V("xq3"), V("xs3"), V(xt))
+    for k in range(2):
+        qz(run("xq3", k, 128), run("xs3", k, 128), run(xt, k, 512))
+        mm(bank(k, 128), V("vq"), V("vs"), run("xq3", k, 128), run("xs3", k, 128))
+        (cp if k else act)(run("ysb", k, 128), bank(k, 128))
     store("y", T.oc[:], V("xq3"), dt.uint8)
-    halves("ysb", V("vq"), V("vs"), "xq3", "xs3")
     store("s", T.y[:], V("ysb"))
     for k in range(4):
         store("y", T.osc[4 * k:4 * k + 4, :], V("xs3", 0, 256, 1, (32 * k, 32 * k + 4)))
@@ -479,9 +592,61 @@ def rank_program(g, core, T, topo):
     emit(g, T, ops)
 
 
+ORDER = {}
+
+
+def schedule(ops, deps, before):
+    n = len(ops)
+    if n in ORDER:
+        return ORDER[n]
+    lag = lambda j, i: (ops[j]["late"] + WAKE) if j in deps[i] or ops[i]["e"] == "x" or ops[j]["e"] != ops[i]["e"] else 0.0
+    pre = [[(j, lag(j, i)) for j in before[i]] for i in range(n)]
+    post = [[] for _ in range(n)]
+    for i in range(n):
+        for j, w in pre[i]:
+            post[j].append((i, w))
+    tail = [ops[i]["late"] if not post[i] else 0.0 for i in range(n)]
+
+    def place(key, ahead, behind, first):
+        left, can, at = [len(a) for a in ahead], list(first), [0.0] * n
+        ready, busy = [i for i in range(n) if not left[i]], {}
+        while ready:
+            i = min(ready, key=key)
+            ready.remove(i)
+            s, c, line = can[i], ops[i]["c"], busy.setdefault(ops[i]["e"], [])
+            k = 0
+            for k, (a, b) in enumerate(line + [(1e9, 1e9)]):
+                if s + c <= a + 1e-9:
+                    break
+                s = max(s, b)
+            line.insert(k, (s, s + c))
+            at[i] = s
+            for j, w in behind[i]:
+                can[j] = max(can[j], s + c + w)
+                left[j] -= 1
+                if not left[j]:
+                    ready.append(j)
+        return at
+
+    base = [0.0] * n
+    for i in range(n - 1, -1, -1):
+        base[i] = ops[i]["c"] + max([tail[i]] + [base[j] + w for j, w in post[i]])
+    best = None
+    for lead in LEADS:
+        way = [base[i] + lead[ops[i]["side"]] for i in range(n)]
+        for _ in range(TURNS):
+            at = place(lambda i: (-way[i], i), pre, post, [0.0] * n)
+            end = max(at[i] + ops[i]["c"] + tail[i] for i in range(n))
+            if best is None or end < best[0]:
+                best = (end, at)
+            back = place(lambda i: (-at[i] - ops[i]["c"], -i), post, pre, tail)
+            way = [back[i] + ops[i]["c"] for i in range(n)]
+    ORDER[n] = sorted(range(n), key=lambda i: (best[1][i], i))
+    return ORDER[n]
+
+
 def emit(g, T, ops):
     Q = {"v": g.vector, "s": g.scalar, "t": g.tensor, "g": g, "y": g.sync}
-    n = len(ops)
     hist, total, members = {}, {}, {}
     for i, o in enumerate(ops):
         if o["sem"] is not None:
@@ -514,28 +679,7 @@ def emit(g, T, ops):
             hist[name] = [h for h in hist.get(name, []) if h[1] & ~m] + [(i, m, True)]
         for name, m in o["r"]:
             hist.setdefault(name, []).append((i, m, False))
-    way, after, left = [0.0] * n, [[] for _ in range(n)], [len(b) for b in before]
-    lag = lambda j, i: (ops[j]["late"] + WAKE) if j in deps[i] or ops[i]["e"] == "x" or ops[j]["e"] != ops[i]["e"] else 0.0
-    for i in range(n - 1, -1, -1):
-        way[i] += ops[i]["c"] + (ops[i]["late"] if not after[i] else 0.0)
-        for j in before[i]:
-            after[j].append(i)
-            way[j] = max(way[j], way[i] + lag(j, i))
-    free, ready, can, order = {e: 0.0 for e in "vstgyx"}, [i for i in range(n) if not left[i]], [0.0] * n, []
-    while ready:
-        at = lambda i: max(can[i], free[ops[i]["e"]])
-        i0 = min(ready, key=at)
-        near = [i for i in ready if ops[i]["e"] == ops[i0]["e"] and at(i) <= at(i0) + min(ops[i0]["c"], AHEAD)]
-        i = max(near, key=lambda k: (way[k], -k))
-        ready.remove(i)
-        order.append(i)
-        done = at(i) + ops[i]["c"]
-        free[ops[i]["e"]] = done
-        for k in after[i]:
-            can[k] = max(can[k], done + lag(i, k))
-            left[k] -= 1
-            if not left[k]:
-                ready.append(k)
+    order = schedule(ops, deps, before)
     known, issued = {e: 0 for e in Q}, {e: 0 for e in Q}
     place = {i: k for k, i in enumerate(order)}
     snap, waits = {}, {}

@@ -28,10 +28,10 @@ def _share(name, d, parts):
 
 for _d, _l in [
     (BF, "xt0 1024 ut 512 vt 512 iota 256 gv 68 e32t 516 lut 1024 pmt 768 elt 704 xm 128 xn 128 jj 320 "
-         "v1 128 va 128 vb 128 v5 128 v22 160 nn 256 szs 256 st 224 lt 288 lb 130 dl 128 tb 320 uu 128 "
-         "ss 128 ny 128 ls 128 cx 192 cv 256 wt 256 gt 2048 ab 224 sc0 1088 sc1 1088 "
+         "v1 128 va 128 vb 128 v5 128 v22 160 nn 256 szs 256 st 224 lt 288 lb 130 dl 128 tb 320 w2 192 uu 128 "
+         "ss 128 ny 128 ls 128 cx 192 cv 256 wt 256 gt 1536 ab 224 zz 768 sc0 1088 sc1 1088 "
          "sc2 1088 sc3 1088 mv 512 tw %d tp 1024 tq 1024 eh 384 ztile 1024 xt1 1024" % (4 * PL)),
-    (F32, "ssb 128 sb0 64 rk 1024 rs 512 te 192 crf 256 zf 96 ysb 256 pf 6 pg 16 csn 512"),
+    (F32, "ssb 128 rk 1024 rs 512 te 192 crf 256 zf 96 ysb 256 csn 512"),
     (I32, "pin 4 ip 2 bi 16 wi 16 wd 32"),
     (U16, "uoff 8 poff 16 jo 48 cl16 36 lab 64 roff 64 zoff 16 ll0 8 ll1 8 ll2 8 el0 16 el1 16 el2 16"),
     (X4, "wq 512 uq 128 uq2 128 vq 128 e32q 512 luq 256 pmq 192 elq 176 gq 512 scq 512 mq 192 tpq 256 zq 256 xq0 256 "
@@ -42,20 +42,24 @@ for _d, _l in [
     _w = _l.split()
     for _i in range(0, len(_w), 2):
         _sb(_w[_i], int(_w[_i + 1]), _d)
-_share("cb", BF, [("jf", 64), ("hf", 64), ("diag", 64), ("r16", 64), ("r32", 128), ("dc", 128), ("r64", 256), ("row", 16),
-                  ("dn", 128), ("base", 128), ("tmp", 128), ("one", 128), ("eq", 128), ("fp", 64), ("jv", 64)])
+_share("cb", BF, [("jf", 64), ("hf", 64), ("diag", 64), ("r16", 64), ("dc", 128), ("r64", 256), ("row", 16),
+                  ("dn", 64), ("base", 128), ("tmp", 128), ("one", 128), ("eq", 128), ("fp", 64), ("jv", 64)])
 _share("sm", BF, [("jm", 64), ("jn", 64), ("sel", 64), ("sg", 64), ("pp", 64), ("mh", 64), ("vm", 128), ("v1c", 128),
-                  ("thr", 128)])
-_share("cq", BF, [("p0f", 64), ("p1f", 64), ("pd", 64), ("pdm", 64), ("p0m", 128), ("p1m", 128), ("dm", 128)])
-_share("cw", F32, [("cf", 16), ("cc", 32)])
+                  ("thr", 128), ("hn", 64), ("wy", 64)])
+_share("cq", BF, [("p0f", 64), ("p1f", 64), ("pd", 64), ("pdm", 128), ("p0m", 128), ("p1m", 128), ("dm", 128)])
+_share("cw", F32, [("cf", 16), ("cc", 32), ("off", 64)])
+_share("sf", F32, [("sb0", 64), ("sb1", 64)])
+_share("lw", F32, [("pf", 16), ("pg", 16)])
+_sb("lf", 36, F32)
 for _t in range(8):
     SCRATCH["ps%d" % _t] = ("psum", [128, 512], F32)
 
-SEMAPHORES = (["qv", "qs", "qt", "qg", "dx0", "dx1", "du", "dp", "dw", "dv", "dout", "sent"]
+SEMAPHORES = (["qv", "qs", "qt", "qg", "dx0", "dx1", "du", "dp", "dw", "dv", "dz", "dout", "sent"]
               + ["aq%d" % t for t in range(3)] + ["al%d" % t for t in range(3)])
-CYC, WAKE, TURNS = 0.00104, 0.17, 3
-LEADS = [(0, a, b) for a in (0, 5) for b in (0, 6)]
-ONV = 3
+CYC, WAKE, LATE, TURNS = 0.0009, 0.21, 6.0, 3
+LEADS = [(0, a, b, 0) for a in (0, 3, 6) for b in (0, 4, 8)]
+KEEP = (0, 0, 0, 40)
+ONV = 2
 ZS = [[1, 1, 0, 0], [1, 1, 1, 0]]
 XA = [[0, 1, 0, 1], [0, 1, 0, 1]]
 
@@ -147,7 +151,7 @@ def rank_program(g, core, T, topo):
         op("v", lambda q: q.tensor_tensor_scan(ap(o), ap(a), ap(b), 0.0, f0, f1), [a, b], [o], _time(o, a))
 
     def qz(oq, osc, a):
-        op("v", lambda q: q.quantize_mx(ap(oq), ap(osc), ap(a)), [a], [oq, osc], 0.015 + 0.000275 * _n(a))
+        op("v", lambda q: q.quantize_mx(ap(oq), ap(osc), ap(a)), [a], [oq, osc], CYC * (14 + 0.265 * _n(a)))
 
     def act(o, a, f=ACT.Copy, scale=1.0, bias=None):
         c = _time(o, a) if a[5] is not None else CYC * max(64, _n(o))
@@ -162,6 +166,10 @@ def rank_program(g, core, T, topo):
     def fill(name, a, b, c):
         for at in range(a, b, 256):
             lin(V(name, at, min(b, at + 256)), V("iota", 0, min(256, b - at)), 0.0, c)
+
+    def clear(o):
+        a = V("zz", 0, _n(o))
+        op("y", lambda q: q.dma_start(ap(o), ap(a)), [a], [o], 0.06, sem="dz", n=16, late=3.0)
 
     def mm(o, wq, ws, xq, xs, start=True, stop=True):
         op("t", lambda q: q.matmul_mx(ap(o), ap(wq), ap(ws), ap(xq), ap(xs), start, stop), [wq, ws, xq, xs], [o],
@@ -185,9 +193,9 @@ def rank_program(g, core, T, topo):
 
     def send(to, o, a, rsem, cast=None):
         rid, pid = topo.addr(to, core)
-        m = topo.mask(core, to)
+        m, calls = topo.mask(core, to), [x for x in ops if x["sem"] == "sent"]
         return op("g", lambda q: q.remote_dma(ap(o, cast), ap(a, cast), T.sem[rsem], T.sem["sent"], pid, rid, m), [a], [],
-                  0.5, sem="sent", n=len(topo.engines(core, to)), late=1.5 if cast is None else 4.0)
+                  0.5 if calls else 2.0, sem="sent", n=len(topo.engines(core, to)), late=1.5 if cast is None else LATE)
 
     def arrive(frm, views, rsem, sends):
         op("x", None, [], views, 0.0, sem=rsem, n=len(sends) * len(topo.engines(frm, core)), after=sends)
@@ -209,13 +217,17 @@ def rank_program(g, core, T, topo):
     load("y", V("wsq"), T.ws[:], "dw")
     load("y", V("vt"), T.v[:], "dv")
 
+    side[0] = 3
     iota(V("ip", 0, 1), [[0, 1]], 0, 1)
     iota(V("iota"), [[1, 256]], 0, 0)
     iota(V("jf"), [[0, 2], [1, 32]], 0, 0)
     iota(V("hf"), [[32, 2], [0, 32]], 0, 0)
     iota(V("diag"), [[0, 4], [1, 16]], 0, 0)
     iota(V("row", 0, 4), [[32, 2], [64, 2]], 0, 0)
+    iota(V("pf"), [[0, 4], [32, 2], [0, 2]], 0, 0)
     iota(V("gv"), [[-2, 34], [-2, 2]], 1, 0)
+    ms(V("zz"), 0.0)
+    side[0] = 1
     ms(V("uoff"), 0)
     ms(V("uoff", 2, 4), 64)
     FIELDS = [(0, 1), (1, 1), (4, 1), (0, 96), (0, 15), (2, 3), (1, 7), (2, 1), (3, 1), (0, 3)]
@@ -228,20 +240,17 @@ def rank_program(g, core, T, topo):
     lin(B32, PAR, 128.0, BAND)
     lin(I1, P16, 1.0, 16.0)
     lin(cc(2), B32, -1.0, 0.0)
-    lin(cc(3), B32, -1.0, 32.0)
     lin(cc(4), PAR, 64.0, cc(2))
-    lin(cc(5), PAR, 64.0, cc(3))
     for a, b, n in TURN:
         act(V("fp", a, a + n), V("iota", b, b + n))
         act(V("jv", a, a + n), V("jf", b, b + n))
-    for k in range(2):
-        cp(V("pf", 3 * k, 3 * k + 2), run("pin", k, 2))
-    cp(V("pf", 2, 6, 3), V("pin", 0, 4, 2))
-    for k in range(2):
-        for h in range(2):
-            a = V("pf", 3 * k + h, 3 * k + h + 2)
-            lin(V("pg", 4 * k + 2 * h, 4 * k + 2 * h + 2), a, 1.0, cc(4 + h))
-            lin(V("pg", 8 + 4 * k + 2 * h, 10 + 4 * k + 2 * h), a, 1.0, cc(2 + h))
+    lin(cc(29), B0, -2.0, 1.0)
+    lin(cc(30), cc(29), B1, 0.0)
+    lin(cc(3), cc(30), 1.0, B0)
+    ts(V("cl16", 30, 31), B2, 2.0, ALU.mult, cc(3), ALU.add)
+    lin(V("pf", 0, 8), V("pf", 0, 8), 1.0, cc(4))
+    lin(V("pf", 8, 16), V("pf", 8, 16), 1.0, cc(2))
+    tt(V("pg"), ind(V("pin"), V("cl16", 30, 31)), V("pf"), ALU.add)
     cp(V("poff"), V("pg"))
     for k in range(2):
         act(V("p%df" % k), ind(V("fp"), V("poff", 8 + 4 * k, 12 + 4 * k)))
@@ -251,15 +260,11 @@ def rank_program(g, core, T, topo):
     ts(V("r16"), V("diag"), 0.0, ALU.not_equal)
     ts(V("diag"), V("diag"), P16, ALU.is_equal)
     for pg, i in enumerate((P16, I1)):
-        ts(run("r32", pg, 64), V("jf"), 0.0, ALU.not_equal)
-        ts(run("dn", pg, 64), V("jv"), 0.0, ALU.not_equal, 128.0, ALU.mult)
         lin(run("tmp", pg, 64), V("hf"), 1.0, i)
         ts(run("eq", pg, 64), V("jf"), i, ALU.is_equal)
         ts(run("base", pg, 64), V("jv"), i, ALU.is_equal, 64.0, ALU.mult)
-        for k in range(2):
-            act(run("p%dm" % k, pg, 64), ind(run("eq", pg, 64), V("poff", 8 + 4 * k, 12 + 4 * k)))
-        tt(run("dn", pg, 64), run("dn", pg, 64), V("fp"), ALU.add)
-    ms(V("dn", 48, 128, 64), 0.0)
+    lin(V("dn"), V("fp"), 1.0, 128.0)
+    ms(V("dn", 0, 64, 48), 0.0)
     tt(V("base"), V("base"), V("tmp"), ALU.add)
     ms(V("dc"), -1.0)
     for at, step in ((15, -1.125), (16, -0.875), (31, 15.0)):
@@ -267,12 +272,15 @@ def rank_program(g, core, T, topo):
     ms(V("r64"), 1.0)
     ms(V("r64", 0, 256, 64), 0.0)
     for k in range(2):
-        tt(V("p%dm" % k), V("p%dm" % k), V("dn"), ALU.mult)
+        for pg in range(2):
+            tt(run("p%dm" % k, pg, 64), ind(run("eq", pg, 64), V("poff", 8 + 4 * k, 12 + 4 * k)), V("dn"), ALU.mult)
         tt(V("p%dm" % k), V("p%dm" % k), V("base"), ALU.max)
     tt(V("dm"), V("p0m"), V("p1m"), ALU.subtract)
     tt(V("pd"), V("p0f"), V("p1f"), ALU.subtract)
-    tt(V("pdm"), V("pd"), V("diag"), ALU.mult)
-    tt(V("xm", 1, 128, 2), V("p1f"), V("diag"), ALU.mult)
+    tt(V("pdm", 0, 128, 2), V("pd"), V("diag"), ALU.mult)
+    tt(V("pdm", 1, 128, 2), V("p1f"), V("diag"), ALU.mult)
+    lin(V("xm", 0, 128, 2), V("diag"), -1.0, 1.0)
+    lin(V("off"), V("diag"), -1e29, 1e29)
     ts(cc(6), P16, 0.0, ALU.not_equal, 64.0, ALU.mult)
     ms(V("v22"), 0.0)
     ms(V("nn"), 0.0)
@@ -281,64 +289,68 @@ def rank_program(g, core, T, topo):
         act(o, V("base", 64))
     ms(V("lb", 128, 130), 0.0)
     ms(V("tb", 64, 128), 0.0)
+    ms(V("w2", 128, 192), 0.0)
     act(V("cx", 0, 64), V("jf"))
     act(V("cx", 64, 128), V("jf"))
     RE, ET, EXL, L1 = V("cl16", 0, 1), V("cl16", 2, 3), V("cl16", 4, 6), V("cl16", 8, 16)
     RX = [V("cl16", 16 + 2 * i, 17 + 2 * i) for i in range(NP)]
-    RY, R16, R32 = V("cl16", 24, 25), V("cl16", 26, 27), V("cl16", 28, 29)
+    RY, R16, R32, SF = V("cl16", 24, 25), V("cl16", 26, 27), V("cl16", 28, 29), V("cl16", 32, 36)
+    F = lambda v: V("lf", v[1], v[2])
+    ms(V("lf"), 0.0)
     lin(cc(7), B0, 64.0, 31.0)
-    ts(RE, B1, 32.0, ALU.mult, cc(7), ALU.add)
+    lin(F(RE), B1, 32.0, cc(7))
     lin(cc(8), PAR, 16.0, 0.0)
     lin(cc(22), P16, 1.0, cc(8))
-    SF = V("cl16", 32, 36)
-    ts(SF, V("row", 0, 4), 2.0, ALU.mult, cc(22), ALU.add)
+    lin(F(SF), V("row", 0, 4), 2.0, cc(22))
     lin(cc(9), B0, 96.0, cc(8))
     lin(cc(10), H7, 32.0, cc(9))
-    ts(ET, cc(10), 191.0, ALU.min)
+    ts(F(ET), cc(10), 191.0, ALU.min)
     lin(cc(11), B32, 0.25, Q3)
     lin(cc(12), B0, 64.0, cc(11))
     lin(cc(13), B1, 4.0, cc(12))
-    ts(EXL, V("iota", 0, 256, 128), cc(13), ALU.add)
+    lin(F(EXL), V("iota", 0, 256, 128), 1.0, cc(13))
     lin(cc(14), PAR, 144.0, P16)
-    lin(cc(15), PAR, -144.0, P16)
+    lin(cc(21), PAR, -144.0, P16)
+    lin(cc(15), cc(21), 1.0, 160.0)
     for pj in range(2):
         for h in range(2):
             o = V("cl16", 8 + 4 * pj + 2 * h, 10 + 4 * pj + 2 * h)
-            ts(o, run("row", h, 2), cc(14 + (pj ^ h)), ALU.add, 160.0 * (pj ^ h), ALU.add)
-    lin(cc(29), B0, -2.0, 1.0)
-    lin(cc(30), cc(29), B1, 0.0)
-    lin(cc(29), cc(30), B2, R3)
-    lin(cc(30), cc(29), 1.0, B3)
-    ts(cc(29), cc(30), 3.0, ALU.min)
-    ts(R16, cc(29), 16.0, ALU.mult, 15.0, ALU.add)
-    ts(R32, cc(29), 32.0, ALU.mult, 31.0, ALU.add)
+            lin(F(o), run("row", h, 2), 1.0, cc(14 + (pj ^ h)))
+    lin(cc(5), cc(30), B2, R3)
+    lin(cc(26), cc(5), 1.0, B3)
+    ts(cc(24), cc(26), 3.0, ALU.min)
+    ts(R16, cc(24), 16.0, ALU.mult, 15.0, ALU.add)
+    ts(R32, cc(24), 32.0, ALU.mult, 31.0, ALU.add)
     first, last = {}, {}
     fill("rs", 0, 128 * NP, 0.0)
-    fill("gt", 0, 512 * NP, 0.0)
+    for o in ([run("gt", i, 768) for i in range(2)] + [V("elt"), V("pmt"), V("mv")]
+              + [V("sc%d" % l, 448, 512) for l in range(4)]):
+        clear(o)
     for i, ls_ in enumerate(PASSES):
         at = 0
         for l in ls_:
             first[l], last[l] = at, at + SEG[l][0]
-            ms(V("rs", 128 * i + at, 128 * i + 128, 64), 1000.0)
-            for h in range(2):
-                ms(col("rs", 128 * i + 64 * h + last[l]), h - 2.0)
+            lin(V("rs", 128 * i + at, 128 * i + 128, 64), V("iota", 0, 2), 0.0, 1000.0)
+            lin(V("rs", 128 * i + last[l], 128 * i + 128, 64), V("iota", 0, 2), 1.0, -2.0)
             at = last[l] + 1
 
-    def by_quarter(o, vals):
-        ts(o, Q3, 0.0, ALU.mult, float(vals[0]), ALU.add)
-        for k in range(1, len(vals)):
-            ts(cc(31), Q3, float(k), ALU.is_ge, float(vals[k] - vals[k - 1]), ALU.mult)
-            tt(o, o, cc(31), ALU.add)
+    def by_quarter(o, vals, a):
+        v = [float(x) for x in vals + vals[-1:] * 3]
+        lin(o, B2, v[1] - v[0], a)
+        lin(o, B3, v[2] - v[0], o)
+        lin(o, cc(31), v[3] - v[2] - v[1] + v[0], o)
+        lin(o, o, 1.0, v[0])
 
+    lin(cc(31), B2, B3, 0.0)
     lin(cc(16), B1, 64.0, 0.0)
     lin(cc(17), B0, 128.0, cc(16))
     for i, ls_ in enumerate(PASSES):
-        by_quarter(cc(18 + i), [last[l] for l in ls_])
-        ts(RX[i], cc(18 + i), cc(17), ALU.add)
+        by_quarter(F(RX[i]), [last[l] for l in ls_], cc(17))
     lin(cc(28), B0, 64.0, 0.0)
     lin(cc(23), B1, 128.0, cc(28))
-    by_quarter(cc(24), [256 * i + last[l] - 1 for i, ls_ in enumerate(PASSES) for l in ls_])
-    ts(RY, cc(24), cc(23), ALU.add)
+    by_quarter(F(RY), [256 * i + last[l] - 1 for i, ls_ in enumerate(PASSES) for l in ls_], cc(23))
+    cp(V("cl16", 0, 26), V("lf", 0, 26))
+    cp(SF, F(SF))
     lin(cc(25), B32, 1.0, -16.0)
     fill("e32t", 0, 516, 32.0)
     select(V("e32t"), V("e32t"), [[-1, 516]], ALU.is_equal, 0.0, 3, 4)
@@ -354,21 +366,16 @@ def rank_program(g, core, T, topo):
             select(e, e, pat, ALU.not_equal, -256.0, o, -1)
             select(V("lut", 512 * pg + par + 2, 512 * pg + 512, 4), V("one"), [[-s, n] for s, n in pat], ALU.is_gt, 0.0, -o, 1)
         qz(run("luq", pg, 128), run("lus", pg, 128), run("lut", pg, 512))
-    fill("elt", 0, 704, 0.0)
     lin(cc(27), B32, 1.0, 16.0)
     for h in range(2):
         for k in range(2):
             e0 = 192 + 256 * h + 2 * h + k
             lin(V("elt", e0, e0 + 61, 4), V("iota", 0, 16), 0.0, cc(27) if k else 1.0)
     qz(V("elq"), V("els"), V("elt"))
-    fill("pmt", 0, 768, 0.0)
     for sl in range(4):
-        ts(V("pmt", 256 + sl, 512, 4), V("iota", 0, 64), -16.0 * sl, ALU.add, P16, ALU.is_equal)
+        act(V("pmt", 256 + 65 * sl, 317 + 65 * sl, 4), V("diag", 0, 16))
     qz(V("pmq"), V("pms"), V("pmt"))
-    fill("mv", 0, 512, 0.0)
     qz(V("mq", 64, 192), V("ms", 64, 192), V("mv"))
-    for l in range(4):
-        fill("sc%d" % l, 448, 512, 0.0)
 
     def decode(bank0, xq, xs, n, stop=True):
         for b in range(4):
@@ -384,16 +391,17 @@ def rank_program(g, core, T, topo):
         part = lambda name, i, at=0: V(name, at + 80 * i, at + 64 + 48 * i)
         plist = lambda o, i: V("jo", o[1] + 8 * i, o[1] + 4 + 6 * i)
         act(V("sb0"), ind(V("ssb"), V("poff", 0, 4)))
+        tt(V("sb1"), ind(V("ssb"), V("poff", 0, 4)), V("off"), ALU.add)
+        tt(V("xm", 1, 128, 2), ind(V("ssb"), V("poff", 4, 8)), V("sb1"), ALU.is_le)
         tt(V("sel"), ind(V("ssb"), V("poff", 4, 8)), V("sb0"), ALU.is_le)
-        tt(V("xm", 0, 128, 2), V("sel"), V("pdm"), ALU.mult)
         tt(V("jm"), V("sel"), V("pd"), ALU.mult)
         for i in range(2):
             tt(part("vm", i), V("sel", 16 * i, 64 - 16 * i), part("dm", i), ALU.mult)
-        scan(V("xn"), V("r32"), V("xm"), ALU.mult, ALU.add)
+        scan(V("xn"), V("xm"), V("pdm"), ALU.mult, ALU.add)
         tt(J(1), V("jm"), V("p1f"), ALU.add)
         tt(V("v1", 0, 112), V("vm", 0, 112), V("p1m", 0, 112), ALU.add)
         cp(run("jo", 0, 16), ind(V("xn"), R32))
-        act(V("v1c", 0, 112), V("v1", 0, 112))
+        tt(V("v1c", 0, 112), V("vm", 0, 112), V("p1m", 0, 112), ALU.add)
 
         def far(o, j, off):
             tt(V("jm"), ind(j, off), V("diag"), ALU.mult)
@@ -465,7 +473,10 @@ def rank_program(g, core, T, topo):
                 break
             u0, u1 = pg_("uu", l & 1), pg_("uu", 1 - (l & 1))
             tt(V("pp"), ind(V("tb", 128, 320), LB), V("sg"), ALU.mult)
-            act(V("mh"), ind(V("tb", 0, 192), LB), ACT.Copy, 0.5)
+            if l < 2:
+                act(V("mh"), ind(V("tb", 0, 192), LB), ACT.Copy, 0.5)
+            else:
+                tt(V("wy"), ind(V("w2"), LB), V("hn"), ALU.mult)
             for pg in range(2):
                 for h in range(2):
                     o, me = run("ss", 2 * pg + h, 32), col("ls", 64 * pg + 32 * h + 31)
@@ -477,12 +488,18 @@ def rank_program(g, core, T, topo):
             tt(u1, u0, V("pp"), ALU.add)
             for pg in range(2):
                 tt(pg_("ny", pg), u1, pg_("ss", pg), ALU.is_lt)
-            tt(W, V("mh"), u1, ALU.add)
             if l < 2:
+                tt(W, V("mh"), u1, ALU.add)
                 tt(A, V("mh"), u1, ALU.subtract)
                 act(A2, A)
                 lin(D, u1, 2.0, 0.0)
                 ts(V("sg"), u1, 0.0, ALU.is_lt, 0.5, ALU.subtract)
+            else:
+                tt(W, W, V("wy"), ALU.add)
+            if l == 1:
+                for k in range(2):
+                    act(run("w2", k, 64), W)
+                ts(V("hn"), u1, 0.0, ALU.is_lt, 1.0, ALU.subtract)
 
     def places(i):
         qz(run("gq", i, 128), run("gs", i, 128), run("gt", i, 512))
@@ -584,8 +601,8 @@ def rank_program(g, core, T, topo):
         qz(run("xq3", k, 128), run("xs3", k, 128), run(xt, k, 512))
         mm(bank(k, 128), V("vq"), V("vs"), run("xq3", k, 128), run("xs3", k, 128))
         (cp if k else act)(run("ysb", k, 128), bank(k, 128))
-    store("y", T.oc[:], V("xq3"), dt.uint8)
-    store("s", T.y[:], V("ysb"))
+        store("y", T.oc[:, 512 * k:512 * k + 512], run("xq3", k, 128), dt.uint8)
+        store("s", T.y[:, 128 * k:128 * k + 128], run("ysb", k, 128))
     for k in range(4):
         store("y", T.osc[4 * k:4 * k + 4, :], V("xs3", 0, 256, 1, (32 * k, 32 * k + 4)))
 
@@ -628,20 +645,31 @@ def schedule(ops, deps, before):
                     ready.append(j)
         return at
 
+    def replay(order, k):
+        free, done = {}, [0.0] * n
+        for i in order:
+            e = ops[i]["e"]
+            s = max([free.get(e, 0.0)] + [done[j] + w for j, w in pre[i]])
+            free[e] = done[i] = s + ops[i]["c"] * (k if e in "vst" else 1.0)
+        return max(done[i] + tail[i] for i in range(n))
+
     base = [0.0] * n
     for i in range(n - 1, -1, -1):
         base[i] = ops[i]["c"] + max([tail[i]] + [base[j] + w for j, w in post[i]])
     best = None
     for lead in LEADS:
-        way = [base[i] + lead[ops[i]["side"]] for i in range(n)]
+        way = [base[i] + lead[ops[i]["side"]] + KEEP[ops[i]["side"]] for i in range(n)]
         for _ in range(TURNS):
+            for i in range(n - 1, -1, -1):
+                way[i] = max([way[i]] + [way[j] + w + ops[i]["c"] for j, w in post[i]])
             at = place(lambda i: (-way[i], i), pre, post, [0.0] * n)
-            end = max(at[i] + ops[i]["c"] + tail[i] for i in range(n))
+            order = sorted(range(n), key=lambda i: (at[i], i))
+            end = sum(replay(order, k) for k in (0.92, 1.15, 1.4))
             if best is None or end < best[0]:
-                best = (end, at)
+                best = (end, order)
             back = place(lambda i: (-at[i] - ops[i]["c"], -i), post, pre, tail)
-            way = [back[i] + ops[i]["c"] for i in range(n)]
-    ORDER[n] = sorted(range(n), key=lambda i: (best[1][i], i))
+            way = [back[i] + ops[i]["c"] + KEEP[ops[i]["side"]] for i in range(n)]
+    ORDER[n] = best[1]
     return ORDER[n]
 
 

from concourse.mybir import dt, AluOpType, ActivationFunctionType

ALU = AluOpType
ACT = ActivationFunctionType
C, K = 256, 96
PARTNER = [1, 2, 4]
PL = K + C
PASSES = [[0], [1, 2], [3]]
SEG = [(32, 1), (17, 0), (9, 0), (5, 0)]
NP = len(PASSES)
F32, BF, I32, U16, X4, U8 = "float32", "bfloat16", "int32", "uint16", "float8_e4m3fn_x4", "uint8"

SCRATCH = {}
PART = {}


def _sb(name, n, d):
    SCRATCH[name] = ("sbuf", [128, n], d)


def _share(name, d, parts):
    at = 0
    for nm, w in parts:
        PART[nm] = (name, at, w)
        at += w
    _sb(name, at, d)


for _d, _l in [
    (BF, "xt0 1024 ut 512 vt 512 iota 256 gv 68 e32t 516 lut 1024 pmt 768 elt 704 xm 128 xn 128 jj 320 "
         "v1 128 va 128 vb 128 v5 128 v22 160 nn 256 szs 256 st 224 lt 288 lb 130 dl 128 tb 320 w2 192 uu 128 "
         "ss 128 ny 128 ls 128 cx 192 cv 256 wt 256 gt 1536 ab 224 zz 768 sc0 1088 sc1 1088 "
         "sc2 1088 sc3 1088 mv 512 tw %d tp 1024 tq 1024 eh 384 ztile 1024 xt1 1024" % (4 * PL)),
    (F32, "ssb 128 rk 1024 rs 512 te 192 crf 256 zf 96 ysb 256 csn 512"),
    (I32, "pin 4 ip 2 bi 16 wi 16 wd 32"),
    (U16, "uoff 8 poff 16 jo 48 cl16 36 lab 64 roff 64 zoff 16 ll0 8 ll1 8 ll2 8 el0 16 el1 16 el2 16"),
    (X4, "wq 512 uq 128 uq2 128 vq 128 e32q 512 luq 256 pmq 192 elq 176 gq 512 scq 512 mq 192 tpq 256 zq 256 xq0 256 "
         "xq1 256 xq2 256 xq3 256 lq0 256 lq1 256 lq2 256"),
    (U8, "wsq 512 us 128 us2 128 vs 128 e32s 512 lus 256 pms 192 els 176 gs 512 scs 512 ms 192 tps 256 zs 256 xs0 256 "
         "xs1 256 xs2 256 xs3 256 ls0 256 ls1 256 ls2 256"),
]:
    _w = _l.split()
    for _i in range(0, len(_w), 2):
        _sb(_w[_i], int(_w[_i + 1]), _d)
_share("cb", BF, [("jf", 64), ("hf", 64), ("diag", 64), ("r16", 64), ("dc", 128), ("r64", 256), ("row", 16),
                  ("dn", 64), ("base", 128), ("tmp", 128), ("one", 128), ("eq", 128), ("fp", 64), ("jv", 64)])
_share("sm", BF, [("jm", 64), ("jn", 64), ("sel", 64), ("sg", 64), ("pp", 64), ("mh", 64), ("vm", 128), ("v1c", 128),
                  ("thr", 128), ("hn", 64), ("wy", 64)])
_share("cq", BF, [("p0f", 64), ("p1f", 64), ("pd", 64), ("pdm", 128), ("p0m", 128), ("p1m", 128), ("dm", 128)])
_share("cw", F32, [("cf", 16), ("cc", 32), ("off", 64)])
_share("sf", F32, [("sb0", 64), ("sb1", 64)])
_share("lw", F32, [("pf", 16), ("pg", 16)])
_sb("lf", 36, F32)
for _t in range(8):
    SCRATCH["ps%d" % _t] = ("psum", [128, 512], F32)

SEMAPHORES = (["qv", "qs", "qt", "qg", "dx0", "dx1", "du", "dp", "dw", "dv", "dz", "dout", "sent"]
              + ["aq%d" % t for t in range(3)] + ["al%d" % t for t in range(3)])
CYC, WAKE, LATE, TURNS = 0.0009, 0.21, 6.0, 3
LEADS = [(0, a, b, 0) for a in (0, 3, 6) for b in (0, 4, 8)]
KEEP = (0, 0, 0, 40)
ONV = 2
ZS = [[1, 1, 0, 0], [1, 1, 1, 0]]
XA = [[0, 1, 0, 1], [0, 1, 0, 1]]


def V(name, a=0, b=None, s=1, p=None):
    if name in PART:
        buf, at, w = PART[name]
        return (buf, at + a, at + (w if b is None else b), s, p, None)
    if b is None:
        b = SCRATCH[name][1][1]
    return (name, a, b, s, p, None)


def col(name, a):
    return V(name, a, a + 1)


def ind(win, off):
    return win[:5] + (off,)


def _mask(v):
    if v[0].startswith("ps"):
        return 1
    m = 0
    for c in range(v[1], v[2], v[3]):
        m |= 1 << c
    return m


def _n(v):
    return len(range(v[1], v[2], v[3]))


def _time(o, a, k=1.0):
    if o[5] is not None:
        return 0.05 + 3.8 * CYC * _n(a)
    if a[5] is not None:
        return 0.06 + 1.56 * CYC * _n(o)
    if SCRATCH[o[0]][2] == BF and SCRATCH[a[0]][2] == BF:
        k *= 0.5
    return CYC * max(64, k * _n(o))


def rank_program(g, core, T, topo):
    rank = T.rank_of(core)
    if rank is None:
        return
    ops, side = [], [1]

    def ap(v, cast=None):
        if not isinstance(v, tuple):
            return v
        name, a, b, s, p, off = v
        ps = slice(None) if p is None else slice(p[0], p[1])
        x = T[name][ps, a:b] if s == 1 else T[name][ps, a:b:s]
        if cast is not None:
            x = x.bitcast(cast)
        if off is not None:
            x = x.indirect(ap(off))
        return x

    def op(eng, fn, rd, wr, c, sem=None, n=0, acc=False, late=0.0, after=None):
        vs = [v for v in rd if isinstance(v, tuple)]
        r = [(v[0], _mask(v)) for v in vs] + [(v[5][0], _mask(v[5])) for v in vs + wr if v[5] is not None]
        ops.append({"e": eng, "fn": fn, "r": r, "w": [(v[0], _mask(v)) for v in wr], "sem": sem, "n": n, "acc": acc,
                    "c": c, "late": late, "after": after, "side": side[0]})
        return len(ops) - 1

    def tt(o, a, b, f):
        op("v", lambda q: q.tensor_tensor(ap(o), ap(a), ap(b), f), [a, b], [o], _time(o, a, 2.0))

    def ts(o, a, s1, f0, s2=None, f1=None):
        if f1 is None:
            op("v", lambda q: q.tensor_scalar(ap(o), ap(a), ap(s1), None, f0), [a, s1], [o], _time(o, a))
        else:
            op("v", lambda q: q.tensor_scalar(ap(o), ap(a), ap(s1), ap(s2), f0, f1), [a, s1, s2], [o], _time(o, a))

    def cp(o, a, cast=None):
        op("v", lambda q: q.tensor_copy(ap(o, cast), ap(a, cast)), [a], [o], _time(o, a))

    def ms(o, c):
        op("v", lambda q: q.memset(ap(o), c), [], [o], _time(o, o))

    def tr(o, a):
        op("v", lambda q: q.transpose(ap(o), ap(a)), [a], [o], _time(o, a))

    def scan(o, a, b, f0, f1):
        op("v", lambda q: q.tensor_tensor_scan(ap(o), ap(a), ap(b), 0.0, f0, f1), [a, b], [o], _time(o, a))

    def qz(oq, osc, a):
        op("v", lambda q: q.quantize_mx(ap(oq), ap(osc), ap(a)), [a], [oq, osc], CYC * (14 + 0.265 * _n(a)))

    def act(o, a, f=ACT.Copy, scale=1.0, bias=None):
        c = _time(o, a) if a[5] is not None else CYC * max(64, _n(o))
        if bias is None:
            op("s", lambda q: q.activation(ap(o), ap(a), f, scale=ap(scale)), [a, scale], [o], c)
        else:
            op("s", lambda q: q.activation(ap(o), ap(a), f, bias=ap(bias), scale=ap(scale)), [a, scale, bias], [o], c)

    def lin(o, a, scale, bias):
        act(o, a, ACT.Identity, scale, bias)

    def fill(name, a, b, c):
        for at in range(a, b, 256):
            lin(V(name, at, min(b, at + 256)), V("iota", 0, min(256, b - at)), 0.0, c)

    def clear(o):
        a = V("zz", 0, _n(o))
        op("y", lambda q: q.dma_start(ap(o), ap(a)), [a], [o], 0.06, sem="dz", n=16, late=3.0)

    def mm(o, wq, ws, xq, xs, start=True, stop=True):
        op("t", lambda q: q.matmul_mx(ap(o), ap(wq), ap(ws), ap(xq), ap(xs), start, stop), [wq, ws, xq, xs], [o],
           0.00063 * (_n(o) + 16), acc=not start)

    def iota(o, pattern, base, cm):
        c = 0.16 + 2 * CYC * _n(o)
        if SCRATCH[o[0]][2] == I32:
            op("g", lambda q: q.iota(ap(o), pattern, base, cm), [], [o], c)
        else:
            op("g", lambda q: q.iota(ap(o), pattern, base, cm, allow_small_or_imprecise_dtypes=True), [], [o], c)

    def select(o, a, pattern, f, other, base, cm):
        op("g", lambda q: q.affine_select(ap(o), ap(a), pattern, f, other, base, cm), [a], [o], 0.2 + 2 * CYC * _n(o))

    def load(eng, o, src, sem, cast=None, late=2.0):
        op(eng, lambda q: q.dma_start(ap(o, cast), src), [], [o], 0.06, sem=sem, n=16, late=late)

    def store(eng, dst, a, cast=None):
        op(eng, lambda q: q.dma_start(dst, ap(a, cast)), [a], [], 0.06, sem="dout", n=16, late=2.5)

    def send(to, o, a, rsem, cast=None):
        rid, pid = topo.addr(to, core)
        m, calls = topo.mask(core, to), [x for x in ops if x["sem"] == "sent"]
        return op("g", lambda q: q.remote_dma(ap(o, cast), ap(a, cast), T.sem[rsem], T.sem["sent"], pid, rid, m), [a], [],
                  0.5 if calls else 2.0, sem="sent", n=len(topo.engines(core, to)), late=1.5 if cast is None else LATE)

    def arrive(frm, views, rsem, sends):
        op("x", None, [], views, 0.0, sem=rsem, n=len(sends) * len(topo.engines(frm, core)), after=sends)

    run = lambda name, i, n: V(name, n * i, n * i + n)
    bank = lambda b, n, a=0: V("ps%d" % b, a, n)
    ends = lambda name, n=128, s=32: V(name, s - 1, n, s)
    block = lambda gi: (gi >> 1) + 4 * (gi & 1)
    TURN = ((0, 0, 32), (32, 48, 16), (48, 32, 16))

    load("s", V("ut"), T.u[:], "du", late=2.4)
    for k in range(2):
        load("y", run("xt0", k, 512), T.x[:, 512 * k:512 * k + 512], "dx%d" % k, late=2.6 + 0.6 * k)
    for gi in range(8):
        b = block(gi)
        load("y", V("pin", 0, 2, 1, (16 * gi, 16 * gi + 16)), T.p0[:, 2 * b:2 * b + 2], "dp")
        load("s", V("pin", 2, 4, 1, (16 * gi, 16 * gi + 16)), T.p1[:, 2 * b:2 * b + 2], "dp")
    load("y", V("wq"), T.wc[:], "dw", dt.uint8)
    load("y", V("wsq"), T.ws[:], "dw")
    load("y", V("vt"), T.v[:], "dv")

    side[0] = 3
    iota(V("ip", 0, 1), [[0, 1]], 0, 1)
    iota(V("iota"), [[1, 256]], 0, 0)
    iota(V("jf"), [[0, 2], [1, 32]], 0, 0)
    iota(V("hf"), [[32, 2], [0, 32]], 0, 0)
    iota(V("diag"), [[0, 4], [1, 16]], 0, 0)
    iota(V("row", 0, 4), [[32, 2], [64, 2]], 0, 0)
    iota(V("pf"), [[0, 4], [32, 2], [0, 2]], 0, 0)
    iota(V("gv"), [[-2, 34], [-2, 2]], 1, 0)
    ms(V("zz"), 0.0)
    side[0] = 1
    ms(V("uoff"), 0)
    ms(V("uoff", 2, 4), 64)
    FIELDS = [(0, 1), (1, 1), (4, 1), (0, 96), (0, 15), (2, 3), (1, 7), (2, 1), (3, 1), (0, 3)]
    for i, (sh, mk) in enumerate(FIELDS):
        ts(col("bi", i), V("ip", 0, 1), sh, ALU.logical_shift_right, mk, ALU.bitwise_and)
    cp(V("cf", 0, 10), V("bi", 0, 10))
    B0, B1, PAR, BAND, P16, Q3, H7, B2, B3, R3 = [col("cf", i) for i in range(10)]
    cc = lambda i: col("cc", i)
    B32, I1 = cc(0), cc(1)
    lin(B32, PAR, 128.0, BAND)
    lin(I1, P16, 1.0, 16.0)
    lin(cc(2), B32, -1.0, 0.0)
    lin(cc(4), PAR, 64.0, cc(2))
    for a, b, n in TURN:
        act(V("fp", a, a + n), V("iota", b, b + n))
        act(V("jv", a, a + n), V("jf", b, b + n))
    lin(cc(29), B0, -2.0, 1.0)
    lin(cc(30), cc(29), B1, 0.0)
    lin(cc(3), cc(30), 1.0, B0)
    ts(V("cl16", 30, 31), B2, 2.0, ALU.mult, cc(3), ALU.add)
    lin(V("pf", 0, 8), V("pf", 0, 8), 1.0, cc(4))
    lin(V("pf", 8, 16), V("pf", 8, 16), 1.0, cc(2))
    tt(V("pg"), ind(V("pin"), V("cl16", 30, 31)), V("pf"), ALU.add)
    cp(V("poff"), V("pg"))
    for k in range(2):
        act(V("p%df" % k), ind(V("fp"), V("poff", 8 + 4 * k, 12 + 4 * k)))
    qz(V("uq"), V("us"), V("ut"))
    cp(V("uq2"), ind(V("uq"), V("uoff")), dt.uint32)
    cp(V("us2"), ind(V("us"), V("uoff")))
    ts(V("r16"), V("diag"), 0.0, ALU.not_equal)
    ts(V("diag"), V("diag"), P16, ALU.is_equal)
    for pg, i in enumerate((P16, I1)):
        lin(run("tmp", pg, 64), V("hf"), 1.0, i)
        ts(run("eq", pg, 64), V("jf"), i, ALU.is_equal)
        ts(run("base", pg, 64), V("jv"), i, ALU.is_equal, 64.0, ALU.mult)
    lin(V("dn"), V("fp"), 1.0, 128.0)
    ms(V("dn", 0, 64, 48), 0.0)
    tt(V("base"), V("base"), V("tmp"), ALU.add)
    ms(V("dc"), -1.0)
    for at, step in ((15, -1.125), (16, -0.875), (31, 15.0)):
        ms(V("dc", at, 128, 32), step)
    ms(V("r64"), 1.0)
    ms(V("r64", 0, 256, 64), 0.0)
    for k in range(2):
        for pg in range(2):
            tt(run("p%dm" % k, pg, 64), ind(run("eq", pg, 64), V("poff", 8 + 4 * k, 12 + 4 * k)), V("dn"), ALU.mult)
        tt(V("p%dm" % k), V("p%dm" % k), V("base"), ALU.max)
    tt(V("dm"), V("p0m"), V("p1m"), ALU.subtract)
    tt(V("pd"), V("p0f"), V("p1f"), ALU.subtract)
    tt(V("pdm", 0, 128, 2), V("pd"), V("diag"), ALU.mult)
    tt(V("pdm", 1, 128, 2), V("p1f"), V("diag"), ALU.mult)
    lin(V("xm", 0, 128, 2), V("diag"), -1.0, 1.0)
    lin(V("off"), V("diag"), -1e29, 1e29)
    ts(cc(6), P16, 0.0, ALU.not_equal, 64.0, ALU.mult)
    ms(V("v22"), 0.0)
    ms(V("nn"), 0.0)
    ms(V("vm"), 0.0)
    for o in (V("va", 64), V("vb", 64), V("v5", 64), V("v1", 64), V("v22", 80, 144)):
        act(o, V("base", 64))
    ms(V("lb", 128, 130), 0.0)
    ms(V("tb", 64, 128), 0.0)
    ms(V("w2", 128, 192), 0.0)
    act(V("cx", 0, 64), V("jf"))
    act(V("cx", 64, 128), V("jf"))
    RE, ET, EXL, L1 = V("cl16", 0, 1), V("cl16", 2, 3), V("cl16", 4, 6), V("cl16", 8, 16)
    RX = [V("cl16", 16 + 2 * i, 17 + 2 * i) for i in range(NP)]
    RY, R16, R32, SF = V("cl16", 24, 25), V("cl16", 26, 27), V("cl16", 28, 29), V("cl16", 32, 36)
    F = lambda v: V("lf", v[1], v[2])
    ms(V("lf"), 0.0)
    lin(cc(7), B0, 64.0, 31.0)
    lin(F(RE), B1, 32.0, cc(7))
    lin(cc(8), PAR, 16.0, 0.0)
    lin(cc(22), P16, 1.0, cc(8))
    lin(F(SF), V("row", 0, 4), 2.0, cc(22))
    lin(cc(9), B0, 96.0, cc(8))
    lin(cc(10), H7, 32.0, cc(9))
    ts(F(ET), cc(10), 191.0, ALU.min)
    lin(cc(11), B32, 0.25, Q3)
    lin(cc(12), B0, 64.0, cc(11))
    lin(cc(13), B1, 4.0, cc(12))
    lin(F(EXL), V("iota", 0, 256, 128), 1.0, cc(13))
    lin(cc(14), PAR, 144.0, P16)
    lin(cc(21), PAR, -144.0, P16)
    lin(cc(15), cc(21), 1.0, 160.0)
    for pj in range(2):
        for h in range(2):
            o = V("cl16", 8 + 4 * pj + 2 * h, 10 + 4 * pj + 2 * h)
            lin(F(o), run("row", h, 2), 1.0, cc(14 + (pj ^ h)))
    lin(cc(5), cc(30), B2, R3)
    lin(cc(26), cc(5), 1.0, B3)
    ts(cc(24), cc(26), 3.0, ALU.min)
    ts(R16, cc(24), 16.0, ALU.mult, 15.0, ALU.add)
    ts(R32, cc(24), 32.0, ALU.mult, 31.0, ALU.add)
    first, last = {}, {}
    fill("rs", 0, 128 * NP, 0.0)
    for o in ([run("gt", i, 768) for i in range(2)] + [V("elt"), V("pmt"), V("mv")]
              + [V("sc%d" % l, 448, 512) for l in range(4)]):
        clear(o)
    for i, ls_ in enumerate(PASSES):
        at = 0
        for l in ls_:
            first[l], last[l] = at, at + SEG[l][0]
            lin(V("rs", 128 * i + at, 128 * i + 128, 64), V("iota", 0, 2), 0.0, 1000.0)
            lin(V("rs", 128 * i + last[l], 128 * i + 128, 64), V("iota", 0, 2), 1.0, -2.0)
            at = last[l] + 1

    def by_quarter(o, vals, a):
        v = [float(x) for x in vals + vals[-1:] * 3]
        lin(o, B2, v[1] - v[0], a)
        lin(o, B3, v[2] - v[0], o)
        lin(o, cc(31), v[3] - v[2] - v[1] + v[0], o)
        lin(o, o, 1.0, v[0])

    lin(cc(31), B2, B3, 0.0)
    lin(cc(16), B1, 64.0, 0.0)
    lin(cc(17), B0, 128.0, cc(16))
    for i, ls_ in enumerate(PASSES):
        by_quarter(F(RX[i]), [last[l] for l in ls_], cc(17))
    lin(cc(28), B0, 64.0, 0.0)
    lin(cc(23), B1, 128.0, cc(28))
    by_quarter(F(RY), [256 * i + last[l] - 1 for i, ls_ in enumerate(PASSES) for l in ls_], cc(23))
    cp(V("cl16", 0, 26), V("lf", 0, 26))
    cp(SF, F(SF))
    lin(cc(25), B32, 1.0, -16.0)
    fill("e32t", 0, 516, 32.0)
    select(V("e32t"), V("e32t"), [[-1, 516]], ALU.is_equal, 0.0, 3, 4)
    for b in range(4):
        qz(run("e32q", b, 128), run("e32s", b, 128), V("e32t", 3 - b, 515 - b))
    qz(V("vq"), V("vs"), V("vt"))
    ms(V("one"), 1.0)
    for pg in range(2):
        for par in range(2):
            pat, o = [[32, 4], [128, 2], [1, 16]], 16 * pg - 128 * par
            e = V("lut", 512 * pg + par, 512 * pg + 512, 4)
            select(e, V("one"), pat, ALU.is_gt, 0.0, o, -1)
            select(e, e, pat, ALU.not_equal, -256.0, o, -1)
            select(V("lut", 512 * pg + par + 2, 512 * pg + 512, 4), V("one"), [[-s, n] for s, n in pat], ALU.is_gt, 0.0, -o, 1)
        qz(run("luq", pg, 128), run("lus", pg, 128), run("lut", pg, 512))
    lin(cc(27), B32, 1.0, 16.0)
    for h in range(2):
        for k in range(2):
            e0 = 192 + 256 * h + 2 * h + k
            lin(V("elt", e0, e0 + 61, 4), V("iota", 0, 16), 0.0, cc(27) if k else 1.0)
    qz(V("elq"), V("els"), V("elt"))
    for sl in range(4):
        act(V("pmt", 256 + 65 * sl, 317 + 65 * sl, 4), V("diag", 0, 16))
    qz(V("pmq"), V("pms"), V("pmt"))
    qz(V("mq", 64, 192), V("ms", 64, 192), V("mv"))

    def decode(bank0, xq, xs, n, stop=True):
        for b in range(4):
            mm(bank(bank0 + b, n), run("e32q", b, 128), run("e32s", b, 128), xq, xs, True, stop)

    W, D, A, A2 = V("tb", 128, 192), V("tb", 192, 256), V("tb", 256, 320), V("tb", 0, 64)
    pg_ = lambda name, i: run(name, i, 64)
    v22 = lambda i: V("v22", 16 + 64 * i, 80 + 64 * i)

    def trees(t):
        J = lambda i: run("jj", i - 1, 64)
        O1, O3, O8 = [V("jo", 16 * i, 16 * i + 4) for i in range(3)]
        part = lambda name, i, at=0: V(name, at + 80 * i, at + 64 + 48 * i)
        plist = lambda o, i: V("jo", o[1] + 8 * i, o[1] + 4 + 6 * i)
        act(V("sb0"), ind(V("ssb"), V("poff", 0, 4)))
        tt(V("sb1"), ind(V("ssb"), V("poff", 0, 4)), V("off"), ALU.add)
        tt(V("xm", 1, 128, 2), ind(V("ssb"), V("poff", 4, 8)), V("sb1"), ALU.is_le)
        tt(V("sel"), ind(V("ssb"), V("poff", 4, 8)), V("sb0"), ALU.is_le)
        tt(V("jm"), V("sel"), V("pd"), ALU.mult)
        for i in range(2):
            tt(part("vm", i), V("sel", 16 * i, 64 - 16 * i), part("dm", i), ALU.mult)
        scan(V("xn"), V("xm"), V("pdm"), ALU.mult, ALU.add)
        tt(J(1), V("jm"), V("p1f"), ALU.add)
        tt(V("v1", 0, 112), V("vm", 0, 112), V("p1m", 0, 112), ALU.add)
        cp(run("jo", 0, 16), ind(V("xn"), R32))
        tt(V("v1c", 0, 112), V("vm", 0, 112), V("p1m", 0, 112), ALU.add)

        def far(o, j, off):
            tt(V("jm"), ind(j, off), V("diag"), ALU.mult)
            scan(V("jn"), V("r16"), V("jm"), ALU.mult, ALU.add)
            cp(run("jo", o, 16), ind(V("jn"), R16))

        act(J(2), ind(J(1), O1))
        far(1, J(2), O1)
        for i in (3, 4, 5):
            act(J(i), ind(J(i - 1), O1))
        far(2, J(5), O3)
        if t == 2:
            act(V("cx", 128, 192), ind(V("jv"), V("jo", 4, 8)))
        for o, w, off, b in [("va", "v1", O1, "v1c"), ("vb", "va", O1, "v1"), ("va", "vb", O1, "v1"), ("v5", "va", O1, "v1"),
                             ("vb", "v5", O3, "va"), ("va", "vb", O3, "v5"), ("vb", "va", O3, "v5")]:
            for i in range(2):
                tt(part(o, i), ind(pg_(w, i), plist(off, i)), part(b, i), ALU.max)
        for i in range(2):
            ts(part("thr", i), part("va", i), 64.0, ALU.is_lt, 64.0 if i else cc(6), ALU.mult)
            tt(part("v22", i, 16), ind(pg_("vb", i), plist(O8, i)), part("va", i), ALU.max)
        for h in range(2):
            tt(V("nn", 64 * h, 64 * h + 32), ind(v22(0), V("jo", 32 + 2 * h, 34 + 2 * h)), run("thr", h, 32), ALU.is_ge)
            tt(V("nn", 128 + 64 * h, 144 + 64 * h), ind(v22(1), col("jo", 40 - 6 * h)), run("thr", 5 + h, 16), ALU.is_ge)
        scan(V("szs"), V("r64"), V("nn"), ALU.mult, ALU.add)
        tr(V("st"), V("szs", 32, 256))
        tr(V("lt", 0, 128), V("v22", 16, 144))
        tr(V("lt", 128, 288), V("v22"))
        act(V("lb", 0, 128), ind(V("lt"), L1))
        tt(V("dl"), V("lb", 0, 128), V("lb", 1, 129), ALU.subtract)
        cp(ends("dl"), ends("lb"))
        ts(pg_("ny", 0), ind(V("st"), SF), 16.0, ALU.is_lt)
        act(W, ind(V("st"), SF), ACT.Copy, 1.0 / 32)
        lin(A, W, -1.0, 1.0)
        lin(A2, W, -1.0, 1.0)
        lin(D, W, 2.0, -1.0)
        lin(pg_("uu", 0), W, 1.0, -0.5)
        ts(V("sg"), W, 0.5, ALU.is_lt, 0.5, ALU.subtract)
        for l in range(4):
            i = [l in p for p in PASSES].index(True)
            tr(run("wt", l, 64), W)
            for h in range(2):
                for par in range(2):
                    e0, (n, v0) = 512 * i + 4 * (64 * h + first[l]) + par, SEG[l]
                    act(V("gt", e0, e0 + 4 * n - 1, 2), V("gv", 2 * v0, 2 * (v0 + n)), ACT.Sign, 0.5 / 32,
                        col("wt", 64 * l + 32 * h + 16 * par))
            if l == 0:
                for pg in range(2):
                    scan(pg_("ls", pg), pg_("ny", 0), pg_("dl", pg), ALU.mult, ALU.add)
                scan(pg_("csn", 0), pg_("ny", 0), pg_("dc", 0), ALU.mult, ALU.add)
                act(pg_("csn", 1), pg_("csn", 0))
            else:
                if l < 3 or t == 2:
                    scan(V("ls"), V("ny"), V("dl"), ALU.mult, ALU.add)
                scan(run("csn", l, 128), V("ny"), V("dc"), ALU.mult, ALU.add)
            if l < 3 or t == 2:
                cp(run("lab", l, 16), ind(V("ls"), RE))
            LB = V("lab", 16 * l, 16 * l + 4)
            for h in range(2):
                for pg in range(2):
                    act(run("cv", 4 * l + 2 * h + pg, 16), V("diag", 0, 16), ACT.Copy,
                        col("csn", 128 * l + 64 * pg * (l > 0) + 32 * h + 31))
            if t == 2:
                for h in range(2):
                    act(run("crf", 4 * h + l, 32), ind(V("cx"), V("lab", 16 * l + 2 * h, 16 * l + 2 * h + 2)),
                        ACT.Identity, 1.0, B32)
            if l == PASSES[i][-1]:
                places(i)
            if l == 3:
                break
            u0, u1 = pg_("uu", l & 1), pg_("uu", 1 - (l & 1))
            tt(V("pp"), ind(V("tb", 128, 320), LB), V("sg"), ALU.mult)
            if l < 2:
                act(V("mh"), ind(V("tb", 0, 192), LB), ACT.Copy, 0.5)
            else:
                tt(V("wy"), ind(V("w2"), LB), V("hn"), ALU.mult)
            for pg in range(2):
                for h in range(2):
                    o, me = run("ss", 2 * pg + h, 32), col("ls", 64 * pg + 32 * h + 31)
                    a = ind(V("iota", 0, 192), V("lab", 16 * l + 2 * h, 16 * l + 2 * h + 2))
                    if pg:
                        act(o, a, ACT.Abs, -1.0, me)
                    else:
                        ts(o, a, me, ALU.not_equal)
            tt(u1, u0, V("pp"), ALU.add)
            for pg in range(2):
                tt(pg_("ny", pg), u1, pg_("ss", pg), ALU.is_lt)
            if l < 2:
                tt(W, V("mh"), u1, ALU.add)
                tt(A, V("mh"), u1, ALU.subtract)
                act(A2, A)
                lin(D, u1, 2.0, 0.0)
                ts(V("sg"), u1, 0.0, ALU.is_lt, 0.5, ALU.subtract)
            else:
                tt(W, W, V("wy"), ALU.add)
            if l == 1:
                for k in range(2):
                    act(run("w2", k, 64), W)
                ts(V("hn"), u1, 0.0, ALU.is_lt, 1.0, ALU.subtract)

    def places(i):
        qz(run("gq", i, 128), run("gs", i, 128), run("gt", i, 512))
        n = 64 + last[PASSES[i][-1]] + 1
        for pg in range(2):
            mm(bank(4 + pg, 128), run("luq", pg, 128), run("lus", pg, 128), run("gq", i, 128), run("gs", i, 128))
            at = 256 * i + 128 * pg
            scan(V("rk", at, at + n), V("rs", 128 * i, 128 * i + n), bank(4 + pg, n), ALU.add, ALU.min)
        ts(run("roff", i, 16), ind(run("rk", i, 256), RX[i]), 513.0, ALU.add, 2.0, ALU.mult)
        for k, l in enumerate(PASSES[i]):
            sc = "sc%d" % l
            act(V(sc, 0, 448, 2), V("iota", 0, 224), ACT.Copy, 0.0)
            cp(ind(V(sc, 64 * (l & 1), 64 * (l & 1) + 1024), V("roff", 16 * i + 4 * k, 16 * i + 4 * k + 4)), run("cv", l, 64))
            if l < ONV:
                act(V("ab"), V(sc, 0, 448, 2), ACT.Abs)
                act(V(sc, 1, 448, 2), V("ab"), ACT.Sign)
            else:
                ts(V(sc, 1, 448, 2), V(sc, 0, 448, 2), 0.0, ALU.not_equal)
            qz(run("scq", l, 128), run("scs", l, 128), V(sc, 0, 512))
            mm(bank(7, 128), V("elq", 48 - 16 * l, 176 - 16 * l), V("els", 48 - 16 * l, 176 - 16 * l),
               run("scq", l, 128), run("scs", l, 128), l == 0, l == 3)

    xt, side[0] = "xt0", 0
    for t, m in enumerate(PARTNER):
        mate = T.cores[rank ^ m]
        xq, xs = "xq%d" % t, "xs%d" % t
        XQ, XS, LQ, LS = V(xq), V(xs), V("lq%d" % t), V("ls%d" % t)
        for k in range(2):
            qz(run(xq, k, 128), run(xs, k, 128), run(xt, k, 512))
            mm(bank(k, 128), run(xq, k, 128), run(xs, k, 128), V("uq2"), V("us2"))
            tr(run("ssb", k, 64), bank(k, 64))
        sends = [send(mate, LQ, XQ, "aq%d" % t, dt.uint8), send(mate, LS, XS, "aq%d" % t)]
        side[0] = 2
        decode(0, XQ, XS, 256)
        for b in range(4):
            for h in range(2):
                act(V("tw", PL * b + K + 128 * h, PL * b + K + 128 * h + 128), bank(b, 128 * h + 128, 128 * h), ACT.Copy, 1.0 / 32)
        arrive(mate, [LQ, LS], "aq%d" % t, sends)
        decode(0, LQ, LS, 256)
        for b in range(4):
            for h in range(2):
                act(V("tp", 512 * h + b, 512 * h + 512, 4), bank(b, 128 * h + 128, 128 * h), ACT.Copy, 1.0 / 32)
        for h in range(2):
            qz(run("tpq", h, 128), run("tps", h, 128), run("tp", h, 512))
        decode(0, V("tpq"), V("tps"), 256)
        for b in range(4):
            for h in range(2):
                act(run("tq", 2 * b + h, 128), bank(b, 128 * h + 128, 128 * h), ACT.Copy, 1.0 / 64)
        decode(0, run(xq, 0, 128), run(xs, 0, 128), 128, False)
        side[0] = 0
        trees(t)
        tr(V("te", 0, 96), bank(7, 96))
        tr(V("te", 96, 192), bank(7, 112, 16))
        EL = "el%d" % t
        cp(V(EL), ind(V("te"), ET))
        sends = [send(mate, V("ll%d" % t, 0, 6), V(EL, 0, 6), "al%d" % t)]
        for b in range(4):
            act(run("eh", b, K), ind(V("tw", PL * b + K, PL * b + PL), V(EL, 0, 6)), ACT.Copy, 0.5)
        z = lambda i: run("zf", i, 16)
        ts(z(0), ind(V("rk", 0, 256 * NP), RY), 0.5, ALU.mult, 127.5, ALU.add)
        lin(z(1), ends("csn", 512), 1.0, cc(25))
        ts(z(2), z(0), -32.0, ALU.is_ge)
        tt(z(3), z(1), z(0), ALU.subtract)
        tt(z(4), z(3), z(2), ALU.mult)
        tt(V("wi"), z(4), z(0), ALU.add)
        ts(V("wd", 0, 16), V("wi"), 15, ALU.bitwise_and)
        tt(V("wd", 16, 32), V("wi"), V("wd", 0, 16), ALU.subtract)
        cp(ind(V("mv", 0, 256), EXL), V("wd"))
        qz(V("mq", 0, 128), V("ms", 0, 128), V("mv"))
        for q in range(4):
            h = q & 1
            mm(bank(6, 128), V("pmq", 64 - 64 * h, 192 - 64 * h), V("pms", 64 - 64 * h, 192 - 64 * h),
               V("mq", 16 * q, 16 * q + 128), V("ms", 16 * q, 16 * q + 128), q == 0, q == 3)
        ts(V("zoff"), bank(6, 16), 128.0, ALU.add)
        decode(4, run(xq, 1, 128), run(xs, 1, 128), 128, False)
        if t == 2:
            for gi in range(8):
                b = block(gi)
                store("y", T.cl[:, 32 * b:32 * b + 32], V("crf", 0, 256, 1, (16 * gi, 16 * gi + 1)))
        LL = V("ll%d" % t, 0, 6)
        arrive(mate, [LL], "al%d" % t, sends)
        for b in range(4):
            tt(V("tw", PL * b, PL * b + K), ind(run("tq", b, 256), LL), run("eh", b, K), ALU.add)
        for k in range(2):
            for b in range(4):
                (act if ZS[k][b] else cp)(V("ztile", 512 * k + b, 512 * k + 512, 4), ind(run("tw", b, PL), run("zoff", k, 8)))
            qz(run("zq", k, 128), run("zs", k, 128), run("ztile", k, 512))
            for b in range(4):
                mm(bank(4 * k + b, 128), run("wq", b, 128), run("wsq", b, 128), run("zq", k, 128), run("zs", k, 128), False, True)
            for b in range(4):
                o = V("xt1", 512 * k + b, 512 * k + 512, 4)
                if XA[k][b]:
                    act(o, bank(4 * k + b, 128), ACT.Copy, 1.0 / 32)
                else:
                    ts(o, bank(4 * k + b, 128), 1.0 / 32, ALU.mult)
        xt = "xt1"

    for k in range(2):
        qz(run("xq3", k, 128), run("xs3", k, 128), run(xt, k, 512))
        mm(bank(k, 128), V("vq"), V("vs"), run("xq3", k, 128), run("xs3", k, 128))
        (cp if k else act)(run("ysb", k, 128), bank(k, 128))
        store("y", T.oc[:, 512 * k:512 * k + 512], run("xq3", k, 128), dt.uint8)
        store("s", T.y[:, 128 * k:128 * k + 128], run("ysb", k, 128))
    for k in range(4):
        store("y", T.osc[4 * k:4 * k + 4, :], V("xs3", 0, 256, 1, (32 * k, 32 * k + 4)))

    emit(g, T, ops)


ORDER = {}


def schedule(ops, deps, before):
    n = len(ops)
    if n in ORDER:
        return ORDER[n]
    lag = lambda j, i: (ops[j]["late"] + WAKE) if j in deps[i] or ops[i]["e"] == "x" or ops[j]["e"] != ops[i]["e"] else 0.0
    pre = [[(j, lag(j, i)) for j in before[i]] for i in range(n)]
    post = [[] for _ in range(n)]
    for i in range(n):
        for j, w in pre[i]:
            post[j].append((i, w))
    tail = [ops[i]["late"] if not post[i] else 0.0 for i in range(n)]

    def place(key, ahead, behind, first):
        left, can, at = [len(a) for a in ahead], list(first), [0.0] * n
        ready, busy = [i for i in range(n) if not left[i]], {}
        while ready:
            i = min(ready, key=key)
            ready.remove(i)
            s, c, line = can[i], ops[i]["c"], busy.setdefault(ops[i]["e"], [])
            k = 0
            for k, (a, b) in enumerate(line + [(1e9, 1e9)]):
                if s + c <= a + 1e-9:
                    break
                s = max(s, b)
            line.insert(k, (s, s + c))
            at[i] = s
            for j, w in behind[i]:
                can[j] = max(can[j], s + c + w)
                left[j] -= 1
                if not left[j]:
                    ready.append(j)
        return at

    def replay(order, k):
        free, done = {}, [0.0] * n
        for i in order:
            e = ops[i]["e"]
            s = max([free.get(e, 0.0)] + [done[j] + w for j, w in pre[i]])
            free[e] = done[i] = s + ops[i]["c"] * (k if e in "vst" else 1.0)
        return max(done[i] + tail[i] for i in range(n))

    base = [0.0] * n
    for i in range(n - 1, -1, -1):
        base[i] = ops[i]["c"] + max([tail[i]] + [base[j] + w for j, w in post[i]])
    best = None
    for lead in LEADS:
        way = [base[i] + lead[ops[i]["side"]] + KEEP[ops[i]["side"]] for i in range(n)]
        for _ in range(TURNS):
            for i in range(n - 1, -1, -1):
                way[i] = max([way[i]] + [way[j] + w + ops[i]["c"] for j, w in post[i]])
            at = place(lambda i: (-way[i], i), pre, post, [0.0] * n)
            order = sorted(range(n), key=lambda i: (at[i], i))
            end = sum(replay(order, k) for k in (0.92, 1.15, 1.4))
            if best is None or end < best[0]:
                best = (end, order)
            back = place(lambda i: (-at[i] - ops[i]["c"], -i), post, pre, tail)
            way = [back[i] + ops[i]["c"] + KEEP[ops[i]["side"]] for i in range(n)]
    ORDER[n] = best[1]
    return ORDER[n]


def emit(g, T, ops):
    Q = {"v": g.vector, "s": g.scalar, "t": g.tensor, "g": g, "y": g.sync}
    hist, total, members = {}, {}, {}
    for i, o in enumerate(ops):
        if o["sem"] is not None:
            total[o["sem"]] = total.get(o["sem"], 0) + o["n"]
            members.setdefault(o["sem"], []).append(i)
    deps, before, lasty = [], [], None
    for i, o in enumerate(ops):
        d, b = set(), set(o["after"] or [])
        for kind in ("r", "w"):
            for name, m in o[kind]:
                for (j, mj, wj) in hist.get(name, []):
                    if not (m & mj):
                        continue
                    if name.startswith("ps"):
                        if ops[j]["e"] != o["e"] or not o["acc"] and (wj or kind == "w"):
                            d.add(j)
                        elif o["acc"]:
                            b.add(j)
                    elif (wj or kind == "w") and (o["sem"] is None or ops[j]["sem"] != o["sem"]):
                        d.add(j)
        for j in d:
            b.update(members[ops[j]["sem"]] if ops[j]["sem"] is not None else [j])
        if o["e"] == "y":
            if lasty is not None:
                b.add(lasty)
            lasty = i
        deps.append(d)
        before.append(b)
        for name, m in o["w"]:
            hist[name] = [h for h in hist.get(name, []) if h[1] & ~m] + [(i, m, True)]
        for name, m in o["r"]:
            hist.setdefault(name, []).append((i, m, False))
    order = schedule(ops, deps, before)
    known, issued = {e: 0 for e in Q}, {e: 0 for e in Q}
    place = {i: k for k, i in enumerate(order)}
    snap, waits = {}, {}
    for i in order:
        o, w = ops[i], []
        e, all_ = o["e"], sum(1 << j for j in members.get(o["sem"], []))
        if e == "x":
            snap[i] = all_
            continue
        for j in sorted(deps[i], key=lambda k: -place[k]):
            if not known[e] >> j & 1:
                w.append(j)
                known[e] |= snap[j]
        if o["sem"] is None:
            issued[e] |= 1 << i
            all_ = issued[e]
        snap[i] = known[e] | all_
        waits[i] = w
    wanted = set(j for w in waits.values() for j in w)
    count, mark, seen = {}, {}, {}
    for i in order:
        o = ops[i]
        e = o["e"]
        if e == "x":
            continue
        for j in waits[i]:
            s, k = (ops[j]["sem"], total[ops[j]["sem"]]) if ops[j]["sem"] is not None else mark[j]
            Q[e].wait_ge(T.sem[s], k)
            seen[s] = max(seen.get(s, 0), k)
        if o["sem"] is None and i in wanted:
            s = "q" + e
            count[s] = count.get(s, 0) + 1
            mark[i] = (s, count[s])
            o["fn"](Q[e]).then_inc(T.sem[s], 1)
        elif o["sem"] is not None and o["sem"] != "sent":
            o["fn"](Q[e]).then_inc(T.sem[o["sem"]], 16)
        else:
            o["fn"](Q[e])
    for s, k in total.items():
        if seen.get(s, 0) < k:
            g.wait_ge(T.sem[s], k)
